import numpy as np
import ml_dtypes


def mxq(x, axis, fmt="e4m3"):
    dtype, down = {"e4m3": (ml_dtypes.float8_e4m3fn, 7), "e5m2": (ml_dtypes.float8_e5m2, 14)}[fmt]
    v = np.moveaxis(np.asarray(x, np.float32).astype(ml_dtypes.bfloat16).astype(np.float64), axis, -1)
    blocks = v.reshape(v.shape[:-1] + (-1, 32))
    amax = np.abs(blocks).max(-1, keepdims=True)
    byte = np.maximum(np.where(amax > 0, np.frexp(amax)[1] - 1 + 127, 0) - down, 1)
    scale = np.exp2(byte - 127.0)
    codes = (blocks / scale).astype(np.float32).astype(dtype).astype(np.float64)
    return np.moveaxis((codes * scale).reshape(v.shape), -1, axis)


WIDE = False


def mx_kscale(k):
    if not WIDE:
        return np.ones(k)
    levels = np.array([10, -10, 5, -5, 0])
    if k % 512:
        return np.exp2(np.random.permutation(np.resize(levels, k // 32))).repeat(32)
    a = np.empty((k // 512, 16))
    for p in range(k // 512):
        a[p, :8] = np.random.permutation(np.resize(levels, 8))
        for g in range(8):
            far = levels[np.abs(levels - a[p, g]) >= 10]
            a[p, g + 8] = far[np.random.randint(len(far))]
    return np.exp2(a.ravel()).repeat(32)


def f64(x):
    return np.asarray(x).astype(np.float64)


def striped(idx):
    return np.tile(idx.reshape(-1, 16).T, (8, 1)).astype(np.uint16)


def unstriped(offs):
    return offs[:16].T.reshape(-1).astype(np.int64)


E2M1 = np.array([0.0, 0.5, 1.0, 1.5, 2.0, 3.0, 4.0, 6.0, -0.0, -0.5, -1.0, -1.5, -2.0, -3.0, -4.0, -6.0])


def pack_weight(w, fmt):
    k, n = w.shape
    w = f64(np.asarray(w, np.float32).astype(ml_dtypes.bfloat16)).reshape(k // 32, 32, n)
    amax = np.abs(w).max(1)
    if fmt == "e4m3":
        byte = np.frexp(amax)[1] - 1 + 127 - 7
    else:
        mant, ex = np.frexp(amax / 6.0)
        byte = np.where(mant > 0.5, ex, ex - 1) + 127
    byte = np.clip(np.where(amax > 0, byte, 1), 1, 254)
    scaled = (w * np.exp2(127.0 - byte)[:, None, :]).reshape(k, n).astype(np.float32)
    by_word = np.ascontiguousarray(scaled.reshape(k // 512, 128, 4, n).transpose(0, 1, 3, 2))
    if fmt == "e4m3":
        words = by_word.astype(ml_dtypes.float8_e4m3fn).view(np.uint8)
    else:
        c = by_word.astype(ml_dtypes.float4_e2m1fn).view(np.uint8) & 0xF
        words = (c[..., 0::2] | (c[..., 1::2] << 4)).reshape(k // 512, 128, 2 * n)
    return np.ascontiguousarray(words), np.ascontiguousarray(byte.astype(np.uint8).reshape(k // 512, 16, n))


def unpack_weight(words, scales, fmt):
    g, _, n = scales.shape
    words = np.ascontiguousarray(words).reshape(g, 128, n, -1)
    if fmt == "e4m3":
        vals = words.view(ml_dtypes.float8_e4m3fn).astype(np.float64)
    else:
        nib = np.empty((g, 128, n, 4), np.uint8)
        nib[..., 0::2] = words & 0xF
        nib[..., 1::2] = words >> 4
        vals = E2M1[nib]
    vals = vals * np.repeat(np.exp2(scales.astype(np.float64) - 127.0), 8, axis=1)[..., None]
    return vals.transpose(0, 1, 3, 2).reshape(g * 512, n)


def gelu(v):
    return 0.5 * v * (1.0 + np.tanh(np.sqrt(2.0 / np.pi) * (v + 0.044715 * v**3)))


K, T, S, H, N = 1024, 4096, 1024, 1024, 512

def setup_inputs():
    n = np.random.standard_normal
    s = mx_kscale(K)[:, None]
    u = mx_kscale(H)[:, None]
    tab_words, tab_scales = pack_weight(n((K, T)) * s, "e4m3")
    w1 = (n((K, H)) / np.sqrt(K) / s * u.T).astype(np.float32)
    w4_words, w4_scales = pack_weight(n((K, H)) / np.sqrt(K) / s, "e2m1")
    w8_words, w8_scales = pack_weight(1.6 * n((H, N)) / np.sqrt(H) / u, "e4m3")
    return {
        "tab_words": tab_words, "tab_scales": tab_scales,
        "offs": striped(np.random.permutation(T)[:S]),
        "w1": w1,
        "w4_words": w4_words, "w4_scales": w4_scales,
        "w8_words": w8_words, "w8_scales": w8_scales,
        "offs2": striped(np.random.permutation(S)),
        "wgo": np.exp(0.3 * n((128, S))).astype(np.float32),
        "x0": n((N, S)).astype(np.float32),
    }

def reference(tab_words, tab_scales, offs, w1, w4_words, w4_scales,
              w8_words, w8_scales, offs2, wgo, x0):
    v = unpack_weight(tab_words, tab_scales, "e4m3")[:, unstriped(offs)]
    a = mxq(f64(w1), 0, "e4m3").T @ v
    b = unpack_weight(w4_words, w4_scales, "e2m1").T @ v
    h = a / (1.0 + np.abs(b))
    y = unpack_weight(w8_words, w8_scales, "e4m3").T @ mxq(h, 0, "e4m3")
    page = np.zeros((N, S))
    page[:, unstriped(offs2)] = np.tile(f64(wgo), (N // 128, 1)) * y
    return f64(x0) / (1.0 + np.square(page))

@@ -1,0 +1,274 @@
+from contextlib import ExitStack
+
+import concourse.mybir as mybir
+
+K, T, S, H, N = 1024, 4096, 1024, 1024, 512
+FLOPS = 2 * K * H * S * 2 + 2 * H * N * S
+
+F32 = mybir.dt.float32
+BF16 = mybir.dt.bfloat16
+I32 = mybir.dt.int32
+U32 = mybir.dt.uint32
+U16 = mybir.dt.uint16
+U8 = mybir.dt.uint8
+FP8X4 = mybir.dt.float8_e4m3fn_x4
+FP4X4 = mybir.dt.float4_e2m1fn_x4
+ACT = mybir.ActivationFunctionType
+MULT = mybir.AluOpType.mult
+
+P = 128
+PACK = 4
+KP = P * PACK
+PASSES = K // KP
+HALF = 512
+CHUNK = 256
+SUB = 128
+CHUNKS = S // CHUNK
+BLOCKS = N // P
+
+
+def tile_list_adna_damage_tempering_kernel(
+    tc, tab_words, tab_scales, offs, w1, w4_words, w4_scales, w8_words, w8_scales, offs2, wgo, x0, out
+):
+    nc = tc.nc
+    with ExitStack() as ctx:
+        keep = ctx.enter_context(tc.tile_pool(name="keep", bufs=1))
+        ring = ctx.enter_context(tc.tile_pool(name="ring", bufs=2))
+        psum = ctx.enter_context(tc.psum_pool(name="psum", bufs=1))
+
+        picks = keep.tile([P, S // 16], U16, name="picks")
+        places = keep.tile([P, S // 16], U16, name="places")
+        nc.sync.dma_start(picks[:], offs)
+
+        w4_sc_raw = keep.tile([P, PASSES * H], U8, name="w4_sc_raw", align_bytes=64)
+        tab_sc = keep.tile([P, PASSES * T], U8, name="tab_sc", align_bytes=64)
+        w8_sc = keep.tile([P, N], U8, name="w8_sc", align_bytes=64)
+        nc.vector.memset(w4_sc_raw[:].bitcast(I32), 0)
+        nc.vector.memset(tab_sc[:].bitcast(I32), 0)
+        nc.vector.memset(w8_sc[:].bitcast(I32), 0)
+
+        warm_in = keep.tile([P, 1], F32, name="warm_in")
+        warm_out = keep.tile([P, 1], F32, name="warm_out")
+        nc.gpsimd.memset(warm_in[:], 1.0)
+        nc.scalar.activation(warm_out[:], warm_in[:], ACT.Abs_reciprocal_sqrt)
+
+        w4_raw = keep.tile([P, PASSES * 2 * H], U8, name="w4_raw", align_bytes=64)
+        nc.sync.dma_start(
+            w4_raw[:].bitcast(I32).rearrange("p (a n) -> p a n", a=PASSES),
+            w4_words.bitcast(I32).rearrange("a p n -> p a n"),
+        )
+        for q in range(4):
+            nc.sync.dma_start(
+                w4_sc_raw[32 * q : 32 * q + 4, :].bitcast(I32).rearrange("r (a n) -> r a n", a=PASSES),
+                w4_scales[:, 4 * q : 4 * q + 4, :].bitcast(I32).rearrange("a r n -> r a n"),
+            )
+        for q in range(4):
+            nc.sync.dma_start(
+                tab_sc[32 * q : 32 * q + 4, :].bitcast(I32).rearrange("r (a n) -> r a n", a=PASSES),
+                tab_scales[:, 4 * q : 4 * q + 4, :].bitcast(I32).rearrange("a r n -> r a n"),
+            )
+        tab = []
+        for a in range(PASSES):
+            words = keep.tile([P, T], I32, name="tab%d" % a, align_bytes=64)
+            nc.sync.dma_start(words[:], tab_words[a].rearrange("p n i -> p (n i)").bitcast(I32))
+            tab.append(words)
+
+        w1_raw = {}
+        for g in range(2):
+            for a in range(PASSES):
+                raw = ring.tile([P, PACK, HALF], F32, name="big", tag="big", bufs=4)
+                rows = w1[KP * a : KP * (a + 1), HALF * g : HALF * (g + 1)]
+                nc.sync.dma_start(raw[:], rows.rearrange("(p j) c -> p j c", j=PACK))
+                w1_raw[g, a] = raw
+
+        w8 = keep.tile([P, PASSES * N], I32, name="w8", align_bytes=64)
+        nc.sync.dma_start(
+            w8[:].rearrange("p (a n) -> p a n", a=PASSES),
+            w8_words.rearrange("a p n i -> p a (n i)").bitcast(I32),
+        )
+        for q in range(4):
+            nc.sync.dma_start(
+                w8_sc[32 * q : 32 * q + 8, :].bitcast(I32),
+                w8_scales[:, 4 * q : 4 * q + 4, :].bitcast(I32),
+            )
+        gain = keep.tile([P, S], F32, name="gain")
+        nc.sync.dma_start(gain[:], wgo)
+        nc.sync.dma_start(places[:], offs2)
+
+        w4 = keep.tile([P, PASSES * 2 * H], U8, name="w4", align_bytes=64)
+        w4_sc = keep.tile([P, PASSES * H], U8, name="w4_sc", align_bytes=64)
+        nc.vector.tensor_copy(
+            w4[:].bitcast(U16).rearrange("p (u t m) -> p u t m", t=PACK, m=P),
+            w4_raw[:].bitcast(U16).rearrange("p (u m t) -> p u t m", t=PACK, m=P),
+        )
+        nc.vector.tensor_copy(
+            w4_sc[:].rearrange("p (u t m) -> p u t m", t=PACK, m=P),
+            w4_sc_raw[:].rearrange("p (u m t) -> p u t m", t=PACK, m=P),
+        )
+
+        v_sc = []
+        for a in range(PASSES):
+            picked = keep.tile([P, S], U8, name="v_sc%d" % a, align_bytes=64)
+            nc.vector.tensor_copy(picked[:], tab_sc[:, T * a : T * (a + 1)].indirect(picks[:]))
+            v_sc.append(picked)
+        v = {}
+
+        def gather_words(a, half):
+            picked = keep.tile([P, HALF], U32, name="v%d_%d" % (a, half), align_bytes=64)
+            cols = HALF // 16
+            nc.vector.tensor_copy(
+                picked[:], tab[a][:].bitcast(U32).indirect(picks[:, cols * half : cols * (half + 1)])
+            )
+            v[a, half] = picked
+
+        for a in range(PASSES):
+            for half in range(2):
+                gather_words(a, half)
+
+        w1_codes, w1_sc = {}, {}
+
+        def quantise_w1(g, a):
+            grouped = ring.tile([P, PACK * HALF], BF16, name="w1_bf", tag="w1_bf", bufs=2, align_bytes=64)
+            nc.vector.tensor_copy(
+                grouped[:].rearrange("p (t m j) -> p m j t", t=PACK, j=PACK),
+                w1_raw[g, a][:].rearrange("p j (m t) -> p m j t", t=PACK),
+            )
+            codes = keep.tile([P, HALF], U32, name="w1c%d_%d" % (g, a), align_bytes=64)
+            plane = keep.tile([P, HALF], U8, name="w1s%d_%d" % (g, a), align_bytes=64)
+            nc.vector.quantize_mx(out=codes[:].bitcast(FP8X4), scales=plane[:], in_=grouped[:])
+            w1_codes[g, a], w1_sc[g, a] = codes, plane
+
+        def moving(a, j0):
+            half, c0 = divmod(j0, HALF)
+            return v[a, half][:, c0 : c0 + SUB].bitcast(FP8X4), v_sc[a][:, j0 : j0 + SUB]
+
+        shrink = {}
+
+        def background(c, g):
+            r = ring.tile([P, CHUNK * PACK], F32, name="shrink", tag="shrink", bufs=8)
+            for s in range(CHUNK // SUB):
+                bank = psum.tile([P, PACK * SUB], F32, name="b_bank", tag="b_bank", bufs=3)
+                for t in range(PACK):
+                    for a in range(PASSES):
+                        col = H * a + HALF * g + P * t
+                        codes, plane = moving(a, CHUNK * c + SUB * s)
+                        nc.tensor.matmul_mx(
+                            out=bank[:, SUB * t : SUB * (t + 1)],
+                            lhsT=w4[:, 2 * col : 2 * (col + P)].bitcast(FP4X4),
+                            lhsT_scale=w4_sc[:, col : col + P],
+                            rhs=codes,
+                            rhs_scale=plane,
+                            start=(a == 0),
+                            stop=(a == PASSES - 1),
+                        )
+                nc.scalar.activation(
+                    r[:, PACK * SUB * s : PACK * SUB * (s + 1)].rearrange("p (j t) -> p j t", t=PACK),
+                    bank[:].rearrange("p (t j) -> p j t", t=PACK),
+                    ACT.Abs,
+                )
+            nc.scalar.activation(r[:], r[:], ACT.Abs_reciprocal_sqrt, bias=1.0)
+            nc.scalar.activation(r[:], r[:], ACT.Square)
+            shrink[c, g] = r
+
+        h_codes, h_sc = {}, {}
+
+        def features(c, g):
+            hb = ring.tile([P, CHUNK * PACK], BF16, name="h_bf", tag="turn%d" % g, bufs=1, align_bytes=64)
+            for s in range(CHUNK // SUB):
+                bank = psum.tile([P, PACK * SUB], F32, name="a_bank", tag="a_bank", bufs=3)
+                for t in range(PACK):
+                    for a in range(PASSES):
+                        codes, plane = moving(a, CHUNK * c + SUB * s)
+                        nc.tensor.matmul_mx(
+                            out=bank[:, SUB * t : SUB * (t + 1)],
+                            lhsT=w1_codes[g, a][:, P * t : P * (t + 1)].bitcast(FP8X4),
+                            lhsT_scale=w1_sc[g, a][:, P * t : P * (t + 1)],
+                            rhs=codes,
+                            rhs_scale=plane,
+                            start=(a == 0),
+                            stop=(a == PASSES - 1),
+                        )
+                cols = slice(PACK * SUB * s, PACK * SUB * (s + 1))
+                nc.vector.tensor_tensor(
+                    hb[:, cols].rearrange("p (j t) -> p j t", t=PACK),
+                    bank[:].rearrange("p (t j) -> p j t", t=PACK),
+                    shrink[c, g][:, cols].rearrange("p (j t) -> p j t", t=PACK),
+                    MULT,
+                )
+            codes = ring.tile([P, CHUNK], U32, name="h_codes", tag="h_codes", bufs=4, align_bytes=64)
+            plane = ring.tile([P, CHUNK], U8, name="h_sc", tag="h_sc", bufs=4, align_bytes=64)
+            nc.vector.quantize_mx(out=codes[:].bitcast(FP8X4), scales=plane[:], in_=hb[:])
+            h_codes[c, g], h_sc[c, g] = codes, plane
+
+        pages = [keep.tile([P, S], F32, name="page%d" % b) for b in range(BLOCKS)]
+        squares = {}
+
+        def damage(c):
+            share = gain[:, CHUNK * c : CHUNK * (c + 1)]
+            nc.scalar.activation(share, share, ACT.Square)
+            for pair in range(BLOCKS // 2):
+                bank = psum.tile([P, 2 * CHUNK], F32, name="y_bank", tag="y_bank", bufs=2)
+                for e in range(2):
+                    b = 2 * pair + e
+                    for g in range(2):
+                        nc.tensor.matmul_mx(
+                            out=bank[:, CHUNK * e : CHUNK * (e + 1)],
+                            lhsT=w8[:, N * g + P * b : N * g + P * (b + 1)].bitcast(FP8X4),
+                            lhsT_scale=w8_sc[4 * g : P, P * b : P * (b + 1)],
+                            rhs=h_codes[c, g][:].bitcast(FP8X4),
+                            rhs_scale=h_sc[c, g][:],
+                            start=(g == 0),
+                            stop=(g == 1),
+                        )
+                y2 = ring.tile([P, 2 * CHUNK], F32, name="y2", tag="turn%d" % pair, bufs=1, align_bytes=64)
+                nc.scalar.activation(y2[:], bank[:], ACT.Square)
+                squares[c, pair] = y2
+
+        def place(c, b):
+            cols = CHUNK // 16
+            y2 = squares[c, b // 2][:, CHUNK * (b % 2) : CHUNK * (b % 2 + 1)]
+            nc.vector.tensor_tensor(
+                pages[b][:].indirect(places[:, cols * c : cols * (c + 1)]),
+                y2,
+                gain[:, CHUNK * c : CHUNK * (c + 1)],
+                MULT,
+            )
+
+        held = []
+
+        def load_x0():
+            for pair in range(BLOCKS // 2):
+                x = ring.tile([P, 2, S], F32, name="big", tag="big", bufs=4)
+                rows = x0[2 * P * pair : 2 * P * (pair + 1), :]
+                nc.sync.dma_start(x[:], rows.rearrange("(e p) m -> p e m", p=P))
+                held.append(x)
+
+        def temper(b):
+            f = ring.tile([P, S], F32, name="factor", tag="factor", bufs=3)
+            width = HALF if b + 1 == BLOCKS else S
+            for m0 in range(0, S, width):
+                cols = slice(m0, m0 + width)
+                nc.scalar.activation(f[:, cols], pages[b][:, cols], ACT.Abs_reciprocal_sqrt, bias=1.0)
+                nc.scalar.activation(f[:, cols], f[:, cols], ACT.Square)
+                nc.vector.tensor_tensor(f[:, cols], f[:, cols], held[b // 2][:, b % 2, cols], MULT)
+                nc.sync.dma_start(out[P * b : P * (b + 1), cols], f[:, cols])
+
+        for g in range(2):
+            background(0, g)
+        for g in range(2):
+            for a in range(PASSES):
+                quantise_w1(g, a)
+        load_x0()
+        for g in range(2):
+            features(0, g)
+        for c in range(CHUNKS):
+            if c + 1 < CHUNKS:
+                for g in range(2):
+                    background(c + 1, g)
+                for g in range(2):
+                    features(c + 1, g)
+            damage(c)
+            for b in range(BLOCKS):
+                place(c, b)
+                if c + 1 == CHUNKS:
+                    temper(b)

@@ -25,6 +25,7 @@ CHUNK = 256
 SUB = 128
 CHUNKS = S // CHUNK
 BLOCKS = N // P
+SLOT = 4 * PACK * HALF
 
 
 def tile_list_adna_damage_tempering_kernel(
@@ -34,22 +35,23 @@ def tile_list_adna_damage_tempering_kernel(
     with ExitStack() as ctx:
         keep = ctx.enter_context(tc.tile_pool(name="keep", bufs=1))
         ring = ctx.enter_context(tc.tile_pool(name="ring", bufs=2))
+        stage = ctx.enter_context(tc.tile_pool(name="stage", bufs=1))
         psum = ctx.enter_context(tc.psum_pool(name="psum", bufs=1))
 
         picks = keep.tile([P, S // 16], U16, name="picks")
         places = keep.tile([P, S // 16], U16, name="places")
         nc.sync.dma_start(picks[:], offs)
+        nc.sync.dma_start(places[:], offs2)
 
+        tab_sc = stage.tile([P, T], U8, name="tab_sc", align_bytes=64, offset=SLOT - T // 2)
         w4_sc_raw = keep.tile([P, PASSES * H], U8, name="w4_sc_raw", align_bytes=64)
-        tab_sc = keep.tile([P, PASSES * T], U8, name="tab_sc", align_bytes=64)
-        w8_sc = keep.tile([P, N], U8, name="w8_sc", align_bytes=64)
-        nc.vector.memset(w4_sc_raw[:].bitcast(I32), 0)
-        nc.vector.memset(tab_sc[:].bitcast(I32), 0)
-        nc.vector.memset(w8_sc[:].bitcast(I32), 0)
+        v_sc = keep.tile([P, PASSES * S], U8, name="v_sc", align_bytes=64)
+        for plane in (tab_sc, w4_sc_raw, v_sc):
+            nc.vector.memset(plane[:].bitcast(I32), 0)
 
         warm_in = keep.tile([P, 1], F32, name="warm_in")
         warm_out = keep.tile([P, 1], F32, name="warm_out")
-        nc.gpsimd.memset(warm_in[:], 1.0)
+        nc.vector.memset(warm_in[:], 1.0)
         nc.scalar.activation(warm_out[:], warm_in[:], ACT.Abs_reciprocal_sqrt)
 
         w4_raw = keep.tile([P, PASSES * 2 * H], U8, name="w4_raw", align_bytes=64)
@@ -57,15 +59,11 @@ def tile_list_adna_damage_tempering_kernel(
             w4_raw[:].bitcast(I32).rearrange("p (a n) -> p a n", a=PASSES),
             w4_words.bitcast(I32).rearrange("a p n -> p a n"),
         )
+        nc.sync.dma_start(tab_sc[0:P:4, :].bitcast(I32), tab_scales.bitcast(I32).rearrange("a q n -> q a n"))
         for q in range(4):
             nc.sync.dma_start(
                 w4_sc_raw[32 * q : 32 * q + 4, :].bitcast(I32).rearrange("r (a n) -> r a n", a=PASSES),
                 w4_scales[:, 4 * q : 4 * q + 4, :].bitcast(I32).rearrange("a r n -> r a n"),
-            )
-        for q in range(4):
-            nc.sync.dma_start(
-                tab_sc[32 * q : 32 * q + 4, :].bitcast(I32).rearrange("r (a n) -> r a n", a=PASSES),
-                tab_scales[:, 4 * q : 4 * q + 4, :].bitcast(I32).rearrange("a r n -> r a n"),
             )
         tab = []
         for a in range(PASSES):
@@ -73,27 +71,23 @@ def tile_list_adna_damage_tempering_kernel(
             nc.sync.dma_start(words[:], tab_words[a].rearrange("p n i -> p (n i)").bitcast(I32))
             tab.append(words)
 
+        v_sc_spread = stage.tile([P, S], U8, name="v_sc_spread", align_bytes=64, offset=3 * SLOT - S // 2)
+        nc.vector.tensor_copy(v_sc_spread[:], tab_sc[:].indirect(picks[:]))
+        for q in range(4):
+            nc.sync.dma_start(
+                v_sc[32 * q : 32 * q + 4, :].bitcast(I32).rearrange("r (a n) -> r a n", a=PASSES),
+                v_sc_spread[32 * q : 32 * q + 32 : 4, :].bitcast(I32),
+            )
+
         w1_raw = {}
         for g in range(2):
             for a in range(PASSES):
-                raw = ring.tile([P, PACK, HALF], F32, name="big", tag="big", bufs=4)
+                raw = stage.tile(
+                    [P, PACK, HALF], F32, name="w1_raw%d_%d" % (g, a), align_bytes=64, offset=SLOT * (2 * g + a)
+                )
                 rows = w1[KP * a : KP * (a + 1), HALF * g : HALF * (g + 1)]
                 nc.sync.dma_start(raw[:], rows.rearrange("(p j) c -> p j c", j=PACK))
                 w1_raw[g, a] = raw
-
-        w8 = keep.tile([P, PASSES * N], I32, name="w8", align_bytes=64)
-        nc.sync.dma_start(
-            w8[:].rearrange("p (a n) -> p a n", a=PASSES),
-            w8_words.rearrange("a p n i -> p a (n i)").bitcast(I32),
-        )
-        for q in range(4):
-            nc.sync.dma_start(
-                w8_sc[32 * q : 32 * q + 8, :].bitcast(I32),
-                w8_scales[:, 4 * q : 4 * q + 4, :].bitcast(I32),
-            )
-        gain = keep.tile([P, S], F32, name="gain")
-        nc.sync.dma_start(gain[:], wgo)
-        nc.sync.dma_start(places[:], offs2)
 
         w4 = keep.tile([P, PASSES * 2 * H], U8, name="w4", align_bytes=64)
         w4_sc = keep.tile([P, PASSES * H], U8, name="w4_sc", align_bytes=64)
@@ -101,37 +95,34 @@ def tile_list_adna_damage_tempering_kernel(
             w4[:].bitcast(U16).rearrange("p (u t m) -> p u t m", t=PACK, m=P),
             w4_raw[:].bitcast(U16).rearrange("p (u m t) -> p u t m", t=PACK, m=P),
         )
-        nc.vector.tensor_copy(
-            w4_sc[:].rearrange("p (u t m) -> p u t m", t=PACK, m=P),
-            w4_sc_raw[:].rearrange("p (u m t) -> p u t m", t=PACK, m=P),
-        )
-
-        v_sc = []
-        for a in range(PASSES):
-            picked = keep.tile([P, S], U8, name="v_sc%d" % a, align_bytes=64)
-            nc.vector.tensor_copy(picked[:], tab_sc[:, T * a : T * (a + 1)].indirect(picks[:]))
-            v_sc.append(picked)
         v = {}
 
         def gather_words(a, half):
-            picked = keep.tile([P, HALF], U32, name="v%d_%d" % (a, half), align_bytes=64)
+            tag = "last" if (a, half) == (1, 1) else "v%d_%d" % (a, half)
+            picked = ring.tile([P, HALF], U32, name="v", tag=tag, bufs=1, align_bytes=64)
             cols = HALF // 16
             nc.vector.tensor_copy(
                 picked[:], tab[a][:].bitcast(U32).indirect(picks[:, cols * half : cols * (half + 1)])
             )
             v[a, half] = picked
 
-        for a in range(PASSES):
-            for half in range(2):
-                gather_words(a, half)
+        gather_words(0, 0)
+        nc.vector.tensor_copy(
+            w4_sc[:].rearrange("p (u t m) -> p u t m", t=PACK, m=P),
+            w4_sc_raw[:].rearrange("p (u m t) -> p u t m", t=PACK, m=P),
+        )
+
+        gather_words(0, 1)
+        gather_words(1, 0)
 
         w1_codes, w1_sc = {}, {}
 
         def quantise_w1(g, a):
-            grouped = ring.tile([P, PACK * HALF], BF16, name="w1_bf", tag="w1_bf", bufs=2, align_bytes=64)
+            tag = "last" if (g, a) == (1, 1) else "turn%d" % a
+            grouped = ring.tile([P, PACK * HALF], BF16, name="w1_bf", tag=tag, bufs=1, align_bytes=64)
             nc.vector.tensor_copy(
-                grouped[:].rearrange("p (t m j) -> p m j t", t=PACK, j=PACK),
-                w1_raw[g, a][:].rearrange("p j (m t) -> p m j t", t=PACK),
+                grouped[:].rearrange("p (t m j) -> p m t j", t=PACK, j=PACK),
+                w1_raw[g, a][:].rearrange("p j (m t) -> p m t j", t=PACK),
             )
             codes = keep.tile([P, HALF], U32, name="w1c%d_%d" % (g, a), align_bytes=64)
             plane = keep.tile([P, HALF], U8, name="w1s%d_%d" % (g, a), align_bytes=64)
@@ -140,14 +131,14 @@ def tile_list_adna_damage_tempering_kernel(
 
         def moving(a, j0):
             half, c0 = divmod(j0, HALF)
-            return v[a, half][:, c0 : c0 + SUB].bitcast(FP8X4), v_sc[a][:, j0 : j0 + SUB]
+            return v[a, half][:, c0 : c0 + SUB].bitcast(FP8X4), v_sc[:, S * a + j0 : S * a + j0 + SUB]
 
         shrink = {}
 
         def background(c, g):
-            r = ring.tile([P, CHUNK * PACK], F32, name="shrink", tag="shrink", bufs=8)
+            parts = []
             for s in range(CHUNK // SUB):
-                bank = psum.tile([P, PACK * SUB], F32, name="b_bank", tag="b_bank", bufs=3)
+                bank = psum.tile([P, PACK * SUB], F32, name="b_bank", tag="b_bank%d" % s)
                 for t in range(PACK):
                     for a in range(PASSES):
                         col = H * a + HALF * g + P * t
@@ -161,21 +152,26 @@ def tile_list_adna_damage_tempering_kernel(
                             start=(a == 0),
                             stop=(a == PASSES - 1),
                         )
+                r = ring.tile([P, SUB * PACK], F32, name="shrink", tag="shrink%d%d" % (g, s), bufs=2)
+                parts.append(r[:])
                 nc.scalar.activation(
-                    r[:, PACK * SUB * s : PACK * SUB * (s + 1)].rearrange("p (j t) -> p j t", t=PACK),
+                    r[:].rearrange("p (j t) -> p j t", t=PACK),
                     bank[:].rearrange("p (t j) -> p j t", t=PACK),
                     ACT.Abs,
                 )
-            nc.scalar.activation(r[:], r[:], ACT.Abs_reciprocal_sqrt, bias=1.0)
-            nc.scalar.activation(r[:], r[:], ACT.Square)
-            shrink[c, g] = r
+            for part in parts:
+                nc.scalar.activation(part, part, ACT.Abs_reciprocal_sqrt, bias=1.0)
+            for part in parts:
+                nc.scalar.activation(part, part, ACT.Square)
+            shrink[c, g] = parts
 
         h_codes, h_sc = {}, {}
 
         def features(c, g):
-            hb = ring.tile([P, CHUNK * PACK], BF16, name="h_bf", tag="turn%d" % g, bufs=1, align_bytes=64)
+            tag = "last" if (c < 2 and g == 0) else "turn%d" % g
+            hb = ring.tile([P, CHUNK * PACK], BF16, name="h_bf", tag=tag, bufs=1, align_bytes=64)
             for s in range(CHUNK // SUB):
-                bank = psum.tile([P, PACK * SUB], F32, name="a_bank", tag="a_bank", bufs=3)
+                bank = psum.tile([P, PACK * SUB], F32, name="a_bank", tag="a_bank%d%d" % (c if c < 2 else g, s))
                 for t in range(PACK):
                     for a in range(PASSES):
                         codes, plane = moving(a, CHUNK * c + SUB * s)
@@ -192,7 +188,7 @@ def tile_list_adna_damage_tempering_kernel(
                 nc.vector.tensor_tensor(
                     hb[:, cols].rearrange("p (j t) -> p j t", t=PACK),
                     bank[:].rearrange("p (t j) -> p j t", t=PACK),
-                    shrink[c, g][:, cols].rearrange("p (j t) -> p j t", t=PACK),
+                    shrink[c, g][s].rearrange("p (j t) -> p j t", t=PACK),
                     MULT,
                 )
             codes = ring.tile([P, CHUNK], U32, name="h_codes", tag="h_codes", bufs=4, align_bytes=64)
@@ -220,7 +216,8 @@ def tile_list_adna_damage_tempering_kernel(
                             start=(g == 0),
                             stop=(g == 1),
                         )
-                y2 = ring.tile([P, 2 * CHUNK], F32, name="y2", tag="turn%d" % pair, bufs=1, align_bytes=64)
+                tag = "first%d" % pair if c == 0 else "turn%d" % pair
+                y2 = ring.tile([P, 2 * CHUNK], F32, name="y2", tag=tag, bufs=1, align_bytes=64)
                 nc.scalar.activation(y2[:], bank[:], ACT.Square)
                 squares[c, pair] = y2
 
@@ -238,31 +235,52 @@ def tile_list_adna_damage_tempering_kernel(
 
         def load_x0():
             for pair in range(BLOCKS // 2):
-                x = ring.tile([P, 2, S], F32, name="big", tag="big", bufs=4)
+                x = stage.tile([P, 2, S], F32, name="x0_%d" % pair, align_bytes=64, offset=SLOT * (2 + pair))
                 rows = x0[2 * P * pair : 2 * P * (pair + 1), :]
                 nc.sync.dma_start(x[:], rows.rearrange("(e p) m -> p e m", p=P))
                 held.append(x)
 
         def temper(b):
             f = ring.tile([P, S], F32, name="factor", tag="factor", bufs=3)
-            width = HALF if b + 1 == BLOCKS else S
-            for m0 in range(0, S, width):
-                cols = slice(m0, m0 + width)
+            halves = [slice(m0, m0 + HALF) for m0 in range(0, S, HALF)]
+            for cols in halves:
                 nc.scalar.activation(f[:, cols], pages[b][:, cols], ACT.Abs_reciprocal_sqrt, bias=1.0)
+            for cols in halves:
                 nc.scalar.activation(f[:, cols], f[:, cols], ACT.Square)
+            for cols in halves if b + 1 == BLOCKS else [slice(0, S)]:
                 nc.vector.tensor_tensor(f[:, cols], f[:, cols], held[b // 2][:, b % 2, cols], MULT)
                 nc.sync.dma_start(out[P * b : P * (b + 1), cols], f[:, cols])
 
-        for g in range(2):
-            background(0, g)
-        for g in range(2):
-            for a in range(PASSES):
-                quantise_w1(g, a)
+        background(0, 0)
+        background(1, 0)
+        quantise_w1(0, 0)
+        quantise_w1(0, 1)
+        quantise_w1(1, 0)
+        features(0, 0)
+        features(1, 0)
+        quantise_w1(1, 1)
+        gather_words(1, 1)
+        w8 = stage.tile([P, PASSES * N], I32, name="w8", align_bytes=64, offset=0)
+        nc.sync.dma_start(
+            w8[:].rearrange("p (a n) -> p a n", a=PASSES),
+            w8_words.rearrange("a p n i -> p a (n i)").bitcast(I32),
+        )
+        w8_sc = stage.tile([P, N], U8, name="w8_sc", align_bytes=64, offset=SLOT // 2)
+        nc.gpsimd.memset(w8_sc[:].bitcast(I32), 0)
+        for q in range(4):
+            nc.sync.dma_start(
+                w8_sc[32 * q : 32 * q + 8, :].bitcast(I32),
+                w8_scales[:, 4 * q : 4 * q + 4, :].bitcast(I32),
+            )
+        gain = stage.tile([P, S], F32, name="gain", align_bytes=64, offset=SLOT)
+        nc.sync.dma_start(gain[:], wgo)
         load_x0()
-        for g in range(2):
-            features(0, g)
+        for c in range(2):
+            background(c, 1)
+        for c in range(2):
+            features(c, 1)
         for c in range(CHUNKS):
-            if c + 1 < CHUNKS:
+            if 2 <= c + 1 < CHUNKS:
                 for g in range(2):
                     background(c + 1, g)
                 for g in range(2):

@@ -41,7 +41,6 @@ def tile_list_adna_damage_tempering_kernel(
         picks = keep.tile([P, S // 16], U16, name="picks")
         places = keep.tile([P, S // 16], U16, name="places")
         nc.sync.dma_start(picks[:], offs)
-        nc.sync.dma_start(places[:], offs2)
 
         tab_sc = stage.tile([P, T], U8, name="tab_sc", align_bytes=64, offset=SLOT - T // 2)
         w4_sc_raw = keep.tile([P, PASSES * H], U8, name="w4_sc_raw", align_bytes=64)
@@ -55,21 +54,23 @@ def tile_list_adna_damage_tempering_kernel(
         nc.scalar.activation(warm_out[:], warm_in[:], ACT.Abs_reciprocal_sqrt)
 
         w4_raw = keep.tile([P, PASSES * 2 * H], U8, name="w4_raw", align_bytes=64)
-        nc.sync.dma_start(
-            w4_raw[:].bitcast(I32).rearrange("p (a n) -> p a n", a=PASSES),
-            w4_words.bitcast(I32).rearrange("a p n -> p a n"),
-        )
+        for a in range(PASSES):
+            nc.sync.dma_start(w4_raw[:, 2 * H * a : 2 * H * (a + 1)].bitcast(I32), w4_words[a].bitcast(I32))
         nc.sync.dma_start(tab_sc[0:P:4, :].bitcast(I32), tab_scales.bitcast(I32).rearrange("a q n -> q a n"))
+        tab = []
+
+        def load_table(a):
+            words = keep.tile([P, T], I32, name="tab%d" % a, align_bytes=64)
+            nc.sync.dma_start(words[:], tab_words[a].rearrange("p n i -> p (n i)").bitcast(I32))
+            tab.append(words)
+
+        load_table(0)
         for q in range(4):
             nc.sync.dma_start(
                 w4_sc_raw[32 * q : 32 * q + 4, :].bitcast(I32).rearrange("r (a n) -> r a n", a=PASSES),
                 w4_scales[:, 4 * q : 4 * q + 4, :].bitcast(I32).rearrange("a r n -> r a n"),
             )
-        tab = []
-        for a in range(PASSES):
-            words = keep.tile([P, T], I32, name="tab%d" % a, align_bytes=64)
-            nc.sync.dma_start(words[:], tab_words[a].rearrange("p n i -> p (n i)").bitcast(I32))
-            tab.append(words)
+        load_table(1)
 
         v_sc_spread = stage.tile([P, S], U8, name="v_sc_spread", align_bytes=64, offset=3 * SLOT - S // 2)
         nc.vector.tensor_copy(v_sc_spread[:], tab_sc[:].indirect(picks[:]))
@@ -98,8 +99,7 @@ def tile_list_adna_damage_tempering_kernel(
         v = {}
 
         def gather_words(a, half):
-            tag = "last" if (a, half) == (1, 1) else "v%d_%d" % (a, half)
-            picked = ring.tile([P, HALF], U32, name="v", tag=tag, bufs=1, align_bytes=64)
+            picked = keep.tile([P, HALF], U32, name="v%d_%d" % (a, half), align_bytes=64)
             cols = HALF // 16
             nc.vector.tensor_copy(
                 picked[:], tab[a][:].bitcast(U32).indirect(picks[:, cols * half : cols * (half + 1)])
@@ -107,19 +107,18 @@ def tile_list_adna_damage_tempering_kernel(
             v[a, half] = picked
 
         gather_words(0, 0)
+        gather_words(0, 1)
         nc.vector.tensor_copy(
             w4_sc[:].rearrange("p (u t m) -> p u t m", t=PACK, m=P),
             w4_sc_raw[:].rearrange("p (u m t) -> p u t m", t=PACK, m=P),
         )
-
-        gather_words(0, 1)
         gather_words(1, 0)
+        gather_words(1, 1)
 
         w1_codes, w1_sc = {}, {}
 
         def quantise_w1(g, a):
-            tag = "last" if (g, a) == (1, 1) else "turn%d" % a
-            grouped = ring.tile([P, PACK * HALF], BF16, name="w1_bf", tag=tag, bufs=1, align_bytes=64)
+            grouped = ring.tile([P, PACK * HALF], BF16, name="w1_bf", tag="w1_bf", bufs=2, align_bytes=64)
             nc.vector.tensor_copy(
                 grouped[:].rearrange("p (t m j) -> p m t j", t=PACK, j=PACK),
                 w1_raw[g, a][:].rearrange("p j (m t) -> p m t j", t=PACK),
@@ -152,7 +151,7 @@ def tile_list_adna_damage_tempering_kernel(
                             start=(a == 0),
                             stop=(a == PASSES - 1),
                         )
-                r = ring.tile([P, SUB * PACK], F32, name="shrink", tag="shrink%d%d" % (g, s), bufs=2)
+                r = ring.tile([P, SUB * PACK], F32, name="shrink", tag="shrink", bufs=10)
                 parts.append(r[:])
                 nc.scalar.activation(
                     r[:].rearrange("p (j t) -> p j t", t=PACK),
@@ -168,10 +167,12 @@ def tile_list_adna_damage_tempering_kernel(
         h_codes, h_sc = {}, {}
 
         def features(c, g):
-            tag = "last" if (c < 2 and g == 0) else "turn%d" % g
-            hb = ring.tile([P, CHUNK * PACK], BF16, name="h_bf", tag=tag, bufs=1, align_bytes=64)
+            if (c, g) == (CHUNKS - 1, 1):
+                hb = ring.tile([P, CHUNK * PACK], BF16, name="h_bf", tag="late_page", bufs=1, align_bytes=64)
+            else:
+                hb = ring.tile([P, CHUNK * PACK], BF16, name="h_bf", tag="h_bf", bufs=2, align_bytes=64)
             for s in range(CHUNK // SUB):
-                bank = psum.tile([P, PACK * SUB], F32, name="a_bank", tag="a_bank%d%d" % (c if c < 2 else g, s))
+                bank = psum.tile([P, PACK * SUB], F32, name="a_bank", tag="a_bank%d%d" % (g, s))
                 for t in range(PACK):
                     for a in range(PASSES):
                         codes, plane = moving(a, CHUNK * c + SUB * s)
@@ -191,43 +192,43 @@ def tile_list_adna_damage_tempering_kernel(
                     shrink[c, g][s].rearrange("p (j t) -> p j t", t=PACK),
                     MULT,
                 )
-            codes = ring.tile([P, CHUNK], U32, name="h_codes", tag="h_codes", bufs=4, align_bytes=64)
-            plane = ring.tile([P, CHUNK], U8, name="h_sc", tag="h_sc", bufs=4, align_bytes=64)
+            codes = ring.tile([P, CHUNK], U32, name="h_codes", tag="h_codes", bufs=8, align_bytes=64)
+            plane = ring.tile([P, CHUNK], U8, name="h_sc", tag="h_sc", bufs=8, align_bytes=64)
             nc.vector.quantize_mx(out=codes[:].bitcast(FP8X4), scales=plane[:], in_=hb[:])
             h_codes[c, g], h_sc[c, g] = codes, plane
 
-        pages = [keep.tile([P, S], F32, name="page%d" % b) for b in range(BLOCKS)]
-        squares = {}
+        pages = {}
 
-        def damage(c):
+        def weigh(c):
             share = gain[:, CHUNK * c : CHUNK * (c + 1)]
             nc.scalar.activation(share, share, ACT.Square)
-            for pair in range(BLOCKS // 2):
-                bank = psum.tile([P, 2 * CHUNK], F32, name="y_bank", tag="y_bank", bufs=2)
-                for e in range(2):
-                    b = 2 * pair + e
-                    for g in range(2):
-                        nc.tensor.matmul_mx(
-                            out=bank[:, CHUNK * e : CHUNK * (e + 1)],
-                            lhsT=w8[:, N * g + P * b : N * g + P * (b + 1)].bitcast(FP8X4),
-                            lhsT_scale=w8_sc[4 * g : P, P * b : P * (b + 1)],
-                            rhs=h_codes[c, g][:].bitcast(FP8X4),
-                            rhs_scale=h_sc[c, g][:],
-                            start=(g == 0),
-                            stop=(g == 1),
-                        )
-                tag = "first%d" % pair if c == 0 else "turn%d" % pair
-                y2 = ring.tile([P, 2 * CHUNK], F32, name="y2", tag=tag, bufs=1, align_bytes=64)
-                nc.scalar.activation(y2[:], bank[:], ACT.Square)
-                squares[c, pair] = y2
 
-        def place(c, b):
-            cols = CHUNK // 16
-            y2 = squares[c, b // 2][:, CHUNK * (b % 2) : CHUNK * (b % 2 + 1)]
+        def damage(b, chunks):
+            width = CHUNK * len(chunks)
+            bank = psum.tile([P, width], F32, name="y_bank", tag="y_bank", bufs=2)
+            for e, c in enumerate(chunks):
+                for g in range(2):
+                    nc.tensor.matmul_mx(
+                        out=bank[:, CHUNK * e : CHUNK * (e + 1)],
+                        lhsT=w8[:, N * g + P * b : N * g + P * (b + 1)].bitcast(FP8X4),
+                        lhsT_scale=w8_sc[4 * g : P, P * b : P * (b + 1)],
+                        rhs=h_codes[c, g][:].bitcast(FP8X4),
+                        rhs_scale=h_sc[c, g][:],
+                        start=(g == 0),
+                        stop=(g == 1),
+                    )
+            y2 = keep.tile([P, width], F32, name="y2_%d_%d" % (b, chunks[0]), align_bytes=64)
+            nc.scalar.activation(y2[:], bank[:], ACT.Square)
+            if b not in pages:
+                if b + 1 == BLOCKS:
+                    pages[b] = ring.tile([P, S], F32, name="page", tag="late_page", bufs=1, align_bytes=64)
+                else:
+                    pages[b] = keep.tile([P, S], F32, name="page%d" % b)
+            j0 = CHUNK * chunks[0]
             nc.vector.tensor_tensor(
-                pages[b][:].indirect(places[:, cols * c : cols * (c + 1)]),
-                y2,
-                gain[:, CHUNK * c : CHUNK * (c + 1)],
+                pages[b][:].indirect(places[:, j0 // 16 : (j0 + width) // 16]),
+                y2[:],
+                gain[:, j0 : j0 + width],
                 MULT,
             )
 
@@ -241,25 +242,24 @@ def tile_list_adna_damage_tempering_kernel(
                 held.append(x)
 
         def temper(b):
-            f = ring.tile([P, S], F32, name="factor", tag="factor", bufs=3)
+            f = ring.tile([P, S], F32, name="factor", tag="factor", bufs=4)
             halves = [slice(m0, m0 + HALF) for m0 in range(0, S, HALF)]
             for cols in halves:
                 nc.scalar.activation(f[:, cols], pages[b][:, cols], ACT.Abs_reciprocal_sqrt, bias=1.0)
             for cols in halves:
                 nc.scalar.activation(f[:, cols], f[:, cols], ACT.Square)
-            for cols in halves if b + 1 == BLOCKS else [slice(0, S)]:
+            for cols in halves if b > 0 else [slice(0, S)]:
                 nc.vector.tensor_tensor(f[:, cols], f[:, cols], held[b // 2][:, b % 2, cols], MULT)
                 nc.sync.dma_start(out[P * b : P * (b + 1), cols], f[:, cols])
 
         background(0, 0)
-        background(1, 0)
+        background(0, 1)
         quantise_w1(0, 0)
         quantise_w1(0, 1)
         quantise_w1(1, 0)
         features(0, 0)
-        features(1, 0)
+        background(1, 0)
         quantise_w1(1, 1)
-        gather_words(1, 1)
         w8 = stage.tile([P, PASSES * N], I32, name="w8", align_bytes=64, offset=0)
         nc.sync.dma_start(
             w8[:].rearrange("p (a n) -> p a n", a=PASSES),
@@ -272,21 +272,36 @@ def tile_list_adna_damage_tempering_kernel(
                 w8_sc[32 * q : 32 * q + 8, :].bitcast(I32),
                 w8_scales[:, 4 * q : 4 * q + 4, :].bitcast(I32),
             )
+        nc.sync.dma_start(places[:], offs2)
         gain = stage.tile([P, S], F32, name="gain", align_bytes=64, offset=SLOT)
         nc.sync.dma_start(gain[:], wgo)
         load_x0()
-        for c in range(2):
-            background(c, 1)
-        for c in range(2):
-            features(c, 1)
-        for c in range(CHUNKS):
-            if 2 <= c + 1 < CHUNKS:
-                for g in range(2):
-                    background(c + 1, g)
-                for g in range(2):
-                    features(c + 1, g)
-            damage(c)
-            for b in range(BLOCKS):
-                place(c, b)
-                if c + 1 == CHUNKS:
-                    temper(b)
+        features(0, 1)
+        features(1, 0)
+
+        def unit(c, g):
+            background(c, g)
+            features(c, g)
+
+        weigh(0)
+        damage(0, [0])
+        damage(1, [0])
+        unit(1, 1)
+        damage(2, [0])
+        weigh(1)
+        unit(2, 0)
+        damage(0, [1])
+        unit(2, 1)
+        damage(1, [1])
+        weigh(2)
+        unit(3, 0)
+        damage(2, [1])
+        weigh(3)
+        unit(3, 1)
+        damage(3, [0, 1])
+        for b in range(BLOCKS - 1):
+            damage(b, [2, 3])
+        temper(0)
+        damage(3, [2, 3])
+        for b in range(1, BLOCKS):
+            temper(b)

@@ -25,6 +25,8 @@ CHUNK = 256
 SUB = 128
 CHUNKS = S // CHUNK
 BLOCKS = N // P
+EARLY_FACTOR = 3
+GPSIMD_HALVES = 5
 SLOT = 4 * PACK * HALF
 
 
@@ -203,7 +205,7 @@ def tile_list_adna_damage_tempering_kernel(
             share = gain[:, CHUNK * c : CHUNK * (c + 1)]
             nc.scalar.activation(share, share, ACT.Square)
 
-        def damage(b, chunks):
+        def damage_values(b, chunks, weighed=True):
             width = CHUNK * len(chunks)
             bank = psum.tile([P, width], F32, name="y_bank", tag="y_bank", bufs=2)
             for e, c in enumerate(chunks):
@@ -219,18 +221,33 @@ def tile_list_adna_damage_tempering_kernel(
                     )
             y2 = keep.tile([P, width], F32, name="y2_%d_%d" % (b, chunks[0]), align_bytes=64)
             nc.scalar.activation(y2[:], bank[:], ACT.Square)
+            if weighed:
+                j0 = CHUNK * chunks[0]
+                nc.gpsimd.tensor_tensor(y2[:], y2[:], gain[:, j0 : j0 + width], MULT)
+            return y2
+
+        def factor(values):
+            nc.scalar.activation(values[:], values[:], ACT.Abs_reciprocal_sqrt, bias=1.0)
+            nc.scalar.activation(values[:], values[:], ACT.Square)
+
+        def place(b, chunks, values, weighed=True):
             if b not in pages:
                 if b + 1 == BLOCKS:
                     pages[b] = ring.tile([P, S], F32, name="page", tag="late_page", bufs=1, align_bytes=64)
                 else:
                     pages[b] = keep.tile([P, S], F32, name="page%d" % b)
-            j0 = CHUNK * chunks[0]
-            nc.vector.tensor_tensor(
-                pages[b][:].indirect(places[:, j0 // 16 : (j0 + width) // 16]),
-                y2[:],
-                gain[:, j0 : j0 + width],
-                MULT,
-            )
+            j0, width = CHUNK * chunks[0], CHUNK * len(chunks)
+            window = pages[b][:].indirect(places[:, j0 // 16 : (j0 + width) // 16])
+            if weighed:
+                nc.vector.tensor_copy(window, values[:])
+            else:
+                nc.vector.tensor_tensor(window, values[:], gain[:, j0 : j0 + width], MULT)
+
+        def damage(b, chunks, weighed=True):
+            values = damage_values(b, chunks, weighed)
+            if b >= EARLY_FACTOR:
+                factor(values)
+            place(b, chunks, values, weighed)
 
         held = []
 
@@ -244,12 +261,16 @@ def tile_list_adna_damage_tempering_kernel(
         def temper(b):
             f = ring.tile([P, S], F32, name="factor", tag="factor", bufs=4)
             halves = [slice(m0, m0 + HALF) for m0 in range(0, S, HALF)]
-            for cols in halves:
-                nc.scalar.activation(f[:, cols], pages[b][:, cols], ACT.Abs_reciprocal_sqrt, bias=1.0)
-            for cols in halves:
-                nc.scalar.activation(f[:, cols], f[:, cols], ACT.Square)
-            for cols in halves if b > 0 else [slice(0, S)]:
-                nc.vector.tensor_tensor(f[:, cols], f[:, cols], held[b // 2][:, b % 2, cols], MULT)
+            placed = pages[b]
+            if b < EARLY_FACTOR:
+                for cols in halves:
+                    nc.scalar.activation(f[:, cols], placed[:, cols], ACT.Abs_reciprocal_sqrt, bias=1.0)
+                for cols in halves:
+                    nc.scalar.activation(f[:, cols], f[:, cols], ACT.Square)
+                placed = f
+            for e, cols in enumerate(halves):
+                engine = nc.gpsimd if 2 * b + e < GPSIMD_HALVES else nc.vector
+                engine.tensor_tensor(f[:, cols], placed[:, cols], held[b // 2][:, b % 2, cols], MULT)
                 nc.sync.dma_start(out[P * b : P * (b + 1), cols], f[:, cols])
 
         background(0, 0)
@@ -284,8 +305,8 @@ def tile_list_adna_damage_tempering_kernel(
             features(c, g)
 
         weigh(0)
-        damage(0, [0])
-        damage(1, [0])
+        damage(0, [0], weighed=False)
+        damage(1, [0], weighed=False)
         unit(1, 1)
         damage(2, [0])
         weigh(1)
@@ -297,11 +318,12 @@ def tile_list_adna_damage_tempering_kernel(
         unit(3, 0)
         damage(2, [1])
         weigh(3)
-        unit(3, 1)
-        damage(3, [0, 1])
-        for b in range(BLOCKS - 1):
+        late = damage_values(3, [0, 1])
+        background(3, 1)
+        factor(late)
+        features(3, 1)
+        place(3, [0, 1], late)
+        for b in range(BLOCKS):
             damage(b, [2, 3])
-        temper(0)
-        damage(3, [2, 3])
-        for b in range(1, BLOCKS):
+        for b in range(BLOCKS):
             temper(b)

@@ -26,7 +26,6 @@ SUB = 128
 CHUNKS = S // CHUNK
 BLOCKS = N // P
 EARLY_FACTOR = 3
-GPSIMD_HALVES = 5
 SLOT = 4 * PACK * HALF
 
 
@@ -120,7 +119,10 @@ def tile_list_adna_damage_tempering_kernel(
         w1_codes, w1_sc = {}, {}
 
         def quantise_w1(g, a):
-            grouped = ring.tile([P, PACK * HALF], BF16, name="w1_bf", tag="w1_bf", bufs=2, align_bytes=64)
+            if (g, a) == (1, 1):
+                grouped = stage.tile([P, PACK * HALF], BF16, name="w1_bf_last", align_bytes=64, offset=4 * SLOT)
+            else:
+                grouped = ring.tile([P, PACK * HALF], BF16, name="w1_bf", tag="w1_bf", bufs=2, align_bytes=64)
             nc.vector.tensor_copy(
                 grouped[:].rearrange("p (t m j) -> p m t j", t=PACK, j=PACK),
                 w1_raw[g, a][:].rearrange("p j (m t) -> p m t j", t=PACK),
@@ -135,11 +137,18 @@ def tile_list_adna_damage_tempering_kernel(
             return v[a, half][:, c0 : c0 + SUB].bitcast(FP8X4), v_sc[:, S * a + j0 : S * a + j0 + SUB]
 
         shrink = {}
+        banks = [psum.tile([P, PACK * SUB], F32, name="bank%d" % e) for e in range(6)]
+
+        def b_pair(c, g):
+            return [0, 1, 0, 2, 0, 1, 2, 0][2 * c + g]
+
+        def a_pair(c, g):
+            return [2, 0, 1, 2, 0, 1, 2, 0][2 * c + g]
 
         def background(c, g):
             parts = []
             for s in range(CHUNK // SUB):
-                bank = psum.tile([P, PACK * SUB], F32, name="b_bank", tag="b_bank%d" % s)
+                bank = banks[2 * b_pair(c, g) + s]
                 for t in range(PACK):
                     for a in range(PASSES):
                         col = H * a + HALF * g + P * t
@@ -162,21 +171,23 @@ def tile_list_adna_damage_tempering_kernel(
                 )
             for part in parts:
                 nc.scalar.activation(part, part, ACT.Abs_reciprocal_sqrt, bias=1.0)
-            for part in parts:
-                nc.scalar.activation(part, part, ACT.Square)
             shrink[c, g] = parts
+
+        def square(c, g):
+            for part in shrink[c, g]:
+                nc.scalar.activation(part, part, ACT.Square)
 
         h_codes, h_sc = {}, {}
 
         def features(c, g):
-            if (c, g) == (CHUNKS - 1, 1):
-                hb = ring.tile([P, CHUNK * PACK], BF16, name="h_bf", tag="late_page", bufs=1, align_bytes=64)
+            if (c, g) == (1, 0):
+                hb = stage.tile([P, CHUNK * PACK], BF16, name="h_bf_held", align_bytes=64, offset=4 * SLOT)
             else:
                 hb = ring.tile([P, CHUNK * PACK], BF16, name="h_bf", tag="h_bf", bufs=2, align_bytes=64)
             for s in range(CHUNK // SUB):
-                bank = psum.tile([P, PACK * SUB], F32, name="a_bank", tag="a_bank%d%d" % (g, s))
+                bank = banks[2 * a_pair(c, g) + s]
                 for t in range(PACK):
-                    for a in range(PASSES):
+                    for a in reversed(range(PASSES)):
                         codes, plane = moving(a, CHUNK * c + SUB * s)
                         nc.tensor.matmul_mx(
                             out=bank[:, SUB * t : SUB * (t + 1)],
@@ -184,8 +195,8 @@ def tile_list_adna_damage_tempering_kernel(
                             lhsT_scale=w1_sc[g, a][:, P * t : P * (t + 1)],
                             rhs=codes,
                             rhs_scale=plane,
-                            start=(a == 0),
-                            stop=(a == PASSES - 1),
+                            start=(a == PASSES - 1),
+                            stop=(a == 0),
                         )
                 cols = slice(PACK * SUB * s, PACK * SUB * (s + 1))
                 nc.vector.tensor_tensor(
@@ -203,7 +214,10 @@ def tile_list_adna_damage_tempering_kernel(
 
         def weigh(c):
             share = gain[:, CHUNK * c : CHUNK * (c + 1)]
-            nc.scalar.activation(share, share, ACT.Square)
+            if c == 0:
+                nc.scalar.activation(share, share, ACT.Square)
+            else:
+                nc.gpsimd.tensor_tensor(share, share, share, MULT)
 
         def damage_values(b, chunks, weighed=True):
             width = CHUNK * len(chunks)
@@ -219,7 +233,10 @@ def tile_list_adna_damage_tempering_kernel(
                         start=(g == 0),
                         stop=(g == 1),
                     )
-            y2 = keep.tile([P, width], F32, name="y2_%d_%d" % (b, chunks[0]), align_bytes=64)
+            if (b, chunks) == (BLOCKS - 2, [CHUNKS - 1]):
+                y2 = stage.tile([P, width], F32, name="y2_late", align_bytes=64, offset=4 * SLOT)
+            else:
+                y2 = keep.tile([P, width], F32, name="y2_%d_%d" % (b, chunks[0]), align_bytes=64)
             nc.scalar.activation(y2[:], bank[:], ACT.Square)
             if weighed:
                 j0 = CHUNK * chunks[0]
@@ -233,7 +250,7 @@ def tile_list_adna_damage_tempering_kernel(
         def place(b, chunks, values, weighed=True):
             if b not in pages:
                 if b + 1 == BLOCKS:
-                    pages[b] = ring.tile([P, S], F32, name="page", tag="late_page", bufs=1, align_bytes=64)
+                    pages[b] = stage.tile([P, S], F32, name="page_late", align_bytes=64, offset=4 * SLOT)
                 else:
                     pages[b] = keep.tile([P, S], F32, name="page%d" % b)
             j0, width = CHUNK * chunks[0], CHUNK * len(chunks)
@@ -259,27 +276,30 @@ def tile_list_adna_damage_tempering_kernel(
                 held.append(x)
 
         def temper(b):
-            f = ring.tile([P, S], F32, name="factor", tag="factor", bufs=4)
             halves = [slice(m0, m0 + HALF) for m0 in range(0, S, HALF)]
-            placed = pages[b]
+            features_in = held[b // 2][:, b % 2, :]
             if b < EARLY_FACTOR:
+                f = ring.tile([P, S], F32, name="factor", tag="factor", bufs=3)
                 for cols in halves:
-                    nc.scalar.activation(f[:, cols], placed[:, cols], ACT.Abs_reciprocal_sqrt, bias=1.0)
+                    nc.scalar.activation(f[:, cols], pages[b][:, cols], ACT.Abs_reciprocal_sqrt, bias=1.0)
                 for cols in halves:
                     nc.scalar.activation(f[:, cols], f[:, cols], ACT.Square)
-                placed = f
-            for e, cols in enumerate(halves):
-                engine = nc.gpsimd if 2 * b + e < GPSIMD_HALVES else nc.vector
-                engine.tensor_tensor(f[:, cols], placed[:, cols], held[b // 2][:, b % 2, cols], MULT)
-                nc.sync.dma_start(out[P * b : P * (b + 1), cols], f[:, cols])
+                placed, result, engine = f[:], f[:], nc.gpsimd
+            else:
+                placed, result, engine = pages[b][:], held[b // 2][:, 0, :], nc.vector
+            for cols in halves:
+                engine.tensor_tensor(result[:, cols], placed[:, cols], features_in[:, cols], MULT)
+                nc.sync.dma_start(out[P * b : P * (b + 1), cols], result[:, cols])
 
-        background(0, 0)
-        background(0, 1)
+        for g in range(2):
+            background(0, g)
+            square(0, g)
         quantise_w1(0, 0)
         quantise_w1(0, 1)
         quantise_w1(1, 0)
         features(0, 0)
         background(1, 0)
+        square(1, 0)
         quantise_w1(1, 1)
         w8 = stage.tile([P, PASSES * N], I32, name="w8", align_bytes=64, offset=0)
         nc.sync.dma_start(
@@ -300,30 +320,37 @@ def tile_list_adna_damage_tempering_kernel(
         features(0, 1)
         features(1, 0)
 
-        def unit(c, g):
+        def unit(c, g, b=None, chunks=None):
             background(c, g)
+            if b is not None:
+                values = damage_values(b, chunks)
+            square(c, g)
+            if b is not None and b >= EARLY_FACTOR:
+                factor(values)
             features(c, g)
+            if b is not None:
+                place(b, chunks, values)
 
-        weigh(0)
+        for c in range(CHUNKS):
+            weigh(c)
         damage(0, [0], weighed=False)
-        damage(1, [0], weighed=False)
         unit(1, 1)
-        damage(2, [0])
-        weigh(1)
-        unit(2, 0)
-        damage(0, [1])
-        unit(2, 1)
-        damage(1, [1])
-        weigh(2)
-        unit(3, 0)
-        damage(2, [1])
-        weigh(3)
-        late = damage_values(3, [0, 1])
-        background(3, 1)
+        damage(1, [0], weighed=False)
+        damage(2, [0], weighed=False)
+        unit(2, 0, 0, [1])
+        unit(2, 1, 1, [1])
+        unit(3, 0, 2, [1])
+        early = damage_values(3, [0, 1])
+        unit(3, 1, 0, [2])
+        factor(early)
+        damage(1, [2])
+        damage(2, [2])
+        damage(0, [3])
+        late = damage_values(3, [2, 3])
         factor(late)
-        features(3, 1)
-        place(3, [0, 1], late)
-        for b in range(BLOCKS):
-            damage(b, [2, 3])
+        damage(1, [3])
+        damage(2, [3])
+        place(3, [0, 1], early)
+        place(3, [2, 3], late)
         for b in range(BLOCKS):
             temper(b)

@@ -43,8 +43,8 @@ def tile_list_adna_damage_tempering_kernel(
         places = keep.tile([P, S // 16], U16, name="places")
         nc.sync.dma_start(picks[:], offs)
 
-        tab_sc = stage.tile([P, T], U8, name="tab_sc", align_bytes=64, offset=SLOT - T // 2)
-        w4_sc_raw = keep.tile([P, PASSES * H], U8, name="w4_sc_raw", align_bytes=64)
+        tab_sc = keep.tile([P, T], U8, name="tab_sc", align_bytes=64)
+        w4_sc_raw = stage.tile([P, PASSES * H], U8, name="w4_sc_raw", align_bytes=64, offset=SLOT - H)
         v_sc = keep.tile([P, PASSES * S], U8, name="v_sc", align_bytes=64)
         for plane in (tab_sc, w4_sc_raw, v_sc):
             nc.vector.memset(plane[:].bitcast(I32), 0)
@@ -65,18 +65,18 @@ def tile_list_adna_damage_tempering_kernel(
             nc.sync.dma_start(words[:], tab_words[a].rearrange("p n i -> p (n i)").bitcast(I32))
             tab.append(words)
 
-        load_table(0)
         for q in range(4):
             nc.sync.dma_start(
                 w4_sc_raw[32 * q : 32 * q + 4, :].bitcast(I32).rearrange("r (a n) -> r a n", a=PASSES),
                 w4_scales[:, 4 * q : 4 * q + 4, :].bitcast(I32).rearrange("a r n -> r a n"),
             )
+        load_table(0)
         load_table(1)
 
         v_sc_spread = stage.tile([P, S], U8, name="v_sc_spread", align_bytes=64, offset=3 * SLOT - S // 2)
         nc.vector.tensor_copy(v_sc_spread[:], tab_sc[:].indirect(picks[:]))
         for q in range(4):
-            nc.sync.dma_start(
+            nc.scalar.dma_start(
                 v_sc[32 * q : 32 * q + 4, :].bitcast(I32).rearrange("r (a n) -> r a n", a=PASSES),
                 v_sc_spread[32 * q : 32 * q + 32 : 4, :].bitcast(I32),
             )
@@ -107,20 +107,19 @@ def tile_list_adna_damage_tempering_kernel(
             )
             v[a, half] = picked
 
-        gather_words(0, 0)
-        gather_words(0, 1)
         nc.vector.tensor_copy(
             w4_sc[:].rearrange("p (u t m) -> p u t m", t=PACK, m=P),
             w4_sc_raw[:].rearrange("p (u m t) -> p u t m", t=PACK, m=P),
         )
-        gather_words(1, 0)
-        gather_words(1, 1)
+        for a in range(PASSES):
+            for half in range(2):
+                gather_words(a, half)
 
         w1_codes, w1_sc = {}, {}
 
         def quantise_w1(g, a):
             if (g, a) == (1, 1):
-                grouped = stage.tile([P, PACK * HALF], BF16, name="w1_bf_last", align_bytes=64, offset=4 * SLOT)
+                grouped = stage.tile([P, PACK * HALF], BF16, name="w1_bf_last", align_bytes=64, offset=4 * SLOT + 4 * S)
             else:
                 grouped = ring.tile([P, PACK * HALF], BF16, name="w1_bf", tag="w1_bf", bufs=2, align_bytes=64)
             nc.vector.tensor_copy(
@@ -181,7 +180,7 @@ def tile_list_adna_damage_tempering_kernel(
 
         def features(c, g):
             if (c, g) == (1, 0):
-                hb = stage.tile([P, CHUNK * PACK], BF16, name="h_bf_held", align_bytes=64, offset=4 * SLOT)
+                hb = stage.tile([P, CHUNK * PACK], BF16, name="h_bf_held", align_bytes=64, offset=3 * SLOT + S)
             else:
                 hb = ring.tile([P, CHUNK * PACK], BF16, name="h_bf", tag="h_bf", bufs=2, align_bytes=64)
             for s in range(CHUNK // SUB):
@@ -213,11 +212,11 @@ def tile_list_adna_damage_tempering_kernel(
         pages = {}
 
         def weigh(c):
-            share = gain[:, CHUNK * c : CHUNK * (c + 1)]
+            cols = slice(CHUNK * c, CHUNK * (c + 1))
             if c == 0:
-                nc.scalar.activation(share, share, ACT.Square)
+                nc.scalar.activation(weight[:, cols], gain[:, cols], ACT.Square)
             else:
-                nc.gpsimd.tensor_tensor(share, share, share, MULT)
+                nc.gpsimd.tensor_tensor(weight[:, cols], gain[:, cols], gain[:, cols], MULT)
 
         def damage_values(b, chunks, weighed=True):
             width = CHUNK * len(chunks)
@@ -240,12 +239,15 @@ def tile_list_adna_damage_tempering_kernel(
             nc.scalar.activation(y2[:], bank[:], ACT.Square)
             if weighed:
                 j0 = CHUNK * chunks[0]
-                nc.gpsimd.tensor_tensor(y2[:], y2[:], gain[:, j0 : j0 + width], MULT)
+                nc.gpsimd.tensor_tensor(y2[:], y2[:], weight[:, j0 : j0 + width], MULT)
             return y2
 
-        def factor(values):
-            nc.scalar.activation(values[:], values[:], ACT.Abs_reciprocal_sqrt, bias=1.0)
-            nc.scalar.activation(values[:], values[:], ACT.Square)
+        def factor(values, last=False):
+            root = values
+            if last:
+                root = stage.tile([P, HALF], F32, name="last_root", align_bytes=64, offset=4 * SLOT + 10 * S)
+            nc.scalar.activation(root[:], values[:], ACT.Abs_reciprocal_sqrt, bias=1.0)
+            nc.scalar.activation(values[:], root[:], ACT.Square)
 
         def place(b, chunks, values, weighed=True):
             if b not in pages:
@@ -258,7 +260,7 @@ def tile_list_adna_damage_tempering_kernel(
             if weighed:
                 nc.vector.tensor_copy(window, values[:])
             else:
-                nc.vector.tensor_tensor(window, values[:], gain[:, j0 : j0 + width], MULT)
+                nc.vector.tensor_tensor(window, values[:], weight[:, j0 : j0 + width], MULT)
 
         def damage(b, chunks, weighed=True):
             values = damage_values(b, chunks, weighed)
@@ -268,28 +270,32 @@ def tile_list_adna_damage_tempering_kernel(
 
         held = []
 
-        def load_x0():
-            for pair in range(BLOCKS // 2):
-                x = stage.tile([P, 2, S], F32, name="x0_%d" % pair, align_bytes=64, offset=SLOT * (2 + pair))
-                rows = x0[2 * P * pair : 2 * P * (pair + 1), :]
-                nc.sync.dma_start(x[:], rows.rearrange("(e p) m -> p e m", p=P))
-                held.append(x)
+        def load_x0(pair):
+            x = stage.tile([P, 2, S], F32, name="x0_%d" % pair, align_bytes=64, offset=SLOT * (2 + pair))
+            rows = x0[2 * P * pair : 2 * P * (pair + 1), :]
+            nc.sync.dma_start(x[:], rows.rearrange("(e p) m -> p e m", p=P))
+            held.append(x)
 
         def temper(b):
             halves = [slice(m0, m0 + HALF) for m0 in range(0, S, HALF)]
             features_in = held[b // 2][:, b % 2, :]
+            rows = out[P * b : P * (b + 1), :]
             if b < EARLY_FACTOR:
-                f = ring.tile([P, S], F32, name="factor", tag="factor", bufs=3)
+                f = factors[:, S * b : S * (b + 1)]
                 for cols in halves:
                     nc.scalar.activation(f[:, cols], pages[b][:, cols], ACT.Abs_reciprocal_sqrt, bias=1.0)
                 for cols in halves:
                     nc.scalar.activation(f[:, cols], f[:, cols], ACT.Square)
-                placed, result, engine = f[:], f[:], nc.gpsimd
+                for cols in halves:
+                    last = b + 1 == EARLY_FACTOR and cols.stop == S
+                    result = factors[:, 0:HALF] if last else f[:, cols]
+                    nc.gpsimd.tensor_tensor(result, f[:, cols], features_in[:, cols], MULT)
+                    nc.sync.dma_start(rows[:, cols], result)
             else:
-                placed, result, engine = pages[b][:], held[b // 2][:, 0, :], nc.vector
-            for cols in halves:
-                engine.tensor_tensor(result[:, cols], placed[:, cols], features_in[:, cols], MULT)
-                nc.sync.dma_start(out[P * b : P * (b + 1), cols], result[:, cols])
+                freed = (held[b // 2][:, 0, HALF:S], factors[:, EARLY_FACTOR * S - HALF :])
+                for cols, result in zip(halves, freed):
+                    nc.vector.tensor_tensor(result, pages[b][:, cols], features_in[:, cols], MULT)
+                    nc.sync.dma_start(rows[:, cols], result)
 
         for g in range(2):
             background(0, g)
@@ -307,7 +313,7 @@ def tile_list_adna_damage_tempering_kernel(
             w8_words.rearrange("a p n i -> p a (n i)").bitcast(I32),
         )
         w8_sc = stage.tile([P, N], U8, name="w8_sc", align_bytes=64, offset=SLOT // 2)
-        nc.gpsimd.memset(w8_sc[:].bitcast(I32), 0)
+        nc.vector.memset(w8_sc[:].bitcast(I32), 0)
         for q in range(4):
             nc.sync.dma_start(
                 w8_sc[32 * q : 32 * q + 8, :].bitcast(I32),
@@ -316,9 +322,11 @@ def tile_list_adna_damage_tempering_kernel(
         nc.sync.dma_start(places[:], offs2)
         gain = stage.tile([P, S], F32, name="gain", align_bytes=64, offset=SLOT)
         nc.sync.dma_start(gain[:], wgo)
-        load_x0()
+        weight = stage.tile([P, S], F32, name="weight", align_bytes=64, offset=4 * SLOT + 6 * S)
+        load_x0(0)
         features(0, 1)
         features(1, 0)
+        load_x0(1)
 
         def unit(c, g, b=None, chunks=None):
             background(c, g)
@@ -347,10 +355,11 @@ def tile_list_adna_damage_tempering_kernel(
         damage(2, [2])
         damage(0, [3])
         late = damage_values(3, [2, 3])
-        factor(late)
+        factor(late, last=True)
         damage(1, [3])
         damage(2, [3])
         place(3, [0, 1], early)
         place(3, [2, 3], late)
+        factors = stage.tile([P, EARLY_FACTOR * S], F32, name="factors", align_bytes=64, offset=4 * SLOT + 10 * S)
         for b in range(BLOCKS):
             temper(b)

@@ -27,6 +27,7 @@ CHUNKS = S // CHUNK
 BLOCKS = N // P
 EARLY_FACTOR = 3
 SLOT = 4 * PACK * HALF
+TURN = 7 * SLOT
 
 
 def tile_list_adna_damage_tempering_kernel(
@@ -148,8 +149,12 @@ def tile_list_adna_damage_tempering_kernel(
             parts = []
             for s in range(CHUNK // SUB):
                 bank = banks[2 * b_pair(c, g) + s]
-                for t in range(PACK):
-                    for a in range(PASSES):
+                early = c == 0
+                steps = [(t, a) for t in range(PACK) for a in range(PASSES)]
+                if early:
+                    steps = [(t, a) for a in range(PASSES) for t in range(PACK)]
+                if True:
+                    for t, a in steps:
                         col = H * a + HALF * g + P * t
                         codes, plane = moving(a, CHUNK * c + SUB * s)
                         nc.tensor.matmul_mx(
@@ -158,8 +163,8 @@ def tile_list_adna_damage_tempering_kernel(
                             lhsT_scale=w4_sc[:, col : col + P],
                             rhs=codes,
                             rhs_scale=plane,
-                            start=(a == 0),
-                            stop=(a == PASSES - 1),
+                            start=((t, a) == steps[0] if early else a == 0),
+                            stop=((t, a) == steps[-1] if early else a == PASSES - 1),
                         )
                 r = ring.tile([P, SUB * PACK], F32, name="shrink", tag="shrink", bufs=10)
                 parts.append(r[:])
@@ -179,14 +184,21 @@ def tile_list_adna_damage_tempering_kernel(
         h_codes, h_sc = {}, {}
 
         def features(c, g):
-            if (c, g) == (1, 0):
+            if c >= 2 and g == 1:
+                offset = TURN + 4 * S * (c - 2)
+                hb = stage.tile([P, CHUNK * PACK], BF16, name="h_turn%d" % c, align_bytes=64, offset=offset)
+            elif (c, g) == (1, 0):
                 hb = stage.tile([P, CHUNK * PACK], BF16, name="h_bf_held", align_bytes=64, offset=3 * SLOT + S)
             else:
                 hb = ring.tile([P, CHUNK * PACK], BF16, name="h_bf", tag="h_bf", bufs=2, align_bytes=64)
             for s in range(CHUNK // SUB):
                 bank = banks[2 * a_pair(c, g) + s]
-                for t in range(PACK):
-                    for a in reversed(range(PASSES)):
+                early = False
+                steps = [(t, a) for t in range(PACK) for a in reversed(range(PASSES))]
+                if early:
+                    steps = [(t, a) for a in range(PASSES) for t in range(PACK)]
+                if True:
+                    for t, a in steps:
                         codes, plane = moving(a, CHUNK * c + SUB * s)
                         nc.tensor.matmul_mx(
                             out=bank[:, SUB * t : SUB * (t + 1)],
@@ -194,8 +206,8 @@ def tile_list_adna_damage_tempering_kernel(
                             lhsT_scale=w1_sc[g, a][:, P * t : P * (t + 1)],
                             rhs=codes,
                             rhs_scale=plane,
-                            start=(a == PASSES - 1),
-                            stop=(a == 0),
+                            start=((t, a) == steps[0] if early else a == PASSES - 1),
+                            stop=((t, a) == steps[-1] if early else a == 0),
                         )
                 cols = slice(PACK * SUB * s, PACK * SUB * (s + 1))
                 nc.vector.tensor_tensor(
@@ -206,7 +218,13 @@ def tile_list_adna_damage_tempering_kernel(
                 )
             codes = ring.tile([P, CHUNK], U32, name="h_codes", tag="h_codes", bufs=8, align_bytes=64)
             plane = ring.tile([P, CHUNK], U8, name="h_sc", tag="h_sc", bufs=8, align_bytes=64)
-            nc.vector.quantize_mx(out=codes[:].bitcast(FP8X4), scales=plane[:], in_=hb[:])
+            for s in range(CHUNK // SUB):
+                words = slice(SUB * s, SUB * (s + 1))
+                nc.vector.quantize_mx(
+                    out=codes[:, words].bitcast(FP8X4),
+                    scales=plane[:, words],
+                    in_=hb[:, PACK * SUB * s : PACK * SUB * (s + 1)],
+                )
             h_codes[c, g], h_sc[c, g] = codes, plane
 
         pages = {}
@@ -218,7 +236,7 @@ def tile_list_adna_damage_tempering_kernel(
             else:
                 nc.gpsimd.tensor_tensor(weight[:, cols], gain[:, cols], gain[:, cols], MULT)
 
-        def damage_values(b, chunks, weighed=True):
+        def damage_values(b, chunks, weighed=True, offset=None):
             width = CHUNK * len(chunks)
             bank = psum.tile([P, width], F32, name="y_bank", tag="y_bank", bufs=2)
             for e, c in enumerate(chunks):
@@ -239,7 +257,11 @@ def tile_list_adna_damage_tempering_kernel(
             nc.scalar.activation(y2[:], bank[:], ACT.Square)
             if weighed:
                 j0 = CHUNK * chunks[0]
-                nc.gpsimd.tensor_tensor(y2[:], y2[:], weight[:, j0 : j0 + width], MULT)
+                z = y2
+                if offset is not None:
+                    z = stage.tile([P, width], F32, name="z%d_%d" % (b, j0), align_bytes=64, offset=offset)
+                nc.gpsimd.tensor_tensor(z[:], y2[:], weight[:, j0 : j0 + width], MULT)
+                return z
             return y2
 
         def factor(values, last=False):
@@ -345,14 +367,18 @@ def tile_list_adna_damage_tempering_kernel(
         unit(1, 1)
         damage(1, [0], weighed=False)
         damage(2, [0], weighed=False)
-        unit(2, 0, 0, [1])
+        background(2, 0)
+        damage(0, [1], weighed=False)
+        square(2, 0)
+        features(2, 0)
         unit(2, 1, 1, [1])
         unit(3, 0, 2, [1])
-        early = damage_values(3, [0, 1])
-        unit(3, 1, 0, [2])
+        early = damage_values(3, [0, 1], offset=TURN)
+        damage(0, [2])
+        unit(3, 1)
         factor(early)
         damage(1, [2])
-        damage(2, [2])
+        place(2, [2], damage_values(2, [2], offset=TURN + 4 * S))
         damage(0, [3])
         late = damage_values(3, [2, 3])
         factor(late, last=True)

@@ -314,8 +314,16 @@ def tile_list_adna_damage_tempering_kernel(
                     nc.gpsimd.tensor_tensor(result, f[:, cols], features_in[:, cols], MULT)
                     nc.sync.dma_start(rows[:, cols], result)
             else:
-                freed = (held[b // 2][:, 0, HALF:S], factors[:, EARLY_FACTOR * S - HALF :])
-                for cols, result in zip(halves, freed):
+                end = EARLY_FACTOR * S
+                pieces = [slice(m0, m0 + CHUNK) for m0 in range(0, S, CHUNK)]
+                spare = held[b // 2][:, 0, :]
+                freed = (
+                    spare[:, HALF : HALF + CHUNK],
+                    spare[:, HALF + CHUNK : S],
+                    factors[:, end - HALF : end - CHUNK],
+                    factors[:, end - CHUNK : end],
+                )
+                for cols, result in zip(pieces, freed):
                     nc.vector.tensor_tensor(result, pages[b][:, cols], features_in[:, cols], MULT)
                     nc.sync.dma_start(rows[:, cols], result)
 

@@ -169,8 +169,8 @@ def tile_list_adna_damage_tempering_kernel(
                 r = ring.tile([P, SUB * PACK], F32, name="shrink", tag="shrink", bufs=10)
                 parts.append(r[:])
                 nc.scalar.activation(
-                    r[:].rearrange("p (j t) -> p j t", t=PACK),
-                    bank[:].rearrange("p (t j) -> p j t", t=PACK),
+                    r[:].rearrange("p (j t e) -> p j t e", t=PACK, e=2),
+                    bank[:].rearrange("p (t j e) -> p j t e", t=PACK, e=2),
                     ACT.Abs,
                 )
             for part in parts:
@@ -211,9 +211,9 @@ def tile_list_adna_damage_tempering_kernel(
                         )
                 cols = slice(PACK * SUB * s, PACK * SUB * (s + 1))
                 nc.vector.tensor_tensor(
-                    hb[:, cols].rearrange("p (j t) -> p j t", t=PACK),
-                    bank[:].rearrange("p (t j) -> p j t", t=PACK),
-                    shrink[c, g][s].rearrange("p (j t) -> p j t", t=PACK),
+                    hb[:, cols].rearrange("p (j e t) -> p j t e", t=PACK, e=2),
+                    bank[:].rearrange("p (t j e) -> p j t e", t=PACK, e=2),
+                    shrink[c, g][s].rearrange("p (j t e) -> p j t e", t=PACK, e=2),
                     MULT,
                 )
             codes = ring.tile([P, CHUNK], U32, name="h_codes", tag="h_codes", bufs=8, align_bytes=64)

@@ -24,10 +24,16 @@ HALF = 512
 CHUNK = 256
 SUB = 128
 CHUNKS = S // CHUNK
-BLOCKS = N // P
-EARLY_FACTOR = 3
-SLOT = 4 * PACK * HALF
-TURN = 7 * SLOT
+PAGES = N // P
+KB = 1024
+RAW = {(1, 0): 0, (1, 1): 8 * KB, (0, 0): 16 * KB, (0, 1): 24 * KB}
+X0_AT = (28 * KB, 2 * KB)
+H_AT = 36 * KB
+LAST_CODES_AT = 52 * KB
+TAB_AT = 56 * KB
+LATE_AT = 88 * KB
+Y2_AT = 92 * KB
+TAIL_AT = 98 * KB
 
 
 def tile_list_adna_damage_tempering_kernel(
@@ -40,12 +46,15 @@ def tile_list_adna_damage_tempering_kernel(
         stage = ctx.enter_context(tc.tile_pool(name="stage", bufs=1))
         psum = ctx.enter_context(tc.psum_pool(name="psum", bufs=1))
 
+        def staged(shape, dtype, name, offset):
+            return stage.tile(shape, dtype, name=name, align_bytes=64, offset=offset)
+
         picks = keep.tile([P, S // 16], U16, name="picks")
         places = keep.tile([P, S // 16], U16, name="places")
         nc.sync.dma_start(picks[:], offs)
 
         tab_sc = keep.tile([P, T], U8, name="tab_sc", align_bytes=64)
-        w4_sc_raw = stage.tile([P, PASSES * H], U8, name="w4_sc_raw", align_bytes=64, offset=SLOT - H)
+        w4_sc_raw = staged([P, PASSES * H], U8, "w4_sc_raw", RAW[0, 1] - H)
         v_sc = keep.tile([P, PASSES * S], U8, name="v_sc", align_bytes=64)
         for plane in (tab_sc, w4_sc_raw, v_sc):
             nc.vector.memset(plane[:].bitcast(I32), 0)
@@ -59,22 +68,18 @@ def tile_list_adna_damage_tempering_kernel(
         for a in range(PASSES):
             nc.sync.dma_start(w4_raw[:, 2 * H * a : 2 * H * (a + 1)].bitcast(I32), w4_words[a].bitcast(I32))
         nc.sync.dma_start(tab_sc[0:P:4, :].bitcast(I32), tab_scales.bitcast(I32).rearrange("a q n -> q a n"))
-        tab = []
-
-        def load_table(a):
-            words = keep.tile([P, T], I32, name="tab%d" % a, align_bytes=64)
-            nc.sync.dma_start(words[:], tab_words[a].rearrange("p n i -> p (n i)").bitcast(I32))
-            tab.append(words)
-
         for q in range(4):
             nc.sync.dma_start(
                 w4_sc_raw[32 * q : 32 * q + 4, :].bitcast(I32).rearrange("r (a n) -> r a n", a=PASSES),
                 w4_scales[:, 4 * q : 4 * q + 4, :].bitcast(I32).rearrange("a r n -> r a n"),
             )
-        load_table(0)
-        load_table(1)
+        tab = []
+        for a in range(PASSES):
+            words = staged([P, T], I32, "tab%d" % a, TAB_AT + 16 * KB * a)
+            nc.sync.dma_start(words[:], tab_words[a].rearrange("p n i -> p (n i)").bitcast(I32))
+            tab.append(words)
 
-        v_sc_spread = stage.tile([P, S], U8, name="v_sc_spread", align_bytes=64, offset=3 * SLOT - S // 2)
+        v_sc_spread = staged([P, S], U8, "v_sc_spread", RAW[1, 1] - S // 2)
         nc.vector.tensor_copy(v_sc_spread[:], tab_sc[:].indirect(picks[:]))
         for q in range(4):
             nc.scalar.dma_start(
@@ -82,167 +87,167 @@ def tile_list_adna_damage_tempering_kernel(
                 v_sc_spread[32 * q : 32 * q + 32 : 4, :].bitcast(I32),
             )
 
-        w1_raw = {}
-        for g in range(2):
-            for a in range(PASSES):
-                raw = stage.tile(
-                    [P, PACK, HALF], F32, name="w1_raw%d_%d" % (g, a), align_bytes=64, offset=SLOT * (2 * g + a)
-                )
-                rows = w1[KP * a : KP * (a + 1), HALF * g : HALF * (g + 1)]
-                nc.sync.dma_start(raw[:], rows.rearrange("(p j) c -> p j c", j=PACK))
-                w1_raw[g, a] = raw
-
         w4 = keep.tile([P, PASSES * 2 * H], U8, name="w4", align_bytes=64)
         w4_sc = keep.tile([P, PASSES * H], U8, name="w4_sc", align_bytes=64)
-        nc.vector.tensor_copy(
-            w4[:].bitcast(U16).rearrange("p (u t m) -> p u t m", t=PACK, m=P),
-            w4_raw[:].bitcast(U16).rearrange("p (u m t) -> p u t m", t=PACK, m=P),
-        )
-        v = {}
-
-        def gather_words(a, half):
-            picked = keep.tile([P, HALF], U32, name="v%d_%d" % (a, half), align_bytes=64)
-            cols = HALF // 16
-            nc.vector.tensor_copy(
-                picked[:], tab[a][:].bitcast(U32).indirect(picks[:, cols * half : cols * (half + 1)])
-            )
-            v[a, half] = picked
-
         nc.vector.tensor_copy(
             w4_sc[:].rearrange("p (u t m) -> p u t m", t=PACK, m=P),
             w4_sc_raw[:].rearrange("p (u m t) -> p u t m", t=PACK, m=P),
         )
+        nc.vector.tensor_copy(
+            w4[:].bitcast(U16).rearrange("p (u t m) -> p u t m", t=PACK, m=P),
+            w4_raw[:].bitcast(U16).rearrange("p (u m t) -> p u t m", t=PACK, m=P),
+        )
+
+        w1_raw = {}
+        for g in range(2):
+            for a in range(PASSES):
+                raw = staged([P, PACK, HALF], F32, "w1_raw%d_%d" % (g, a), RAW[g, a])
+                rows = w1[KP * a : KP * (a + 1), HALF * g : HALF * (g + 1)]
+                nc.sync.dma_start(raw[:], rows.rearrange("(p j) c -> p j c", j=PACK))
+                w1_raw[g, a] = raw
+
+        v = {}
         for a in range(PASSES):
             for half in range(2):
-                gather_words(a, half)
+                picked = keep.tile([P, HALF], U32, name="v%d_%d" % (a, half), align_bytes=64)
+                cols = HALF // 16
+                nc.vector.tensor_copy(
+                    picked[:], tab[a][:].bitcast(U32).indirect(picks[:, cols * half : cols * (half + 1)])
+                )
+                v[a, half] = picked
 
-        w1_codes, w1_sc = {}, {}
+        w1_bf, w1_codes, w1_sc = {}, {}, {}
 
-        def quantise_w1(g, a):
-            if (g, a) == (1, 1):
-                grouped = stage.tile([P, PACK * HALF], BF16, name="w1_bf_last", align_bytes=64, offset=4 * SLOT + 4 * S)
-            else:
-                grouped = ring.tile([P, PACK * HALF], BF16, name="w1_bf", tag="w1_bf", bufs=2, align_bytes=64)
+        def round_w1(g, a):
+            grouped = ring.tile([P, PACK * HALF], BF16, name="w1_bf", tag="w1_bf", bufs=1, align_bytes=64)
             nc.vector.tensor_copy(
                 grouped[:].rearrange("p (t m j) -> p m t j", t=PACK, j=PACK),
                 w1_raw[g, a][:].rearrange("p j (m t) -> p m t j", t=PACK),
             )
+            w1_bf[g, a] = grouped
+
+        def quantise_w1(g, a):
             codes = keep.tile([P, HALF], U32, name="w1c%d_%d" % (g, a), align_bytes=64)
             plane = keep.tile([P, HALF], U8, name="w1s%d_%d" % (g, a), align_bytes=64)
-            nc.vector.quantize_mx(out=codes[:].bitcast(FP8X4), scales=plane[:], in_=grouped[:])
+            nc.vector.quantize_mx(out=codes[:].bitcast(FP8X4), scales=plane[:], in_=w1_bf[g, a][:])
             w1_codes[g, a], w1_sc[g, a] = codes, plane
 
-        def moving(a, j0):
-            half, c0 = divmod(j0, HALF)
-            return v[a, half][:, c0 : c0 + SUB].bitcast(FP8X4), v_sc[:, S * a + j0 : S * a + j0 + SUB]
-
-        shrink = {}
+        y_banks = [psum.tile([P, 2 * CHUNK], F32, name="y_bank%d" % e) for e in range(2)]
         banks = [psum.tile([P, PACK * SUB], F32, name="bank%d" % e) for e in range(6)]
 
-        def b_pair(c, g):
-            return [0, 1, 0, 2, 0, 1, 2, 0][2 * c + g]
+        def bank_of(k, s):
+            return banks[2 * (k % 3) + s]
 
-        def a_pair(c, g):
-            return [2, 0, 1, 2, 0, 1, 2, 0][2 * c + g]
-
-        def background(c, g):
-            parts = []
-            for s in range(CHUNK // SUB):
-                bank = banks[2 * b_pair(c, g) + s]
-                early = c == 0
-                steps = [(t, a) for t in range(PACK) for a in range(PASSES)]
-                if early:
-                    steps = [(t, a) for a in range(PASSES) for t in range(PACK)]
-                if True:
-                    for t, a in steps:
-                        col = H * a + HALF * g + P * t
-                        codes, plane = moving(a, CHUNK * c + SUB * s)
-                        nc.tensor.matmul_mx(
-                            out=bank[:, SUB * t : SUB * (t + 1)],
-                            lhsT=w4[:, 2 * col : 2 * (col + P)].bitcast(FP4X4),
-                            lhsT_scale=w4_sc[:, col : col + P],
-                            rhs=codes,
-                            rhs_scale=plane,
-                            start=((t, a) == steps[0] if early else a == 0),
-                            stop=((t, a) == steps[-1] if early else a == PASSES - 1),
-                        )
-                r = ring.tile([P, SUB * PACK], F32, name="shrink", tag="shrink", bufs=10)
-                parts.append(r[:])
-                nc.scalar.activation(
-                    r[:].rearrange("p (j t e) -> p j t e", t=PACK, e=2),
-                    bank[:].rearrange("p (t j e) -> p j t e", t=PACK, e=2),
-                    ACT.Abs,
+        def first_stage(bank, j0, stationary, one_group):
+            half, c0 = divmod(j0, HALF)
+            steps = [(t, a) for t in range(PACK) for a in range(PASSES)]
+            if one_group:
+                steps = [(t, a) for a in range(PASSES) for t in range(PACK)]
+            for t, a in steps:
+                codes, plane = stationary(t, a)
+                nc.tensor.matmul_mx(
+                    out=bank[:, SUB * t : SUB * (t + 1)],
+                    lhsT=codes,
+                    lhsT_scale=plane,
+                    rhs=v[a, half][:, c0 : c0 + SUB].bitcast(FP8X4),
+                    rhs_scale=v_sc[:, S * a + j0 : S * a + j0 + SUB],
+                    start=((t, a) == steps[0] if one_group else a == 0),
+                    stop=((t, a) == steps[-1] if one_group else a == PASSES - 1),
                 )
-            for part in parts:
-                nc.scalar.activation(part, part, ACT.Abs_reciprocal_sqrt, bias=1.0)
-            shrink[c, g] = parts
 
-        def square(c, g):
-            for part in shrink[c, g]:
-                nc.scalar.activation(part, part, ACT.Square)
+        pairs = [(0, 0), (1, 0), (0, 1), (1, 1), (2, 0), (2, 1), (3, 0), (3, 1)]
+        shrink = {}
 
-        h_codes, h_sc = {}, {}
+        def size_of_b(k, s):
+            c, g = pairs[k]
+            bank = y_banks[s] if k == 3 else bank_of(k, s)
 
-        def features(c, g):
-            if c >= 2 and g == 1:
-                offset = TURN + 4 * S * (c - 2)
-                hb = stage.tile([P, CHUNK * PACK], BF16, name="h_turn%d" % c, align_bytes=64, offset=offset)
-            elif (c, g) == (1, 0):
-                hb = stage.tile([P, CHUNK * PACK], BF16, name="h_bf_held", align_bytes=64, offset=3 * SLOT + S)
+            def columns(t, a):
+                col = H * a + HALF * g + P * t
+                return w4[:, 2 * col : 2 * (col + P)].bitcast(FP4X4), w4_sc[:, col : col + P]
+
+            first_stage(bank, CHUNK * c + SUB * s, columns, k < 3)
+            if (k, s) == (3, 0):
+                shrink[k] = staged([P, CHUNK * PACK], F32, "shrink3", root_at(4))
+            elif s == 0:
+                shrink[k] = ring.tile([P, CHUNK * PACK], F32, name="shrink", tag="shrink", bufs=3)
+            part = shrink[k][:, PACK * SUB * s : PACK * SUB * (s + 1)]
+            nc.scalar.activation(
+                part.rearrange("p (j t e) -> p j t e", t=PACK, e=2),
+                bank[:].rearrange("p (t j e) -> p j t e", t=PACK, e=2),
+                ACT.Abs,
+            )
+
+        def root(result, values):
+            nc.scalar.activation(result, values, ACT.Abs_reciprocal_sqrt, bias=1.0)
+
+        def square(result, values):
+            nc.scalar.activation(result, values, ACT.Square)
+
+        def root_at(k):
+            return TAB_AT + 4 * KB * k
+
+        def factor(k, first, second):
+            r = staged([P, CHUNK * PACK], F32, "root%d" % k, root_at(k))
+            for step in first:
+                step()
+            root(r[:], shrink[k][:])
+            for step in second:
+                step()
+            square(shrink[k][:], r[:])
+
+        def b_step(k, s):
+            return lambda: size_of_b(k, s)
+
+        h_bf, h_codes, h_sc = {}, {}, {}
+
+        def signal(k):
+            c, g = pairs[k]
+
+            def columns(t, a):
+                return (
+                    w1_codes[g, a][:, P * t : P * (t + 1)].bitcast(FP8X4),
+                    w1_sc[g, a][:, P * t : P * (t + 1)],
+                )
+
+            for s in range(2):
+                first_stage(bank_of(k, s), CHUNK * c + SUB * s, columns, k in (2, 3))
+
+        def feature(k, s):
+            if s == 0:
+                if k < 2:
+                    h_bf[k] = staged([P, CHUNK * PACK], BF16, "h_first%d" % k, RAW[1, k] + 6 * KB * k)
+                else:
+                    h_bf[k] = staged([P, CHUNK * PACK], BF16, "h_bf%d" % k, H_AT + 2 * KB * k)
+            cols = slice(PACK * SUB * s, PACK * SUB * (s + 1))
+            nc.vector.tensor_tensor(
+                h_bf[k][:, cols].rearrange("p (j e t) -> p j t e", t=PACK, e=2),
+                bank_of(k, s)[:].rearrange("p (t j e) -> p j t e", t=PACK, e=2),
+                shrink[k][:, cols].rearrange("p (j t e) -> p j t e", t=PACK, e=2),
+                MULT,
+            )
+
+        def features(k):
+            signal(k)
+            feature(k, 0)
+            feature(k, 1)
+
+        def quantise_h(k):
+            if k + 1 == len(pairs):
+                codes = staged([P, CHUNK], U32, "h_codes_last", LAST_CODES_AT)
             else:
-                hb = ring.tile([P, CHUNK * PACK], BF16, name="h_bf", tag="h_bf", bufs=2, align_bytes=64)
-            for s in range(CHUNK // SUB):
-                bank = banks[2 * a_pair(c, g) + s]
-                early = False
-                steps = [(t, a) for t in range(PACK) for a in reversed(range(PASSES))]
-                if early:
-                    steps = [(t, a) for a in range(PASSES) for t in range(PACK)]
-                if True:
-                    for t, a in steps:
-                        codes, plane = moving(a, CHUNK * c + SUB * s)
-                        nc.tensor.matmul_mx(
-                            out=bank[:, SUB * t : SUB * (t + 1)],
-                            lhsT=w1_codes[g, a][:, P * t : P * (t + 1)].bitcast(FP8X4),
-                            lhsT_scale=w1_sc[g, a][:, P * t : P * (t + 1)],
-                            rhs=codes,
-                            rhs_scale=plane,
-                            start=((t, a) == steps[0] if early else a == PASSES - 1),
-                            stop=((t, a) == steps[-1] if early else a == 0),
-                        )
-                cols = slice(PACK * SUB * s, PACK * SUB * (s + 1))
-                nc.vector.tensor_tensor(
-                    hb[:, cols].rearrange("p (j e t) -> p j t e", t=PACK, e=2),
-                    bank[:].rearrange("p (t j e) -> p j t e", t=PACK, e=2),
-                    shrink[c, g][s].rearrange("p (j t e) -> p j t e", t=PACK, e=2),
-                    MULT,
-                )
-            codes = ring.tile([P, CHUNK], U32, name="h_codes", tag="h_codes", bufs=8, align_bytes=64)
-            plane = ring.tile([P, CHUNK], U8, name="h_sc", tag="h_sc", bufs=8, align_bytes=64)
-            for s in range(CHUNK // SUB):
-                words = slice(SUB * s, SUB * (s + 1))
-                nc.vector.quantize_mx(
-                    out=codes[:, words].bitcast(FP8X4),
-                    scales=plane[:, words],
-                    in_=hb[:, PACK * SUB * s : PACK * SUB * (s + 1)],
-                )
-            h_codes[c, g], h_sc[c, g] = codes, plane
+                codes = keep.tile([P, CHUNK], U32, name="h_codes%d" % k, align_bytes=64)
+            plane = keep.tile([P, CHUNK], U8, name="h_sc%d" % k, align_bytes=64)
+            nc.vector.quantize_mx(out=codes[:].bitcast(FP8X4), scales=plane[:], in_=h_bf[k][:])
+            h_codes[pairs[k]], h_sc[pairs[k]] = codes, plane
 
-        pages = {}
+        y2 = {}
 
-        def weigh(c):
-            cols = slice(CHUNK * c, CHUNK * (c + 1))
-            if c == 0:
-                nc.scalar.activation(weight[:, cols], gain[:, cols], ACT.Square)
-            else:
-                nc.gpsimd.tensor_tensor(weight[:, cols], gain[:, cols], gain[:, cols], MULT)
-
-        def damage_values(b, chunks, weighed=True, offset=None):
-            width = CHUNK * len(chunks)
-            bank = psum.tile([P, width], F32, name="y_bank", tag="y_bank", bufs=2)
-            for e, c in enumerate(chunks):
+        def damage(c, e, blocks):
+            for i, b in enumerate(blocks):
                 for g in range(2):
                     nc.tensor.matmul_mx(
-                        out=bank[:, CHUNK * e : CHUNK * (e + 1)],
+                        out=y_banks[e][:, chunk(i)],
                         lhsT=w8[:, N * g + P * b : N * g + P * (b + 1)].bitcast(FP8X4),
                         lhsT_scale=w8_sc[4 * g : P, P * b : P * (b + 1)],
                         rhs=h_codes[c, g][:].bitcast(FP8X4),
@@ -250,99 +255,65 @@ def tile_list_adna_damage_tempering_kernel(
                         start=(g == 0),
                         stop=(g == 1),
                     )
-            if (b, chunks) == (BLOCKS - 2, [CHUNKS - 1]):
-                y2 = stage.tile([P, width], F32, name="y2_late", align_bytes=64, offset=4 * SLOT)
-            else:
-                y2 = keep.tile([P, width], F32, name="y2_%d_%d" % (b, chunks[0]), align_bytes=64)
-            nc.scalar.activation(y2[:], bank[:], ACT.Square)
-            if weighed:
-                j0 = CHUNK * chunks[0]
-                z = y2
-                if offset is not None:
-                    z = stage.tile([P, width], F32, name="z%d_%d" % (b, j0), align_bytes=64, offset=offset)
-                nc.gpsimd.tensor_tensor(z[:], y2[:], weight[:, j0 : j0 + width], MULT)
-                return z
-            return y2
 
-        def factor(values, last=False):
-            root = values
-            if last:
-                root = stage.tile([P, HALF], F32, name="last_root", align_bytes=64, offset=4 * SLOT + 10 * S)
-            nc.scalar.activation(root[:], values[:], ACT.Abs_reciprocal_sqrt, bias=1.0)
-            nc.scalar.activation(values[:], root[:], ACT.Square)
+        def read_y(c, e, blocks, first=0, at=None):
+            shape, name = [P, CHUNK * len(blocks)], "y2_%d_%d" % (blocks[0], c)
+            values = keep.tile(shape, F32, name=name) if at is None else staged(shape, F32, name, at)
+            square(values[:], y_banks[e][:, CHUNK * first : CHUNK * (first + len(blocks))])
+            for i, b in enumerate(blocks):
+                y2[b, c] = values[:, chunk(i)]
 
-        def place(b, chunks, values, weighed=True):
-            if b not in pages:
-                if b + 1 == BLOCKS:
-                    pages[b] = stage.tile([P, S], F32, name="page_late", align_bytes=64, offset=4 * SLOT)
-                else:
-                    pages[b] = keep.tile([P, S], F32, name="page%d" % b)
-            j0, width = CHUNK * chunks[0], CHUNK * len(chunks)
-            window = pages[b][:].indirect(places[:, j0 // 16 : (j0 + width) // 16])
-            if weighed:
-                nc.vector.tensor_copy(window, values[:])
-            else:
-                nc.vector.tensor_tensor(window, values[:], weight[:, j0 : j0 + width], MULT)
+        def chunk(c):
+            return slice(CHUNK * c, CHUNK * (c + 1))
 
-        def damage(b, chunks, weighed=True):
-            values = damage_values(b, chunks, weighed)
-            if b >= EARLY_FACTOR:
-                factor(values)
-            place(b, chunks, values, weighed)
+        pages = [keep.tile([P, S], F32, name="page%d" % b) for b in range(PAGES - 1)]
+        pages.append(staged([P, S], F32, "page_last", LAST_CODES_AT))
+
+        def window(b, j0, width):
+            return pages[b][:].indirect(places[:, j0 // 16 : (j0 + width) // 16])
+
+        def place_weighed(b, c):
+            nc.vector.tensor_tensor(window(b, CHUNK * c, CHUNK), y2[b, c], weight[c], MULT)
+
+        def place(b, j0, values, width):
+            nc.vector.tensor_copy(window(b, j0, width), values)
 
         held = []
 
         def load_x0(pair):
-            x = stage.tile([P, 2, S], F32, name="x0_%d" % pair, align_bytes=64, offset=SLOT * (2 + pair))
+            x = staged([P, 2, S], F32, "x0_%d" % pair, X0_AT[pair])
             rows = x0[2 * P * pair : 2 * P * (pair + 1), :]
             nc.sync.dma_start(x[:], rows.rearrange("(e p) m -> p e m", p=P))
             held.append(x)
 
-        def temper(b):
-            halves = [slice(m0, m0 + HALF) for m0 in range(0, S, HALF)]
-            features_in = held[b // 2][:, b % 2, :]
-            rows = out[P * b : P * (b + 1), :]
-            if b < EARLY_FACTOR:
-                f = factors[:, S * b : S * (b + 1)]
-                for cols in halves:
-                    nc.scalar.activation(f[:, cols], pages[b][:, cols], ACT.Abs_reciprocal_sqrt, bias=1.0)
-                for cols in halves:
-                    nc.scalar.activation(f[:, cols], f[:, cols], ACT.Square)
-                for cols in halves:
-                    last = b + 1 == EARLY_FACTOR and cols.stop == S
-                    result = factors[:, 0:HALF] if last else f[:, cols]
-                    nc.gpsimd.tensor_tensor(result, f[:, cols], features_in[:, cols], MULT)
-                    nc.sync.dma_start(rows[:, cols], result)
-            else:
-                end = EARLY_FACTOR * S
-                pieces = [slice(m0, m0 + CHUNK) for m0 in range(0, S, CHUNK)]
-                spare = held[b // 2][:, 0, :]
-                freed = (
-                    spare[:, HALF : HALF + CHUNK],
-                    spare[:, HALF + CHUNK : S],
-                    factors[:, end - HALF : end - CHUNK],
-                    factors[:, end - CHUNK : end],
-                )
-                for cols, result in zip(pieces, freed):
-                    nc.vector.tensor_tensor(result, pages[b][:, cols], features_in[:, cols], MULT)
-                    nc.sync.dma_start(rows[:, cols], result)
+        halves = [slice(m0, m0 + HALF) for m0 in range(0, S, HALF)]
 
-        for g in range(2):
-            background(0, g)
-            square(0, g)
-        quantise_w1(0, 0)
-        quantise_w1(0, 1)
-        quantise_w1(1, 0)
-        features(0, 0)
-        background(1, 0)
-        square(1, 0)
-        quantise_w1(1, 1)
-        w8 = stage.tile([P, PASSES * N], I32, name="w8", align_bytes=64, offset=0)
+        factors = [keep.tile([P, S], F32, name="factor%d" % b) for b in range(PAGES - 1)]
+
+        def page_root(b, cols):
+            root(factors[b][:, cols], pages[b][:, cols])
+
+        def page_square(b, cols):
+            square(factors[b][:, cols], factors[b][:, cols])
+
+        def temper(b, cols, values=None):
+            f = factors[b][:, cols]
+            nc.gpsimd.tensor_tensor(f, f if values is None else values, held[b // 2][:, b % 2, cols], MULT)
+            nc.sync.dma_start(out[P * b : P * (b + 1), cols], f)
+
+        size_of_b(0, 0)
+        size_of_b(0, 1)
+        for k in range(3):
+            factor(k, [b_step(k + 1, 0)], [b_step(k + 1, 1)])
+        for a in range(PASSES):
+            round_w1(0, a)
+            quantise_w1(0, a)
+        w8 = staged([P, PASSES * N], I32, "w8", RAW[0, 0])
         nc.sync.dma_start(
             w8[:].rearrange("p (a n) -> p a n", a=PASSES),
             w8_words.rearrange("a p n i -> p a (n i)").bitcast(I32),
         )
-        w8_sc = stage.tile([P, N], U8, name="w8_sc", align_bytes=64, offset=SLOT // 2)
+        w8_sc = staged([P, N], U8, "w8_sc", RAW[0, 0] + 4 * KB)
         nc.vector.memset(w8_sc[:].bitcast(I32), 0)
         for q in range(4):
             nc.sync.dma_start(
@@ -350,50 +321,130 @@ def tile_list_adna_damage_tempering_kernel(
                 w8_scales[:, 4 * q : 4 * q + 4, :].bitcast(I32),
             )
         nc.sync.dma_start(places[:], offs2)
-        gain = stage.tile([P, S], F32, name="gain", align_bytes=64, offset=SLOT)
+        gain = staged([P, S], F32, "gain", RAW[0, 1])
         nc.sync.dma_start(gain[:], wgo)
-        weight = stage.tile([P, S], F32, name="weight", align_bytes=64, offset=4 * SLOT + 6 * S)
         load_x0(0)
-        features(0, 1)
-        features(1, 0)
+
+        round_w1(1, 0)
+        signal(0)
+        feature(0, 0)
+        quantise_w1(1, 0)
+        feature(0, 1)
+        round_w1(1, 1)
+        quantise_h(0)
+        quantise_w1(1, 1)
+        features(1)
+        features(2)
+        quantise_h(1)
+        quantise_h(2)
         load_x0(1)
 
-        def unit(c, g, b=None, chunks=None):
-            background(c, g)
-            if b is not None:
-                values = damage_values(b, chunks)
-            square(c, g)
-            if b is not None and b >= EARLY_FACTOR:
-                factor(values)
-            features(c, g)
-            if b is not None:
-                place(b, chunks, values)
+        weight = {}
 
-        for c in range(CHUNKS):
-            weigh(c)
-        damage(0, [0], weighed=False)
-        unit(1, 1)
-        damage(1, [0], weighed=False)
-        damage(2, [0], weighed=False)
-        background(2, 0)
-        damage(0, [1], weighed=False)
-        square(2, 0)
-        features(2, 0)
-        unit(2, 1, 1, [1])
-        unit(3, 0, 2, [1])
-        early = damage_values(3, [0, 1], offset=TURN)
-        damage(0, [2])
-        unit(3, 1)
-        factor(early)
-        damage(1, [2])
-        place(2, [2], damage_values(2, [2], offset=TURN + 4 * S))
-        damage(0, [3])
-        late = damage_values(3, [2, 3])
-        factor(late, last=True)
-        damage(1, [3])
-        damage(2, [3])
-        place(3, [0, 1], early)
-        place(3, [2, 3], late)
-        factors = stage.tile([P, EARLY_FACTOR * S], F32, name="factors", align_bytes=64, offset=4 * SLOT + 10 * S)
-        for b in range(BLOCKS):
-            temper(b)
+        def weigh(c):
+            weight[c] = keep.tile([P, CHUNK], F32, name="weight%d" % c)[:]
+            square(weight[c], gain[:, chunk(c)])
+
+        def weigh_beside(c, at):
+            weight[c] = staged([P, CHUNK], F32, "weight%d" % c, at)[:]
+            nc.gpsimd.tensor_tensor(weight[c], gain[:, chunk(c)], gain[:, chunk(c)], MULT)
+
+
+        def weighed_early(c, over):
+            z = staged([P, CHUNK], F32, "z3_%d" % c, over)
+            nc.gpsimd.tensor_tensor(z[:], y2[3, c], weight[c], MULT)
+            return z
+
+        def h_at(k):
+            return H_AT + 2 * KB * k
+
+        def y2_at(c):
+            return Y2_AT + 2 * KB * c
+
+        early = {}
+        factor(3, [], [lambda: weigh(0)])
+        size_of_b(4, 0)
+        size_of_b(4, 1)
+        damage(0, 0, (0, 3))
+        damage(0, 1, (1, 2))
+        read_y(0, 0, (0, 3))
+        read_y(0, 1, (1, 2), at=y2_at(0))
+        features(3)
+        place_weighed(0, 0)
+        quantise_h(3)
+        place_weighed(1, 0)
+        place_weighed(2, 0)
+        early[0] = weighed_early(0, y2_at(0))
+        weigh(1)
+        factor(4, [], [b_step(5, 0), b_step(5, 1)])
+        for c in (1, 2):
+            k = 2 * c + 2
+            damage(c, 0, (0, 3))
+            read_y(c, 0, (0, 3))
+            features(k)
+            place_weighed(0, c)
+            quantise_h(k)
+            damage(c, 1, (1, 2))
+            if c == 1:
+                weigh_beside(2, h_at(k))
+                factor(k + 1, [], [b_step(k + 2, 0), b_step(k + 2, 1)])
+                read_y(c, 1, (1,))
+            else:
+                early[c] = weighed_early(c, h_at(k))
+                factor(k + 1, [], [lambda: weigh(3), lambda: root(early[0][:], early[0][:])])
+                read_y(c, 1, (1,), at=root_at(k + 1))
+            features(k + 1)
+            place_weighed(1, c)
+            quantise_h(k + 1)
+            if c == 1:
+                factor(k + 2, [], [lambda: read_y(1, 1, (2,), 1, y2_at(1)), b_step(k + 3, 0), b_step(k + 3, 1)])
+                place_weighed(2, c)
+                early[c] = weighed_early(c, y2_at(c))
+        first = keep.tile([P, CHUNK], F32, name="first")
+        rest = keep.tile([P, 3 * CHUNK], F32, name="rest")
+        square(first[:], early[0][:])
+        root(early[1][:], early[1][:])
+        read_y(2, 1, (2,), 1)
+        place_weighed(2, 2)
+        root(early[2][:], early[2][:])
+        for c in (1, 2):
+            square(rest[:, chunk(c - 1)], early[c][:])
+        damage(3, 0, (0,))
+        damage(3, 1, (1, 2))
+        read_y(3, 0, (0,), at=LATE_AT)
+        place_weighed(0, 3)
+        read_y(3, 1, (1, 2))
+        damage(3, 0, (3,))
+        read_y(3, 0, (3,))
+        place(3, 0, first[:], CHUNK)
+        late = staged([P, 3 * CHUNK], F32, "late", LATE_AT)
+        for i, b in enumerate((1, 2, 3)):
+            nc.gpsimd.tensor_tensor(late[:, chunk(i)], y2[b, 3], weight[3], MULT)
+        place(1, 3 * CHUNK, late[:, chunk(0)], CHUNK)
+        place(2, 3 * CHUNK, late[:, chunk(1)], CHUNK)
+        low, high = halves
+        for step in (page_root, page_square, temper):
+            for cols in halves:
+                step(0, cols)
+        root(late[:, chunk(2)], late[:, chunk(2)])
+        page_root(1, low)
+        square(rest[:, chunk(2)], late[:, chunk(2)])
+        place(3, CHUNK, rest[:], 3 * CHUNK)
+        page_square(1, low)
+        temper(1, low)
+        page_root(1, high)
+        page_root(2, low)
+        page_square(1, high)
+        temper(1, high)
+        page_root(2, high)
+        page_square(2, low)
+        temper(2, low)
+        factor_last = staged([P, CHUNK], F32, "factor_last", TAIL_AT)
+        square(factor_last[:], factors[2][:, chunk(2)])
+        page_square(2, chunk(3))
+        temper(2, chunk(2), factor_last[:])
+        jobs = [(factors[2], 2, 3)] + [(pages[3], 3, c) for c in range(CHUNKS)]
+        tail = staged([P, 5 * CHUNK], F32, "tail", TAIL_AT)
+        for i, (f, b, c) in enumerate(jobs):
+            nc.vector.tensor_tensor(tail[:, chunk(i)], f[:, chunk(c)], held[1][:, b % 2, chunk(c)], MULT)
+            nc.sync.dma_start(out[P * b : P * (b + 1), chunk(c)], tail[:, chunk(i)])

@@ -25,6 +25,8 @@ CHUNK = 256
 SUB = 128
 CHUNKS = S // CHUNK
 PAGES = N // P
+OPENED = 3
+FIRST = 192
 KB = 1024
 RAW = {(1, 0): 0, (1, 1): 8 * KB, (0, 0): 16 * KB, (0, 1): 24 * KB}
 X0_AT = (28 * KB, 2 * KB)
@@ -34,6 +36,7 @@ TAB_AT = 56 * KB
 LATE_AT = 88 * KB
 Y2_AT = 92 * KB
 TAIL_AT = 98 * KB
+MID_AT = 104 * KB
 
 
 def tile_list_adna_damage_tempering_kernel(
@@ -132,18 +135,20 @@ def tile_list_adna_damage_tempering_kernel(
             nc.vector.quantize_mx(out=codes[:].bitcast(FP8X4), scales=plane[:], in_=w1_bf[g, a][:])
             w1_codes[g, a], w1_sc[g, a] = codes, plane
 
-        y_banks = [psum.tile([P, 2 * CHUNK], F32, name="y_bank%d" % e) for e in range(2)]
-        banks = [psum.tile([P, PACK * SUB], F32, name="bank%d" % e) for e in range(6)]
+        banks = [psum.tile([P, PACK * SUB], F32, name="bank%d" % e) for e in range(8)]
+
+        def y_bank(c, e):
+            return banks[(6 if c == 0 else 4) + e]
 
         def bank_of(k, s):
-            return banks[2 * (k % 3) + s]
+            return banks[2 * (0, 1, 2, 0, 1, 3, 0, 1)[k] + s]
 
-        def first_stage(bank, j0, stationary, one_group):
+        def first_stage(bank, j0, stationary, one_group, passes=(0, 1)):
             half, c0 = divmod(j0, HALF)
             steps = [(t, a) for t in range(PACK) for a in range(PASSES)]
             if one_group:
                 steps = [(t, a) for a in range(PASSES) for t in range(PACK)]
-            for t, a in steps:
+            for t, a in [step for step in steps if step[1] in passes]:
                 codes, plane = stationary(t, a)
                 nc.tensor.matmul_mx(
                     out=bank[:, SUB * t : SUB * (t + 1)],
@@ -158,15 +163,19 @@ def tile_list_adna_damage_tempering_kernel(
         pairs = [(0, 0), (1, 0), (0, 1), (1, 1), (2, 0), (2, 1), (3, 0), (3, 1)]
         shrink = {}
 
-        def size_of_b(k, s):
+        def background(k, s, passes):
             c, g = pairs[k]
-            bank = y_banks[s] if k == 3 else bank_of(k, s)
+            bank = banks[6 + s] if k == 3 else bank_of(k, s)
 
             def columns(t, a):
                 col = H * a + HALF * g + P * t
                 return w4[:, 2 * col : 2 * (col + P)].bitcast(FP4X4), w4_sc[:, col : col + P]
 
-            first_stage(bank, CHUNK * c + SUB * s, columns, k < 3)
+            first_stage(bank, CHUNK * c + SUB * s, columns, k < OPENED, passes)
+            return bank
+
+        def size_of_b(k, s):
+            bank = background(k, s, (1,) if k < OPENED else (0, 1))
             if (k, s) == (3, 0):
                 shrink[k] = staged([P, CHUNK * PACK], F32, "shrink3", root_at(4))
             elif s == 0:
@@ -211,12 +220,12 @@ def tile_list_adna_damage_tempering_kernel(
                 )
 
             for s in range(2):
-                first_stage(bank_of(k, s), CHUNK * c + SUB * s, columns, k in (2, 3))
+                first_stage(bank_of(k, s), CHUNK * c + SUB * s, columns, k < 4)
 
         def feature(k, s):
             if s == 0:
-                if k < 2:
-                    h_bf[k] = staged([P, CHUNK * PACK], BF16, "h_first%d" % k, RAW[1, k] + 6 * KB * k)
+                if k == 1:
+                    h_bf[k] = staged([P, CHUNK * PACK], BF16, "h_held", RAW[1, 1] + 6 * KB)
                 else:
                     h_bf[k] = staged([P, CHUNK * PACK], BF16, "h_bf%d" % k, H_AT + 2 * KB * k)
             cols = slice(PACK * SUB * s, PACK * SUB * (s + 1))
@@ -247,7 +256,7 @@ def tile_list_adna_damage_tempering_kernel(
             for i, b in enumerate(blocks):
                 for g in range(2):
                     nc.tensor.matmul_mx(
-                        out=y_banks[e][:, chunk(i)],
+                        out=y_bank(c, e)[:, chunk(i)],
                         lhsT=w8[:, N * g + P * b : N * g + P * (b + 1)].bitcast(FP8X4),
                         lhsT_scale=w8_sc[4 * g : P, P * b : P * (b + 1)],
                         rhs=h_codes[c, g][:].bitcast(FP8X4),
@@ -259,7 +268,7 @@ def tile_list_adna_damage_tempering_kernel(
         def read_y(c, e, blocks, first=0, at=None):
             shape, name = [P, CHUNK * len(blocks)], "y2_%d_%d" % (blocks[0], c)
             values = keep.tile(shape, F32, name=name) if at is None else staged(shape, F32, name, at)
-            square(values[:], y_banks[e][:, CHUNK * first : CHUNK * (first + len(blocks))])
+            square(values[:], y_bank(c, e)[:, CHUNK * first : CHUNK * (first + len(blocks))])
             for i, b in enumerate(blocks):
                 y2[b, c] = values[:, chunk(i)]
 
@@ -301,6 +310,9 @@ def tile_list_adna_damage_tempering_kernel(
             nc.gpsimd.tensor_tensor(f, f if values is None else values, held[b // 2][:, b % 2, cols], MULT)
             nc.sync.dma_start(out[P * b : P * (b + 1), cols], f)
 
+        for k in range(OPENED):
+            for s in range(2):
+                background(k, s, (0,))
         size_of_b(0, 0)
         size_of_b(0, 1)
         for k in range(3):
@@ -334,7 +346,10 @@ def tile_list_adna_damage_tempering_kernel(
         quantise_h(0)
         quantise_w1(1, 1)
         features(1)
-        features(2)
+        signal(2)
+        signal(3)
+        feature(2, 0)
+        feature(2, 1)
         quantise_h(1)
         quantise_h(2)
         load_x0(1)
@@ -369,7 +384,8 @@ def tile_list_adna_damage_tempering_kernel(
         damage(0, 1, (1, 2))
         read_y(0, 0, (0, 3))
         read_y(0, 1, (1, 2), at=y2_at(0))
-        features(3)
+        feature(3, 0)
+        feature(3, 1)
         place_weighed(0, 0)
         quantise_h(3)
         place_weighed(1, 0)
@@ -400,42 +416,47 @@ def tile_list_adna_damage_tempering_kernel(
                 factor(k + 2, [], [lambda: read_y(1, 1, (2,), 1, y2_at(1)), b_step(k + 3, 0), b_step(k + 3, 1)])
                 place_weighed(2, c)
                 early[c] = weighed_early(c, y2_at(c))
-        first = keep.tile([P, CHUNK], F32, name="first")
-        rest = keep.tile([P, 3 * CHUNK], F32, name="rest")
-        square(first[:], early[0][:])
+        last = keep.tile([P, S], F32, name="last")
+        square(last[:, 0:FIRST], early[0][:, 0:FIRST])
         root(early[1][:], early[1][:])
         read_y(2, 1, (2,), 1)
         place_weighed(2, 2)
         root(early[2][:], early[2][:])
-        for c in (1, 2):
-            square(rest[:, chunk(c - 1)], early[c][:])
+        over = FIRST + SUB - CHUNK
+        square(last[:, CHUNK + over : 2 * CHUNK], early[1][:, over:CHUNK])
+        square(last[:, chunk(2)], early[2][:])
         damage(3, 0, (0,))
         damage(3, 1, (1, 2))
         read_y(3, 0, (0,), at=LATE_AT)
         place_weighed(0, 3)
-        read_y(3, 1, (1, 2))
+        read_y(3, 1, (1,), at=MID_AT)
         damage(3, 0, (3,))
         read_y(3, 0, (3,))
-        place(3, 0, first[:], CHUNK)
+        read_y(3, 1, (2,), 1)
+        place(3, 0, last[:, 0:FIRST], FIRST)
         late = staged([P, 3 * CHUNK], F32, "late", LATE_AT)
-        for i, b in enumerate((1, 2, 3)):
+        for i, b in enumerate((1, 3, 2)):
             nc.gpsimd.tensor_tensor(late[:, chunk(i)], y2[b, 3], weight[3], MULT)
         place(1, 3 * CHUNK, late[:, chunk(0)], CHUNK)
-        place(2, 3 * CHUNK, late[:, chunk(1)], CHUNK)
         low, high = halves
+        page_root(0, low)
+        page_root(0, high)
+        middle = staged([P, SUB], F32, "middle", MID_AT)
+        square(middle[:, 0 : SUB - over], early[0][:, FIRST:CHUNK])
+        square(middle[:, SUB - over : SUB], early[1][:, 0:over])
+        page_square(0, low)
+        place(3, FIRST, middle[:], SUB)
+        place(2, 3 * CHUNK, late[:, chunk(2)], CHUNK)
+        root(late[:, chunk(1)], late[:, chunk(1)])
+        page_square(0, high)
+        square(last[:, chunk(3)], late[:, chunk(1)])
+        place(3, FIRST + SUB, last[:, FIRST + SUB : S], S - FIRST - SUB)
+        temper(0, low)
+        temper(0, high)
         for step in (page_root, page_square, temper):
             for cols in halves:
-                step(0, cols)
-        root(late[:, chunk(2)], late[:, chunk(2)])
-        page_root(1, low)
-        square(rest[:, chunk(2)], late[:, chunk(2)])
-        place(3, CHUNK, rest[:], 3 * CHUNK)
-        page_square(1, low)
-        temper(1, low)
-        page_root(1, high)
+                step(1, cols)
         page_root(2, low)
-        page_square(1, high)
-        temper(1, high)
         page_root(2, high)
         page_square(2, low)
         temper(2, low)

@@ -181,11 +181,7 @@ def tile_list_adna_damage_tempering_kernel(
             elif s == 0:
                 shrink[k] = ring.tile([P, CHUNK * PACK], F32, name="shrink", tag="shrink", bufs=3)
             part = shrink[k][:, PACK * SUB * s : PACK * SUB * (s + 1)]
-            nc.scalar.activation(
-                part.rearrange("p (j t e) -> p j t e", t=PACK, e=2),
-                bank[:].rearrange("p (t j e) -> p j t e", t=PACK, e=2),
-                ACT.Abs,
-            )
+            nc.scalar.activation(part, bank[:], ACT.Abs)
 
         def root(result, values):
             nc.scalar.activation(result, values, ACT.Abs_reciprocal_sqrt, bias=1.0)
@@ -232,7 +228,7 @@ def tile_list_adna_damage_tempering_kernel(
             nc.vector.tensor_tensor(
                 h_bf[k][:, cols].rearrange("p (j e t) -> p j t e", t=PACK, e=2),
                 bank_of(k, s)[:].rearrange("p (t j e) -> p j t e", t=PACK, e=2),
-                shrink[k][:, cols].rearrange("p (j t e) -> p j t e", t=PACK, e=2),
+                shrink[k][:, cols].rearrange("p (t j e) -> p j t e", t=PACK, e=2),
                 MULT,
             )
 

@@ -26,7 +26,6 @@ SUB = 128
 CHUNKS = S // CHUNK
 PAGES = N // P
 OPENED = 3
-FIRST = 192
 KB = 1024
 RAW = {(1, 0): 0, (1, 1): 8 * KB, (0, 0): 16 * KB, (0, 1): 24 * KB}
 X0_AT = (28 * KB, 2 * KB)
@@ -36,7 +35,6 @@ TAB_AT = 56 * KB
 LATE_AT = 88 * KB
 Y2_AT = 92 * KB
 TAIL_AT = 98 * KB
-MID_AT = 104 * KB
 
 
 def tile_list_adna_damage_tempering_kernel(
@@ -66,6 +64,8 @@ def tile_list_adna_damage_tempering_kernel(
         warm_out = keep.tile([P, 1], F32, name="warm_out")
         nc.vector.memset(warm_in[:], 1.0)
         nc.scalar.activation(warm_out[:], warm_in[:], ACT.Abs_reciprocal_sqrt)
+        warm_product = keep.tile([P, 1], F32, name="warm_product")
+        nc.gpsimd.tensor_tensor(warm_product[:], warm_in[:], warm_in[:], MULT)
 
         w4_raw = keep.tile([P, PASSES * 2 * H], U8, name="w4_raw", align_bytes=64)
         for a in range(PASSES):
@@ -413,46 +413,40 @@ def tile_list_adna_damage_tempering_kernel(
                 place_weighed(2, c)
                 early[c] = weighed_early(c, y2_at(c))
         last = keep.tile([P, S], F32, name="last")
-        square(last[:, 0:FIRST], early[0][:, 0:FIRST])
+        square(last[:, chunk(0)], early[0][:])
         root(early[1][:], early[1][:])
         read_y(2, 1, (2,), 1)
         place_weighed(2, 2)
         root(early[2][:], early[2][:])
-        over = FIRST + SUB - CHUNK
-        square(last[:, CHUNK + over : 2 * CHUNK], early[1][:, over:CHUNK])
-        square(last[:, chunk(2)], early[2][:])
+        for c in (1, 2):
+            square(last[:, chunk(c)], early[c][:])
         damage(3, 0, (0,))
         damage(3, 1, (1, 2))
         read_y(3, 0, (0,), at=LATE_AT)
         place_weighed(0, 3)
-        read_y(3, 1, (1,), at=MID_AT)
+        read_y(3, 1, (1, 2))
         damage(3, 0, (3,))
         read_y(3, 0, (3,))
-        read_y(3, 1, (2,), 1)
-        place(3, 0, last[:, 0:FIRST], FIRST)
+        place(3, 0, last[:, chunk(0)], CHUNK)
         late = staged([P, 3 * CHUNK], F32, "late", LATE_AT)
-        for i, b in enumerate((1, 3, 2)):
-            nc.gpsimd.tensor_tensor(late[:, chunk(i)], y2[b, 3], weight[3], MULT)
-        place(1, 3 * CHUNK, late[:, chunk(0)], CHUNK)
+        for b in (1, 2, 3):
+            nc.gpsimd.tensor_tensor(late[:, chunk(b - 1)], y2[b, 3], weight[3], MULT)
+        for b in (1, 2):
+            place(b, 3 * CHUNK, late[:, chunk(b - 1)], CHUNK)
         low, high = halves
-        page_root(0, low)
-        page_root(0, high)
-        middle = staged([P, SUB], F32, "middle", MID_AT)
-        square(middle[:, 0 : SUB - over], early[0][:, FIRST:CHUNK])
-        square(middle[:, SUB - over : SUB], early[1][:, 0:over])
-        page_square(0, low)
-        place(3, FIRST, middle[:], SUB)
-        place(2, 3 * CHUNK, late[:, chunk(2)], CHUNK)
-        root(late[:, chunk(1)], late[:, chunk(1)])
-        page_square(0, high)
-        square(last[:, chunk(3)], late[:, chunk(1)])
-        place(3, FIRST + SUB, last[:, FIRST + SUB : S], S - FIRST - SUB)
-        temper(0, low)
-        temper(0, high)
         for step in (page_root, page_square, temper):
             for cols in halves:
-                step(1, cols)
+                step(0, cols)
+        root(late[:, chunk(2)], late[:, chunk(2)])
+        page_root(1, low)
+        square(last[:, chunk(3)], late[:, chunk(2)])
+        place(3, CHUNK, last[:, CHUNK:S], S - CHUNK)
+        page_square(1, low)
+        temper(1, low)
+        page_root(1, high)
         page_root(2, low)
+        page_square(1, high)
+        temper(1, high)
         page_root(2, high)
         page_square(2, low)
         temper(2, low)

@@ -25,7 +25,7 @@ CHUNK = 256
 SUB = 128
 CHUNKS = S // CHUNK
 PAGES = N // P
-OPENED = 3
+OPENED = 1
 KB = 1024
 RAW = {(1, 0): 0, (1, 1): 8 * KB, (0, 0): 16 * KB, (0, 1): 24 * KB}
 X0_AT = (28 * KB, 2 * KB)

@@ -145,7 +145,7 @@ def tile_list_adna_damage_tempering_kernel(
 
         def first_stage(bank, j0, stationary, one_group, passes=(0, 1)):
             half, c0 = divmod(j0, HALF)
-            steps = [(t, a) for t in range(PACK) for a in range(PASSES)]
+            steps = [(t, a) for t in range(PACK) for a in (1, 0)]
             if one_group:
                 steps = [(t, a) for a in range(PASSES) for t in range(PACK)]
             for t, a in [step for step in steps if step[1] in passes]:
@@ -156,8 +156,8 @@ def tile_list_adna_damage_tempering_kernel(
                     lhsT_scale=plane,
                     rhs=v[a, half][:, c0 : c0 + SUB].bitcast(FP8X4),
                     rhs_scale=v_sc[:, S * a + j0 : S * a + j0 + SUB],
-                    start=((t, a) == steps[0] if one_group else a == 0),
-                    stop=((t, a) == steps[-1] if one_group else a == PASSES - 1),
+                    start=((t, a) == steps[0] if one_group else a == 1),
+                    stop=((t, a) == steps[-1] if one_group else a == 0),
                 )
 
         pairs = [(0, 0), (1, 0), (0, 1), (1, 1), (2, 0), (2, 1), (3, 0), (3, 1)]

@@ -25,7 +25,6 @@ CHUNK = 256
 SUB = 128
 CHUNKS = S // CHUNK
 PAGES = N // P
-OPENED = 1
 KB = 1024
 RAW = {(1, 0): 0, (1, 1): 8 * KB, (0, 0): 16 * KB, (0, 1): 24 * KB}
 X0_AT = (28 * KB, 2 * KB)
@@ -64,8 +63,6 @@ def tile_list_adna_damage_tempering_kernel(
         warm_out = keep.tile([P, 1], F32, name="warm_out")
         nc.vector.memset(warm_in[:], 1.0)
         nc.scalar.activation(warm_out[:], warm_in[:], ACT.Abs_reciprocal_sqrt)
-        warm_product = keep.tile([P, 1], F32, name="warm_product")
-        nc.gpsimd.tensor_tensor(warm_product[:], warm_in[:], warm_in[:], MULT)
 
         w4_raw = keep.tile([P, PASSES * 2 * H], U8, name="w4_raw", align_bytes=64)
         for a in range(PASSES):
@@ -141,13 +138,14 @@ def tile_list_adna_damage_tempering_kernel(
             return banks[(6 if c == 0 else 4) + e]
 
         def bank_of(k, s):
-            return banks[2 * (0, 1, 2, 0, 1, 3, 0, 1)[k] + s]
+            return banks[(6 if k == 5 else 2 * (k % 3)) + s]
 
         def first_stage(bank, j0, stationary, one_group, passes=(0, 1)):
             half, c0 = divmod(j0, HALF)
-            steps = [(t, a) for t in range(PACK) for a in (1, 0)]
             if one_group:
                 steps = [(t, a) for a in range(PASSES) for t in range(PACK)]
+            else:
+                steps = [(t, a) for t in range(PACK) for a in reversed(range(PASSES))]
             for t, a in [step for step in steps if step[1] in passes]:
                 codes, plane = stationary(t, a)
                 nc.tensor.matmul_mx(
@@ -156,11 +154,11 @@ def tile_list_adna_damage_tempering_kernel(
                     lhsT_scale=plane,
                     rhs=v[a, half][:, c0 : c0 + SUB].bitcast(FP8X4),
                     rhs_scale=v_sc[:, S * a + j0 : S * a + j0 + SUB],
-                    start=((t, a) == steps[0] if one_group else a == 1),
+                    start=((t, a) == steps[0] if one_group else a == PASSES - 1),
                     stop=((t, a) == steps[-1] if one_group else a == 0),
                 )
 
-        pairs = [(0, 0), (1, 0), (0, 1), (1, 1), (2, 0), (2, 1), (3, 0), (3, 1)]
+        pairs = [(c, g) for g in range(2) for c in range(2)] + [(c, g) for c in range(2, CHUNKS) for g in range(2)]
         shrink = {}
 
         def background(k, s, passes):
@@ -171,17 +169,16 @@ def tile_list_adna_damage_tempering_kernel(
                 col = H * a + HALF * g + P * t
                 return w4[:, 2 * col : 2 * (col + P)].bitcast(FP4X4), w4_sc[:, col : col + P]
 
-            first_stage(bank, CHUNK * c + SUB * s, columns, k < OPENED, passes)
+            first_stage(bank, CHUNK * c + SUB * s, columns, k == 0, passes)
             return bank
 
         def size_of_b(k, s):
-            bank = background(k, s, (1,) if k < OPENED else (0, 1))
+            bank = background(k, s, (1,) if k == 0 else (0, 1))
             if (k, s) == (3, 0):
                 shrink[k] = staged([P, CHUNK * PACK], F32, "shrink3", root_at(4))
             elif s == 0:
                 shrink[k] = ring.tile([P, CHUNK * PACK], F32, name="shrink", tag="shrink", bufs=3)
-            part = shrink[k][:, PACK * SUB * s : PACK * SUB * (s + 1)]
-            nc.scalar.activation(part, bank[:], ACT.Abs)
+            nc.scalar.activation(shrink[k][:, PACK * SUB * s : PACK * SUB * (s + 1)], bank[:], ACT.Abs)
 
         def root(result, values):
             nc.scalar.activation(result, values, ACT.Abs_reciprocal_sqrt, bias=1.0)
@@ -206,6 +203,9 @@ def tile_list_adna_damage_tempering_kernel(
 
         h_bf, h_codes, h_sc = {}, {}, {}
 
+        def h_at(k):
+            return H_AT + 2 * KB * k
+
         def signal(k):
             c, g = pairs[k]
 
@@ -220,10 +220,8 @@ def tile_list_adna_damage_tempering_kernel(
 
         def feature(k, s):
             if s == 0:
-                if k == 1:
-                    h_bf[k] = staged([P, CHUNK * PACK], BF16, "h_held", RAW[1, 1] + 6 * KB)
-                else:
-                    h_bf[k] = staged([P, CHUNK * PACK], BF16, "h_bf%d" % k, H_AT + 2 * KB * k)
+                at = RAW[1, 1] + 6 * KB if k == 1 else h_at(k)
+                h_bf[k] = staged([P, CHUNK * PACK], BF16, "h_bf%d" % k, at)
             cols = slice(PACK * SUB * s, PACK * SUB * (s + 1))
             nc.vector.tensor_tensor(
                 h_bf[k][:, cols].rearrange("p (j e t) -> p j t e", t=PACK, e=2),
@@ -306,9 +304,8 @@ def tile_list_adna_damage_tempering_kernel(
             nc.gpsimd.tensor_tensor(f, f if values is None else values, held[b // 2][:, b % 2, cols], MULT)
             nc.sync.dma_start(out[P * b : P * (b + 1), cols], f)
 
-        for k in range(OPENED):
-            for s in range(2):
-                background(k, s, (0,))
+        for s in range(2):
+            background(0, s, (0,))
         size_of_b(0, 0)
         size_of_b(0, 1)
         for k in range(3):
@@ -360,14 +357,10 @@ def tile_list_adna_damage_tempering_kernel(
             weight[c] = staged([P, CHUNK], F32, "weight%d" % c, at)[:]
             nc.gpsimd.tensor_tensor(weight[c], gain[:, chunk(c)], gain[:, chunk(c)], MULT)
 
-
         def weighed_early(c, over):
             z = staged([P, CHUNK], F32, "z3_%d" % c, over)
             nc.gpsimd.tensor_tensor(z[:], y2[3, c], weight[c], MULT)
             return z
-
-        def h_at(k):
-            return H_AT + 2 * KB * k
 
         def y2_at(c):
             return Y2_AT + 2 * KB * c
@@ -389,29 +382,35 @@ def tile_list_adna_damage_tempering_kernel(
         early[0] = weighed_early(0, y2_at(0))
         weigh(1)
         factor(4, [], [b_step(5, 0), b_step(5, 1)])
-        for c in (1, 2):
-            k = 2 * c + 2
+
+        def first_half(c):
             damage(c, 0, (0, 3))
             read_y(c, 0, (0, 3))
-            features(k)
+            features(2 * c + 2)
             place_weighed(0, c)
-            quantise_h(k)
+            quantise_h(2 * c + 2)
             damage(c, 1, (1, 2))
-            if c == 1:
-                weigh_beside(2, h_at(k))
-                factor(k + 1, [], [b_step(k + 2, 0), b_step(k + 2, 1)])
-                read_y(c, 1, (1,))
-            else:
-                early[c] = weighed_early(c, h_at(k))
-                factor(k + 1, [], [lambda: weigh(3), lambda: root(early[0][:], early[0][:])])
-                read_y(c, 1, (1,), at=root_at(k + 1))
-            features(k + 1)
+
+        def second_half(c):
+            features(2 * c + 3)
             place_weighed(1, c)
-            quantise_h(k + 1)
-            if c == 1:
-                factor(k + 2, [], [lambda: read_y(1, 1, (2,), 1, y2_at(1)), b_step(k + 3, 0), b_step(k + 3, 1)])
-                place_weighed(2, c)
-                early[c] = weighed_early(c, y2_at(c))
+            quantise_h(2 * c + 3)
+
+        first_half(1)
+        weigh_beside(2, h_at(4))
+        factor(5, [], [b_step(6, 0), b_step(6, 1)])
+        read_y(1, 1, (1,))
+        second_half(1)
+        factor(6, [], [lambda: read_y(1, 1, (2,), 1, y2_at(1)), b_step(7, 0), b_step(7, 1)])
+        place_weighed(2, 1)
+        early[1] = weighed_early(1, y2_at(1))
+
+        first_half(2)
+        early[2] = weighed_early(2, h_at(6))
+        factor(7, [], [lambda: weigh(3), lambda: root(early[0][:], early[0][:])])
+        read_y(2, 1, (1,), at=root_at(7))
+        second_half(2)
+
         last = keep.tile([P, S], F32, name="last")
         square(last[:, chunk(0)], early[0][:])
         root(early[1][:], early[1][:])

@@ -34,6 +34,9 @@ TAB_AT = 56 * KB
 LATE_AT = 88 * KB
 Y2_AT = 92 * KB
 TAIL_AT = 98 * KB
+TAB_SC_AT = 104 * KB
+FIRST_CODES_AT = 110 * KB
+ROUNDED_AT = 114 * KB
 
 
 def tile_list_adna_damage_tempering_kernel(
@@ -53,7 +56,7 @@ def tile_list_adna_damage_tempering_kernel(
         places = keep.tile([P, S // 16], U16, name="places")
         nc.sync.dma_start(picks[:], offs)
 
-        tab_sc = keep.tile([P, T], U8, name="tab_sc", align_bytes=64)
+        tab_sc = staged([P, T], U8, "tab_sc", TAB_SC_AT)
         w4_sc_raw = staged([P, PASSES * H], U8, "w4_sc_raw", RAW[0, 1] - H)
         v_sc = keep.tile([P, PASSES * S], U8, name="v_sc", align_bytes=64)
         for plane in (tab_sc, w4_sc_raw, v_sc):
@@ -65,8 +68,10 @@ def tile_list_adna_damage_tempering_kernel(
         nc.scalar.activation(warm_out[:], warm_in[:], ACT.Abs_reciprocal_sqrt)
 
         w4_raw = keep.tile([P, PASSES * 2 * H], U8, name="w4_raw", align_bytes=64)
-        for a in range(PASSES):
-            nc.sync.dma_start(w4_raw[:, 2 * H * a : 2 * H * (a + 1)].bitcast(I32), w4_words[a].bitcast(I32))
+        nc.sync.dma_start(
+            w4_raw[:].bitcast(I32).rearrange("p (a n) -> p a n", a=PASSES),
+            w4_words.bitcast(I32).rearrange("a p n -> p a n"),
+        )
         nc.sync.dma_start(tab_sc[0:P:4, :].bitcast(I32), tab_scales.bitcast(I32).rearrange("a q n -> q a n"))
         for q in range(4):
             nc.sync.dma_start(
@@ -87,7 +92,7 @@ def tile_list_adna_damage_tempering_kernel(
                 v_sc_spread[32 * q : 32 * q + 32 : 4, :].bitcast(I32),
             )
 
-        w4 = keep.tile([P, PASSES * 2 * H], U8, name="w4", align_bytes=64)
+        w4 = staged([P, PASSES * 2 * H], U8, "w4", TAB_SC_AT)
         w4_sc = keep.tile([P, PASSES * H], U8, name="w4_sc", align_bytes=64)
         nc.vector.tensor_copy(
             w4_sc[:].rearrange("p (u t m) -> p u t m", t=PACK, m=P),
@@ -107,19 +112,19 @@ def tile_list_adna_damage_tempering_kernel(
                 w1_raw[g, a] = raw
 
         v = {}
-        for a in range(PASSES):
-            for half in range(2):
-                picked = keep.tile([P, HALF], U32, name="v%d_%d" % (a, half), align_bytes=64)
-                cols = HALF // 16
-                nc.vector.tensor_copy(
-                    picked[:], tab[a][:].bitcast(U32).indirect(picks[:, cols * half : cols * (half + 1)])
-                )
-                v[a, half] = picked
+        for a, c0, count in ((0, 0, 2), (0, 2, 2), (1, 0, 1), (1, 1, 1), (1, 2, 2)):
+            picked = keep.tile([P, CHUNK * count], U32, name="v%d_%d" % (a, c0), align_bytes=64)
+            cols = CHUNK // 16
+            nc.vector.tensor_copy(
+                picked[:], tab[a][:].bitcast(U32).indirect(picks[:, cols * c0 : cols * (c0 + count)])
+            )
+            for i in range(count):
+                v[a, c0 + i] = picked[:, CHUNK * i : CHUNK * (i + 1)]
 
         w1_bf, w1_codes, w1_sc = {}, {}, {}
 
         def round_w1(g, a):
-            grouped = ring.tile([P, PACK * HALF], BF16, name="w1_bf", tag="w1_bf", bufs=1, align_bytes=64)
+            grouped = staged([P, PACK * HALF], BF16, "w1_bf%d_%d" % (g, a), ROUNDED_AT + 4 * KB * a)
             nc.vector.tensor_copy(
                 grouped[:].rearrange("p (t m j) -> p m t j", t=PACK, j=PACK),
                 w1_raw[g, a][:].rearrange("p j (m t) -> p m t j", t=PACK),
@@ -141,7 +146,7 @@ def tile_list_adna_damage_tempering_kernel(
             return banks[(6 if k == 5 else 2 * (k % 3)) + s]
 
         def first_stage(bank, j0, stationary, one_group, passes=(0, 1)):
-            half, c0 = divmod(j0, HALF)
+            c, c0 = divmod(j0, CHUNK)
             if one_group:
                 steps = [(t, a) for a in range(PASSES) for t in range(PACK)]
             else:
@@ -152,7 +157,7 @@ def tile_list_adna_damage_tempering_kernel(
                     out=bank[:, SUB * t : SUB * (t + 1)],
                     lhsT=codes,
                     lhsT_scale=plane,
-                    rhs=v[a, half][:, c0 : c0 + SUB].bitcast(FP8X4),
+                    rhs=v[a, c][:, c0 : c0 + SUB].bitcast(FP8X4),
                     rhs_scale=v_sc[:, S * a + j0 : S * a + j0 + SUB],
                     start=((t, a) == steps[0] if one_group else a == PASSES - 1),
                     stop=((t, a) == steps[-1] if one_group else a == 0),
@@ -172,13 +177,20 @@ def tile_list_adna_damage_tempering_kernel(
             first_stage(bank, CHUNK * c + SUB * s, columns, k == 0, passes)
             return bank
 
+        parts = []
+
+        def factor_part(k, s):
+            return parts[s][:] if k == 4 else shrink[k][:, PACK * SUB * s : PACK * SUB * (s + 1)]
+
         def size_of_b(k, s):
             bank = background(k, s, (1,) if k == 0 else (0, 1))
             if (k, s) == (3, 0):
                 shrink[k] = staged([P, CHUNK * PACK], F32, "shrink3", root_at(4))
+            elif k == 4:
+                parts.append(staged([P, PACK * SUB], F32, "shrink4_%d" % s, FIRST_CODES_AT + (64 if s else -2 * KB)))
             elif s == 0:
                 shrink[k] = ring.tile([P, CHUNK * PACK], F32, name="shrink", tag="shrink", bufs=3)
-            nc.scalar.activation(shrink[k][:, PACK * SUB * s : PACK * SUB * (s + 1)], bank[:], ACT.Abs)
+            nc.scalar.activation(factor_part(k, s), bank[:], ACT.Abs)
 
         def root(result, values):
             nc.scalar.activation(result, values, ACT.Abs_reciprocal_sqrt, bias=1.0)
@@ -226,7 +238,7 @@ def tile_list_adna_damage_tempering_kernel(
             nc.vector.tensor_tensor(
                 h_bf[k][:, cols].rearrange("p (j e t) -> p j t e", t=PACK, e=2),
                 bank_of(k, s)[:].rearrange("p (t j e) -> p j t e", t=PACK, e=2),
-                shrink[k][:, cols].rearrange("p (t j e) -> p j t e", t=PACK, e=2),
+                factor_part(k, s).rearrange("p (t j e) -> p j t e", t=PACK, e=2),
                 MULT,
             )
 
@@ -238,6 +250,8 @@ def tile_list_adna_damage_tempering_kernel(
         def quantise_h(k):
             if k + 1 == len(pairs):
                 codes = staged([P, CHUNK], U32, "h_codes_last", LAST_CODES_AT)
+            elif k == 2:
+                codes = staged([P, CHUNK], U32, "h_codes%d" % k, FIRST_CODES_AT + KB * k)
             else:
                 codes = keep.tile([P, CHUNK], U32, name="h_codes%d" % k, align_bytes=64)
             plane = keep.tile([P, CHUNK], U8, name="h_sc%d" % k, align_bytes=64)
@@ -349,8 +363,9 @@ def tile_list_adna_damage_tempering_kernel(
 
         weight = {}
 
-        def weigh(c):
-            weight[c] = keep.tile([P, CHUNK], F32, name="weight%d" % c)[:]
+        def weigh(c, at=None):
+            name = "weight%d" % c
+            weight[c] = (keep.tile([P, CHUNK], F32, name=name) if at is None else staged([P, CHUNK], F32, name, at))[:]
             square(weight[c], gain[:, chunk(c)])
 
         def weigh_beside(c, at):
@@ -366,12 +381,14 @@ def tile_list_adna_damage_tempering_kernel(
             return Y2_AT + 2 * KB * c
 
         early = {}
-        factor(3, [], [lambda: weigh(0)])
-        size_of_b(4, 0)
-        size_of_b(4, 1)
+        both = staged([P, 2 * CHUNK], F32, "weight01", ROUNDED_AT + 4 * KB)
+        nc.gpsimd.tensor_tensor(both[:], gain[:, halves[0]], gain[:, halves[0]], MULT)
+        weight[0], weight[1] = both[:, chunk(0)], both[:, chunk(1)]
+        factor(3, [], [b_step(4, 0)])
         damage(0, 0, (0, 3))
         damage(0, 1, (1, 2))
         read_y(0, 0, (0, 3))
+        size_of_b(4, 1)
         read_y(0, 1, (1, 2), at=y2_at(0))
         feature(3, 0)
         feature(3, 1)
@@ -380,8 +397,13 @@ def tile_list_adna_damage_tempering_kernel(
         place_weighed(1, 0)
         place_weighed(2, 0)
         early[0] = weighed_early(0, y2_at(0))
-        weigh(1)
-        factor(4, [], [b_step(5, 0), b_step(5, 1)])
+        r4 = staged([P, CHUNK * PACK], F32, "root4", root_at(4))
+        for s in range(2):
+            root(r4[:, halves[s]], parts[s][:])
+        size_of_b(5, 0)
+        size_of_b(5, 1)
+        for s in range(2):
+            square(parts[s][:], r4[:, halves[s]])
 
         def first_half(c):
             damage(c, 0, (0, 3))
@@ -407,8 +429,9 @@ def tile_list_adna_damage_tempering_kernel(
 
         first_half(2)
         early[2] = weighed_early(2, h_at(6))
-        factor(7, [], [lambda: weigh(3), lambda: root(early[0][:], early[0][:])])
+        factor(7, [], [lambda: root(early[0][:], early[0][:])])
         read_y(2, 1, (1,), at=root_at(7))
+        weigh(3, root_at(7) + KB)
         second_half(2)
 
         last = keep.tile([P, S], F32, name="last")

@@ -34,7 +34,6 @@ TAB_AT = 56 * KB
 LATE_AT = 88 * KB
 Y2_AT = 92 * KB
 TAIL_AT = 98 * KB
-TAB_SC_AT = 104 * KB
 FIRST_CODES_AT = 110 * KB
 ROUNDED_AT = 114 * KB
 
@@ -56,10 +55,10 @@ def tile_list_adna_damage_tempering_kernel(
         places = keep.tile([P, S // 16], U16, name="places")
         nc.sync.dma_start(picks[:], offs)
 
-        tab_sc = staged([P, T], U8, "tab_sc", TAB_SC_AT)
+        tab_sc = keep.tile([P, T], U8, name="tab_sc", align_bytes=64)
         w4_sc_raw = staged([P, PASSES * H], U8, "w4_sc_raw", RAW[0, 1] - H)
-        v_sc = keep.tile([P, PASSES * S], U8, name="v_sc", align_bytes=64)
-        for plane in (tab_sc, w4_sc_raw, v_sc):
+        v_sc = [keep.tile([P, PASSES * HALF], U8, name="v_sc%d" % half, align_bytes=64) for half in range(2)]
+        for plane in (tab_sc, w4_sc_raw, v_sc[0], v_sc[1]):
             nc.vector.memset(plane[:].bitcast(I32), 0)
 
         warm_in = keep.tile([P, 1], F32, name="warm_in")
@@ -68,10 +67,8 @@ def tile_list_adna_damage_tempering_kernel(
         nc.scalar.activation(warm_out[:], warm_in[:], ACT.Abs_reciprocal_sqrt)
 
         w4_raw = keep.tile([P, PASSES * 2 * H], U8, name="w4_raw", align_bytes=64)
-        nc.sync.dma_start(
-            w4_raw[:].bitcast(I32).rearrange("p (a n) -> p a n", a=PASSES),
-            w4_words.bitcast(I32).rearrange("a p n -> p a n"),
-        )
+        for a in range(PASSES):
+            nc.sync.dma_start(w4_raw[:, 2 * H * a : 2 * H * (a + 1)].bitcast(I32), w4_words[a].bitcast(I32))
         nc.sync.dma_start(tab_sc[0:P:4, :].bitcast(I32), tab_scales.bitcast(I32).rearrange("a q n -> q a n"))
         for q in range(4):
             nc.sync.dma_start(
@@ -84,15 +81,19 @@ def tile_list_adna_damage_tempering_kernel(
             nc.sync.dma_start(words[:], tab_words[a].rearrange("p n i -> p (n i)").bitcast(I32))
             tab.append(words)
 
-        v_sc_spread = staged([P, S], U8, "v_sc_spread", RAW[1, 1] - S // 2)
-        nc.vector.tensor_copy(v_sc_spread[:], tab_sc[:].indirect(picks[:]))
-        for q in range(4):
-            nc.scalar.dma_start(
-                v_sc[32 * q : 32 * q + 4, :].bitcast(I32).rearrange("r (a n) -> r a n", a=PASSES),
-                v_sc_spread[32 * q : 32 * q + 32 : 4, :].bitcast(I32),
-            )
+        def pick_scales(half, at, queue):
+            spread = staged([P, HALF], U8, "v_sc_spread%d" % half, at)
+            cols = HALF // 16
+            nc.vector.tensor_copy(spread[:], tab_sc[:].indirect(picks[:, cols * half : cols * (half + 1)]))
+            for q in range(4):
+                queue.dma_start(
+                    v_sc[half][32 * q : 32 * q + 4, :].bitcast(I32).rearrange("r (a n) -> r a n", a=PASSES),
+                    spread[32 * q : 32 * q + 32 : 4, :].bitcast(I32),
+                )
 
-        w4 = staged([P, PASSES * 2 * H], U8, "w4", TAB_SC_AT)
+        pick_scales(0, RAW[1, 1] - HALF // 2, nc.scalar)
+
+        w4 = keep.tile([P, PASSES * 2 * H], U8, name="w4", align_bytes=64)
         w4_sc = keep.tile([P, PASSES * H], U8, name="w4_sc", align_bytes=64)
         nc.vector.tensor_copy(
             w4_sc[:].rearrange("p (u t m) -> p u t m", t=PACK, m=P),
@@ -104,12 +105,15 @@ def tile_list_adna_damage_tempering_kernel(
         )
 
         w1_raw = {}
-        for g in range(2):
-            for a in range(PASSES):
-                raw = staged([P, PACK, HALF], F32, "w1_raw%d_%d" % (g, a), RAW[g, a])
-                rows = w1[KP * a : KP * (a + 1), HALF * g : HALF * (g + 1)]
-                nc.sync.dma_start(raw[:], rows.rearrange("(p j) c -> p j c", j=PACK))
-                w1_raw[g, a] = raw
+
+        def load_w1(g, a):
+            raw = staged([P, PACK, HALF], F32, "w1_raw%d_%d" % (g, a), RAW[g, a])
+            rows = w1[KP * a : KP * (a + 1), HALF * g : HALF * (g + 1)]
+            nc.sync.dma_start(raw[:], rows.rearrange("(p j) c -> p j c", j=PACK))
+            w1_raw[g, a] = raw
+
+        for g, a in ((0, 0), (0, 1), (1, 0)):
+            load_w1(g, a)
 
         v = {}
         for a, c0, count in ((0, 0, 2), (0, 2, 2), (1, 0, 1), (1, 1, 1), (1, 2, 2)):
@@ -120,6 +124,9 @@ def tile_list_adna_damage_tempering_kernel(
             )
             for i in range(count):
                 v[a, c0 + i] = picked[:, CHUNK * i : CHUNK * (i + 1)]
+            if (a, c0) == (0, 2):
+                pick_scales(1, TAB_AT + 12 * KB, nc.sync)
+                load_w1(1, 1)
 
         w1_bf, w1_codes, w1_sc = {}, {}, {}
 
@@ -158,7 +165,7 @@ def tile_list_adna_damage_tempering_kernel(
                     lhsT=codes,
                     lhsT_scale=plane,
                     rhs=v[a, c][:, c0 : c0 + SUB].bitcast(FP8X4),
-                    rhs_scale=v_sc[:, S * a + j0 : S * a + j0 + SUB],
+                    rhs_scale=v_sc[j0 // HALF][:, HALF * a + j0 % HALF : HALF * a + j0 % HALF + SUB],
                     start=((t, a) == steps[0] if one_group else a == PASSES - 1),
                     stop=((t, a) == steps[-1] if one_group else a == 0),
                 )

@@ -26,14 +26,16 @@ SUB = 128
 CHUNKS = S // CHUNK
 PAGES = N // P
 KB = 1024
-RAW = {(1, 0): 0, (1, 1): 8 * KB, (0, 0): 16 * KB, (0, 1): 24 * KB}
-X0_AT = (28 * KB, 2 * KB)
-H_AT = 36 * KB
-LAST_CODES_AT = 52 * KB
-TAB_AT = 56 * KB
-LATE_AT = 88 * KB
-Y2_AT = 92 * KB
-TAIL_AT = 98 * KB
+OPENED = 4
+RAW = {(1, 0): 0, (1, 1): 8 * KB, (0, 0): 16 * KB, (0, 1): 28 * KB}
+W4_AT = 24 * KB
+X0_AT = (32 * KB, 2 * KB)
+H_AT = 40 * KB
+LAST_CODES_AT = 56 * KB
+TAB_AT = 60 * KB
+LATE_AT = 92 * KB
+Y2_AT = 96 * KB
+TAIL_AT = 102 * KB
 FIRST_CODES_AT = 110 * KB
 ROUNDED_AT = 114 * KB
 
@@ -56,7 +58,7 @@ def tile_list_adna_damage_tempering_kernel(
         nc.sync.dma_start(picks[:], offs)
 
         tab_sc = keep.tile([P, T], U8, name="tab_sc", align_bytes=64)
-        w4_sc_raw = staged([P, PASSES * H], U8, "w4_sc_raw", RAW[0, 1] - H)
+        w4_sc_raw = staged([P, 4 * KB + 128], U8, "w4_sc_raw", W4_AT - 64)[:, 0 : PASSES * H]
         v_sc = [keep.tile([P, PASSES * HALF], U8, name="v_sc%d" % half, align_bytes=64) for half in range(2)]
         for plane in (tab_sc, w4_sc_raw, v_sc[0], v_sc[1]):
             nc.vector.memset(plane[:].bitcast(I32), 0)
@@ -75,25 +77,27 @@ def tile_list_adna_damage_tempering_kernel(
                 w4_sc_raw[32 * q : 32 * q + 4, :].bitcast(I32).rearrange("r (a n) -> r a n", a=PASSES),
                 w4_scales[:, 4 * q : 4 * q + 4, :].bitcast(I32).rearrange("a r n -> r a n"),
             )
-        tab = []
-        for a in range(PASSES):
-            words = staged([P, T], I32, "tab%d" % a, TAB_AT + 16 * KB * a)
-            nc.sync.dma_start(words[:], tab_words[a].rearrange("p n i -> p (n i)").bitcast(I32))
-            tab.append(words)
+        tab = [staged([P, T], I32, "tab%d" % a, TAB_AT + 16 * KB * a) for a in range(PASSES)]
 
-        def pick_scales(half, at, queue):
+        def load_tab(a):
+            nc.sync.dma_start(tab[a][:], tab_words[a].rearrange("p n i -> p (n i)").bitcast(I32))
+
+        load_tab(0)
+
+        def pick_scales(half, at):
             spread = staged([P, HALF], U8, "v_sc_spread%d" % half, at)
             cols = HALF // 16
             nc.vector.tensor_copy(spread[:], tab_sc[:].indirect(picks[:, cols * half : cols * (half + 1)]))
             for q in range(4):
-                queue.dma_start(
+                nc.sync.dma_start(
                     v_sc[half][32 * q : 32 * q + 4, :].bitcast(I32).rearrange("r (a n) -> r a n", a=PASSES),
                     spread[32 * q : 32 * q + 32 : 4, :].bitcast(I32),
                 )
 
-        pick_scales(0, RAW[1, 1] - HALF // 2, nc.scalar)
+        pick_scales(0, RAW[1, 1] - HALF // 2)
+        load_tab(1)
 
-        w4 = keep.tile([P, PASSES * 2 * H], U8, name="w4", align_bytes=64)
+        w4 = staged([P, PASSES * 2 * H], U8, "w4", W4_AT)
         w4_sc = keep.tile([P, PASSES * H], U8, name="w4_sc", align_bytes=64)
         nc.vector.tensor_copy(
             w4_sc[:].rearrange("p (u t m) -> p u t m", t=PACK, m=P),
@@ -125,24 +129,29 @@ def tile_list_adna_damage_tempering_kernel(
             for i in range(count):
                 v[a, c0 + i] = picked[:, CHUNK * i : CHUNK * (i + 1)]
             if (a, c0) == (0, 2):
-                pick_scales(1, TAB_AT + 12 * KB, nc.sync)
+                pick_scales(1, TAB_AT + 12 * KB)
                 load_w1(1, 1)
 
         w1_bf, w1_codes, w1_sc = {}, {}, {}
 
-        def round_w1(g, a):
-            grouped = staged([P, PACK * HALF], BF16, "w1_bf%d_%d" % (g, a), ROUNDED_AT + 4 * KB * a)
+        def round_w1(g, a, t0=0, count=PACK):
+            if t0 == 0:
+                w1_bf[g, a] = staged([P, PACK * HALF], BF16, "w1_bf%d_%d" % (g, a), ROUNDED_AT + 4 * KB * a)
             nc.vector.tensor_copy(
-                grouped[:].rearrange("p (t m j) -> p m t j", t=PACK, j=PACK),
-                w1_raw[g, a][:].rearrange("p j (m t) -> p m t j", t=PACK),
+                w1_bf[g, a][:, HALF * t0 : HALF * (t0 + count)].rearrange("p (t m j) -> p m t j", t=count, j=PACK),
+                w1_raw[g, a][:].rearrange("p j (m t) -> p m t j", t=PACK)[:, :, t0 : t0 + count, :],
             )
-            w1_bf[g, a] = grouped
 
-        def quantise_w1(g, a):
-            codes = keep.tile([P, HALF], U32, name="w1c%d_%d" % (g, a), align_bytes=64)
-            plane = keep.tile([P, HALF], U8, name="w1s%d_%d" % (g, a), align_bytes=64)
-            nc.vector.quantize_mx(out=codes[:].bitcast(FP8X4), scales=plane[:], in_=w1_bf[g, a][:])
-            w1_codes[g, a], w1_sc[g, a] = codes, plane
+        def quantise_w1(g, a, t0=0, count=PACK):
+            if t0 == 0:
+                w1_codes[g, a] = keep.tile([P, HALF], U32, name="w1c%d_%d" % (g, a), align_bytes=64)
+                w1_sc[g, a] = keep.tile([P, HALF], U8, name="w1s%d_%d" % (g, a), align_bytes=64)
+            cols = slice(P * t0, P * (t0 + count))
+            nc.vector.quantize_mx(
+                out=w1_codes[g, a][:, cols].bitcast(FP8X4),
+                scales=w1_sc[g, a][:, cols],
+                in_=w1_bf[g, a][:, HALF * t0 : HALF * (t0 + count)],
+            )
 
         banks = [psum.tile([P, PACK * SUB], F32, name="bank%d" % e) for e in range(8)]
 
@@ -181,7 +190,7 @@ def tile_list_adna_damage_tempering_kernel(
                 col = H * a + HALF * g + P * t
                 return w4[:, 2 * col : 2 * (col + P)].bitcast(FP4X4), w4_sc[:, col : col + P]
 
-            first_stage(bank, CHUNK * c + SUB * s, columns, k == 0, passes)
+            first_stage(bank, CHUNK * c + SUB * s, columns, k < OPENED, passes)
             return bank
 
         parts = []
@@ -190,7 +199,7 @@ def tile_list_adna_damage_tempering_kernel(
             return parts[s][:] if k == 4 else shrink[k][:, PACK * SUB * s : PACK * SUB * (s + 1)]
 
         def size_of_b(k, s):
-            bank = background(k, s, (1,) if k == 0 else (0, 1))
+            bank = background(k, s, (1,) if k < OPENED else (0, 1))
             if (k, s) == (3, 0):
                 shrink[k] = staged([P, CHUNK * PACK], F32, "shrink3", root_at(4))
             elif k == 4:
@@ -325,15 +334,17 @@ def tile_list_adna_damage_tempering_kernel(
             nc.gpsimd.tensor_tensor(f, f if values is None else values, held[b // 2][:, b % 2, cols], MULT)
             nc.sync.dma_start(out[P * b : P * (b + 1), cols], f)
 
-        for s in range(2):
-            background(0, s, (0,))
+        for k in range(OPENED):
+            for s in range(2):
+                background(k, s, (0,))
         size_of_b(0, 0)
         size_of_b(0, 1)
         for k in range(3):
             factor(k, [b_step(k + 1, 0)], [b_step(k + 1, 1)])
         for a in range(PASSES):
-            round_w1(0, a)
-            quantise_w1(0, a)
+            for step in (round_w1, quantise_w1):
+                for t0 in (0, 2):
+                    step(0, a, t0, 2)
         w8 = staged([P, PASSES * N], I32, "w8", RAW[0, 0])
         nc.sync.dma_start(
             w8[:].rearrange("p (a n) -> p a n", a=PASSES),

@@ -36,7 +36,7 @@ TAB_AT = 60 * KB
 LATE_AT = 92 * KB
 Y2_AT = 96 * KB
 TAIL_AT = 102 * KB
-FIRST_CODES_AT = 110 * KB
+W4_RAW_AT = 108 * KB
 ROUNDED_AT = 114 * KB
 
 
@@ -57,10 +57,10 @@ def tile_list_adna_damage_tempering_kernel(
         places = keep.tile([P, S // 16], U16, name="places")
         nc.sync.dma_start(picks[:], offs)
 
-        tab_sc = keep.tile([P, T], U8, name="tab_sc", align_bytes=64)
+        tab_sc = staged([P, T], U8, "tab_sc", TAB_AT + 16 * KB)
         w4_sc_raw = staged([P, 4 * KB + 128], U8, "w4_sc_raw", W4_AT - 64)[:, 0 : PASSES * H]
-        v_sc = [keep.tile([P, PASSES * HALF], U8, name="v_sc%d" % half, align_bytes=64) for half in range(2)]
-        for plane in (tab_sc, w4_sc_raw, v_sc[0], v_sc[1]):
+        v_sc = [keep.tile([P, PASSES * HALF], U8, name="v_sc0", align_bytes=64)]
+        for plane in (tab_sc, w4_sc_raw, v_sc[0]):
             nc.vector.memset(plane[:].bitcast(I32), 0)
 
         warm_in = keep.tile([P, 1], F32, name="warm_in")
@@ -68,7 +68,7 @@ def tile_list_adna_damage_tempering_kernel(
         nc.vector.memset(warm_in[:], 1.0)
         nc.scalar.activation(warm_out[:], warm_in[:], ACT.Abs_reciprocal_sqrt)
 
-        w4_raw = keep.tile([P, PASSES * 2 * H], U8, name="w4_raw", align_bytes=64)
+        w4_raw = staged([P, PASSES * 2 * H], U8, "w4_raw", W4_RAW_AT)
         for a in range(PASSES):
             nc.sync.dma_start(w4_raw[:, 2 * H * a : 2 * H * (a + 1)].bitcast(I32), w4_words[a].bitcast(I32))
         nc.sync.dma_start(tab_sc[0:P:4, :].bitcast(I32), tab_scales.bitcast(I32).rearrange("a q n -> q a n"))
@@ -84,17 +84,22 @@ def tile_list_adna_damage_tempering_kernel(
 
         load_tab(0)
 
-        def pick_scales(half, at):
-            spread = staged([P, HALF], U8, "v_sc_spread%d" % half, at)
-            cols = HALF // 16
-            nc.vector.tensor_copy(spread[:], tab_sc[:].indirect(picks[:, cols * half : cols * (half + 1)]))
+        spread = [
+            staged([P, HALF], U8, "v_sc_spread0", RAW[1, 1] - HALF // 2),
+            keep.tile([P, HALF], U8, name="v_sc_spread1", align_bytes=64),
+        ]
+
+        def move_scales(half):
             for q in range(4):
-                nc.sync.dma_start(
+                nc.scalar.dma_start(
                     v_sc[half][32 * q : 32 * q + 4, :].bitcast(I32).rearrange("r (a n) -> r a n", a=PASSES),
-                    spread[32 * q : 32 * q + 32 : 4, :].bitcast(I32),
+                    spread[half][32 * q : 32 * q + 32 : 4, :].bitcast(I32),
                 )
 
-        pick_scales(0, RAW[1, 1] - HALF // 2)
+        for half in range(2):
+            cols = HALF // 16
+            nc.vector.tensor_copy(spread[half][:], tab_sc[:].indirect(picks[:, cols * half : cols * (half + 1)]))
+        move_scales(0)
         load_tab(1)
 
         w4 = staged([P, PASSES * 2 * H], U8, "w4", W4_AT)
@@ -108,6 +113,10 @@ def tile_list_adna_damage_tempering_kernel(
             w4_raw[:].bitcast(U16).rearrange("p (u m t) -> p u t m", t=PACK, m=P),
         )
 
+        v_sc.append(staged([P, PASSES * HALF], U8, "v_sc1", W4_RAW_AT))
+        nc.vector.memset(v_sc[1][:].bitcast(I32), 0)
+        move_scales(1)
+
         w1_raw = {}
 
         def load_w1(g, a):
@@ -116,8 +125,9 @@ def tile_list_adna_damage_tempering_kernel(
             nc.sync.dma_start(raw[:], rows.rearrange("(p j) c -> p j c", j=PACK))
             w1_raw[g, a] = raw
 
-        for g, a in ((0, 0), (0, 1), (1, 0)):
-            load_w1(g, a)
+        for g in range(2):
+            for a in range(PASSES):
+                load_w1(g, a)
 
         v = {}
         for a, c0, count in ((0, 0, 2), (0, 2, 2), (1, 0, 1), (1, 1, 1), (1, 2, 2)):
@@ -128,9 +138,6 @@ def tile_list_adna_damage_tempering_kernel(
             )
             for i in range(count):
                 v[a, c0 + i] = picked[:, CHUNK * i : CHUNK * (i + 1)]
-            if (a, c0) == (0, 2):
-                pick_scales(1, TAB_AT + 12 * KB)
-                load_w1(1, 1)
 
         w1_bf, w1_codes, w1_sc = {}, {}, {}
 
@@ -193,20 +200,13 @@ def tile_list_adna_damage_tempering_kernel(
             first_stage(bank, CHUNK * c + SUB * s, columns, k < OPENED, passes)
             return bank
 
-        parts = []
-
-        def factor_part(k, s):
-            return parts[s][:] if k == 4 else shrink[k][:, PACK * SUB * s : PACK * SUB * (s + 1)]
-
         def size_of_b(k, s):
             bank = background(k, s, (1,) if k < OPENED else (0, 1))
             if (k, s) == (3, 0):
                 shrink[k] = staged([P, CHUNK * PACK], F32, "shrink3", root_at(4))
-            elif k == 4:
-                parts.append(staged([P, PACK * SUB], F32, "shrink4_%d" % s, FIRST_CODES_AT + (64 if s else -2 * KB)))
             elif s == 0:
                 shrink[k] = ring.tile([P, CHUNK * PACK], F32, name="shrink", tag="shrink", bufs=3)
-            nc.scalar.activation(factor_part(k, s), bank[:], ACT.Abs)
+            nc.scalar.activation(shrink[k][:, PACK * SUB * s : PACK * SUB * (s + 1)], bank[:], ACT.Abs)
 
         def root(result, values):
             nc.scalar.activation(result, values, ACT.Abs_reciprocal_sqrt, bias=1.0)
@@ -254,7 +254,7 @@ def tile_list_adna_damage_tempering_kernel(
             nc.vector.tensor_tensor(
                 h_bf[k][:, cols].rearrange("p (j e t) -> p j t e", t=PACK, e=2),
                 bank_of(k, s)[:].rearrange("p (t j e) -> p j t e", t=PACK, e=2),
-                factor_part(k, s).rearrange("p (t j e) -> p j t e", t=PACK, e=2),
+                shrink[k][:, cols].rearrange("p (t j e) -> p j t e", t=PACK, e=2),
                 MULT,
             )
 
@@ -266,8 +266,6 @@ def tile_list_adna_damage_tempering_kernel(
         def quantise_h(k):
             if k + 1 == len(pairs):
                 codes = staged([P, CHUNK], U32, "h_codes_last", LAST_CODES_AT)
-            elif k == 2:
-                codes = staged([P, CHUNK], U32, "h_codes%d" % k, FIRST_CODES_AT + KB * k)
             else:
                 codes = keep.tile([P, CHUNK], U32, name="h_codes%d" % k, align_bytes=64)
             plane = keep.tile([P, CHUNK], U8, name="h_sc%d" % k, align_bytes=64)
@@ -402,7 +400,11 @@ def tile_list_adna_damage_tempering_kernel(
         both = staged([P, 2 * CHUNK], F32, "weight01", ROUNDED_AT + 4 * KB)
         nc.gpsimd.tensor_tensor(both[:], gain[:, halves[0]], gain[:, halves[0]], MULT)
         weight[0], weight[1] = both[:, chunk(0)], both[:, chunk(1)]
-        factor(3, [], [b_step(4, 0)])
+        r3 = staged([P, CHUNK * PACK], F32, "root3", root_at(3))
+        root(r3[:], shrink[3][:])
+        size_of_b(4, 0)
+        for cols in halves:
+            square(shrink[3][:, cols], r3[:, cols])
         damage(0, 0, (0, 3))
         damage(0, 1, (1, 2))
         read_y(0, 0, (0, 3))
@@ -415,13 +417,7 @@ def tile_list_adna_damage_tempering_kernel(
         place_weighed(1, 0)
         place_weighed(2, 0)
         early[0] = weighed_early(0, y2_at(0))
-        r4 = staged([P, CHUNK * PACK], F32, "root4", root_at(4))
-        for s in range(2):
-            root(r4[:, halves[s]], parts[s][:])
-        size_of_b(5, 0)
-        size_of_b(5, 1)
-        for s in range(2):
-            square(parts[s][:], r4[:, halves[s]])
+        factor(4, [], [b_step(5, 0), b_step(5, 1)])
 
         def first_half(c):
             damage(c, 0, (0, 3))

@@ -38,6 +38,7 @@ Y2_AT = 96 * KB
 TAIL_AT = 102 * KB
 W4_RAW_AT = 108 * KB
 ROUNDED_AT = 114 * KB
+FIRST_CODES_AT = 124 * KB
 
 
 def tile_list_adna_damage_tempering_kernel(
@@ -141,24 +142,19 @@ def tile_list_adna_damage_tempering_kernel(
 
         w1_bf, w1_codes, w1_sc = {}, {}, {}
 
-        def round_w1(g, a, t0=0, count=PACK):
-            if t0 == 0:
-                w1_bf[g, a] = staged([P, PACK * HALF], BF16, "w1_bf%d_%d" % (g, a), ROUNDED_AT + 4 * KB * a)
+        def round_w1(g, a):
+            grouped = staged([P, PACK * HALF], BF16, "w1_bf%d_%d" % (g, a), ROUNDED_AT + 4 * KB * a)
             nc.vector.tensor_copy(
-                w1_bf[g, a][:, HALF * t0 : HALF * (t0 + count)].rearrange("p (t m j) -> p m t j", t=count, j=PACK),
-                w1_raw[g, a][:].rearrange("p j (m t) -> p m t j", t=PACK)[:, :, t0 : t0 + count, :],
+                grouped[:].rearrange("p (t m j) -> p m t j", t=PACK, j=PACK),
+                w1_raw[g, a][:].rearrange("p j (m t) -> p m t j", t=PACK),
             )
+            w1_bf[g, a] = grouped
 
-        def quantise_w1(g, a, t0=0, count=PACK):
-            if t0 == 0:
-                w1_codes[g, a] = keep.tile([P, HALF], U32, name="w1c%d_%d" % (g, a), align_bytes=64)
-                w1_sc[g, a] = keep.tile([P, HALF], U8, name="w1s%d_%d" % (g, a), align_bytes=64)
-            cols = slice(P * t0, P * (t0 + count))
-            nc.vector.quantize_mx(
-                out=w1_codes[g, a][:, cols].bitcast(FP8X4),
-                scales=w1_sc[g, a][:, cols],
-                in_=w1_bf[g, a][:, HALF * t0 : HALF * (t0 + count)],
-            )
+        def quantise_w1(g, a):
+            codes = keep.tile([P, HALF], U32, name="w1c%d_%d" % (g, a), align_bytes=64)
+            plane = keep.tile([P, HALF], U8, name="w1s%d_%d" % (g, a), align_bytes=64)
+            nc.vector.quantize_mx(out=codes[:].bitcast(FP8X4), scales=plane[:], in_=w1_bf[g, a][:])
+            w1_codes[g, a], w1_sc[g, a] = codes, plane
 
         banks = [psum.tile([P, PACK * SUB], F32, name="bank%d" % e) for e in range(8)]
 
@@ -200,13 +196,20 @@ def tile_list_adna_damage_tempering_kernel(
             first_stage(bank, CHUNK * c + SUB * s, columns, k < OPENED, passes)
             return bank
 
+        parts = []
+
+        def factor_part(k, s):
+            return parts[s][:] if k == 4 else shrink[k][:, PACK * SUB * s : PACK * SUB * (s + 1)]
+
         def size_of_b(k, s):
             bank = background(k, s, (1,) if k < OPENED else (0, 1))
             if (k, s) == (3, 0):
                 shrink[k] = staged([P, CHUNK * PACK], F32, "shrink3", root_at(4))
+            elif k == 4:
+                parts.append(staged([P, PACK * SUB], F32, "shrink4_%d" % s, FIRST_CODES_AT + (64 if s else -2 * KB)))
             elif s == 0:
                 shrink[k] = ring.tile([P, CHUNK * PACK], F32, name="shrink", tag="shrink", bufs=3)
-            nc.scalar.activation(shrink[k][:, PACK * SUB * s : PACK * SUB * (s + 1)], bank[:], ACT.Abs)
+            nc.scalar.activation(factor_part(k, s), bank[:], ACT.Abs)
 
         def root(result, values):
             nc.scalar.activation(result, values, ACT.Abs_reciprocal_sqrt, bias=1.0)
@@ -254,7 +257,7 @@ def tile_list_adna_damage_tempering_kernel(
             nc.vector.tensor_tensor(
                 h_bf[k][:, cols].rearrange("p (j e t) -> p j t e", t=PACK, e=2),
                 bank_of(k, s)[:].rearrange("p (t j e) -> p j t e", t=PACK, e=2),
-                shrink[k][:, cols].rearrange("p (t j e) -> p j t e", t=PACK, e=2),
+                factor_part(k, s).rearrange("p (t j e) -> p j t e", t=PACK, e=2),
                 MULT,
             )
 
@@ -266,6 +269,8 @@ def tile_list_adna_damage_tempering_kernel(
         def quantise_h(k):
             if k + 1 == len(pairs):
                 codes = staged([P, CHUNK], U32, "h_codes_last", LAST_CODES_AT)
+            elif k == 2:
+                codes = staged([P, CHUNK], U32, "h_codes%d" % k, FIRST_CODES_AT + 2 * KB)
             else:
                 codes = keep.tile([P, CHUNK], U32, name="h_codes%d" % k, align_bytes=64)
             plane = keep.tile([P, CHUNK], U8, name="h_sc%d" % k, align_bytes=64)
@@ -340,9 +345,8 @@ def tile_list_adna_damage_tempering_kernel(
         for k in range(3):
             factor(k, [b_step(k + 1, 0)], [b_step(k + 1, 1)])
         for a in range(PASSES):
-            for step in (round_w1, quantise_w1):
-                for t0 in (0, 2):
-                    step(0, a, t0, 2)
+            round_w1(0, a)
+            quantise_w1(0, a)
         w8 = staged([P, PASSES * N], I32, "w8", RAW[0, 0])
         nc.sync.dma_start(
             w8[:].rearrange("p (a n) -> p a n", a=PASSES),
@@ -417,7 +421,13 @@ def tile_list_adna_damage_tempering_kernel(
         place_weighed(1, 0)
         place_weighed(2, 0)
         early[0] = weighed_early(0, y2_at(0))
-        factor(4, [], [b_step(5, 0), b_step(5, 1)])
+        r4 = staged([P, CHUNK * PACK], F32, "root4", root_at(4))
+        for s in range(2):
+            root(r4[:, halves[s]], parts[s][:])
+        size_of_b(5, 0)
+        size_of_b(5, 1)
+        for s in range(2):
+            square(parts[s][:], r4[:, halves[s]])
 
         def first_half(c):
             damage(c, 0, (0, 3))
@@ -434,10 +444,11 @@ def tile_list_adna_damage_tempering_kernel(
 
         first_half(1)
         weigh_beside(2, h_at(4))
-        factor(5, [], [b_step(6, 0), b_step(6, 1)])
+        factor(5, [], [b_step(6, 0)])
         read_y(1, 1, (1,))
+        size_of_b(6, 1)
         second_half(1)
-        factor(6, [], [lambda: read_y(1, 1, (2,), 1, y2_at(1)), b_step(7, 0), b_step(7, 1)])
+        factor(6, [lambda: read_y(1, 1, (2,), 1, y2_at(1))], [b_step(7, 0), b_step(7, 1)])
         place_weighed(2, 1)
         early[1] = weighed_early(1, y2_at(1))
 

@@ -26,7 +26,7 @@ SUB = 128
 CHUNKS = S // CHUNK
 PAGES = N // P
 KB = 1024
-OPENED = 4
+OPENED = 1
 RAW = {(1, 0): 0, (1, 1): 8 * KB, (0, 0): 16 * KB, (0, 1): 28 * KB}
 W4_AT = 24 * KB
 X0_AT = (32 * KB, 2 * KB)
@@ -36,7 +36,6 @@ TAB_AT = 60 * KB
 LATE_AT = 92 * KB
 Y2_AT = 96 * KB
 TAIL_AT = 102 * KB
-W4_RAW_AT = 108 * KB
 ROUNDED_AT = 114 * KB
 FIRST_CODES_AT = 124 * KB
 
@@ -58,10 +57,10 @@ def tile_list_adna_damage_tempering_kernel(
         places = keep.tile([P, S // 16], U16, name="places")
         nc.sync.dma_start(picks[:], offs)
 
-        tab_sc = staged([P, T], U8, "tab_sc", TAB_AT + 16 * KB)
+        tab_sc = keep.tile([P, T], U8, name="tab_sc", align_bytes=64)
         w4_sc_raw = staged([P, 4 * KB + 128], U8, "w4_sc_raw", W4_AT - 64)[:, 0 : PASSES * H]
-        v_sc = [keep.tile([P, PASSES * HALF], U8, name="v_sc0", align_bytes=64)]
-        for plane in (tab_sc, w4_sc_raw, v_sc[0]):
+        v_sc = keep.tile([P, PASSES * S], U8, name="v_sc", align_bytes=64)
+        for plane in (tab_sc, w4_sc_raw, v_sc):
             nc.vector.memset(plane[:].bitcast(I32), 0)
 
         warm_in = keep.tile([P, 1], F32, name="warm_in")
@@ -69,7 +68,7 @@ def tile_list_adna_damage_tempering_kernel(
         nc.vector.memset(warm_in[:], 1.0)
         nc.scalar.activation(warm_out[:], warm_in[:], ACT.Abs_reciprocal_sqrt)
 
-        w4_raw = staged([P, PASSES * 2 * H], U8, "w4_raw", W4_RAW_AT)
+        w4_raw = keep.tile([P, PASSES * 2 * H], U8, name="w4_raw", align_bytes=64)
         for a in range(PASSES):
             nc.sync.dma_start(w4_raw[:, 2 * H * a : 2 * H * (a + 1)].bitcast(I32), w4_words[a].bitcast(I32))
         nc.sync.dma_start(tab_sc[0:P:4, :].bitcast(I32), tab_scales.bitcast(I32).rearrange("a q n -> q a n"))
@@ -78,30 +77,19 @@ def tile_list_adna_damage_tempering_kernel(
                 w4_sc_raw[32 * q : 32 * q + 4, :].bitcast(I32).rearrange("r (a n) -> r a n", a=PASSES),
                 w4_scales[:, 4 * q : 4 * q + 4, :].bitcast(I32).rearrange("a r n -> r a n"),
             )
-        tab = [staged([P, T], I32, "tab%d" % a, TAB_AT + 16 * KB * a) for a in range(PASSES)]
+        tab = []
+        for a in range(PASSES):
+            words = staged([P, T], I32, "tab%d" % a, TAB_AT + 16 * KB * a)
+            nc.sync.dma_start(words[:], tab_words[a].rearrange("p n i -> p (n i)").bitcast(I32))
+            tab.append(words)
 
-        def load_tab(a):
-            nc.sync.dma_start(tab[a][:], tab_words[a].rearrange("p n i -> p (n i)").bitcast(I32))
-
-        load_tab(0)
-
-        spread = [
-            staged([P, HALF], U8, "v_sc_spread0", RAW[1, 1] - HALF // 2),
-            keep.tile([P, HALF], U8, name="v_sc_spread1", align_bytes=64),
-        ]
-
-        def move_scales(half):
-            for q in range(4):
-                nc.scalar.dma_start(
-                    v_sc[half][32 * q : 32 * q + 4, :].bitcast(I32).rearrange("r (a n) -> r a n", a=PASSES),
-                    spread[half][32 * q : 32 * q + 32 : 4, :].bitcast(I32),
-                )
-
-        for half in range(2):
-            cols = HALF // 16
-            nc.vector.tensor_copy(spread[half][:], tab_sc[:].indirect(picks[:, cols * half : cols * (half + 1)]))
-        move_scales(0)
-        load_tab(1)
+        v_sc_spread = keep.tile([P, S], U8, name="v_sc_spread", align_bytes=64)
+        nc.vector.tensor_copy(v_sc_spread[:], tab_sc[:].indirect(picks[:]))
+        for q in range(4):
+            nc.scalar.dma_start(
+                v_sc[32 * q : 32 * q + 4, :].bitcast(I32).rearrange("r (a n) -> r a n", a=PASSES),
+                v_sc_spread[32 * q : 32 * q + 32 : 4, :].bitcast(I32),
+            )
 
         w4 = staged([P, PASSES * 2 * H], U8, "w4", W4_AT)
         w4_sc = keep.tile([P, PASSES * H], U8, name="w4_sc", align_bytes=64)
@@ -113,10 +101,6 @@ def tile_list_adna_damage_tempering_kernel(
             w4[:].bitcast(U16).rearrange("p (u t m) -> p u t m", t=PACK, m=P),
             w4_raw[:].bitcast(U16).rearrange("p (u m t) -> p u t m", t=PACK, m=P),
         )
-
-        v_sc.append(staged([P, PASSES * HALF], U8, "v_sc1", W4_RAW_AT))
-        nc.vector.memset(v_sc[1][:].bitcast(I32), 0)
-        move_scales(1)
 
         w1_raw = {}
 
@@ -177,13 +161,14 @@ def tile_list_adna_damage_tempering_kernel(
                     lhsT=codes,
                     lhsT_scale=plane,
                     rhs=v[a, c][:, c0 : c0 + SUB].bitcast(FP8X4),
-                    rhs_scale=v_sc[j0 // HALF][:, HALF * a + j0 % HALF : HALF * a + j0 % HALF + SUB],
+                    rhs_scale=v_sc[:, S * a + j0 : S * a + j0 + SUB],
                     start=((t, a) == steps[0] if one_group else a == PASSES - 1),
                     stop=((t, a) == steps[-1] if one_group else a == 0),
                 )
 
         pairs = [(c, g) for g in range(2) for c in range(2)] + [(c, g) for c in range(2, CHUNKS) for g in range(2)]
         shrink = {}
+        halves = [slice(m0, m0 + HALF) for m0 in range(0, S, HALF)]
 
         def background(k, s, passes):
             c, g = pairs[k]
@@ -228,6 +213,13 @@ def tile_list_adna_damage_tempering_kernel(
             for step in second:
                 step()
             square(shrink[k][:], r[:])
+
+        def factor_by_banks(k):
+            r = staged([P, CHUNK * PACK], F32, "root%d" % k, root_at(k))
+            for cols in halves:
+                root(r[:, cols], shrink[k][:, cols])
+            for cols in halves:
+                square(shrink[k][:, cols], r[:, cols])
 
         def b_step(k, s):
             return lambda: size_of_b(k, s)
@@ -322,8 +314,6 @@ def tile_list_adna_damage_tempering_kernel(
             nc.sync.dma_start(x[:], rows.rearrange("(e p) m -> p e m", p=P))
             held.append(x)
 
-        halves = [slice(m0, m0 + HALF) for m0 in range(0, S, HALF)]
-
         factors = [keep.tile([P, S], F32, name="factor%d" % b) for b in range(PAGES - 1)]
 
         def page_root(b, cols):
@@ -342,7 +332,10 @@ def tile_list_adna_damage_tempering_kernel(
                 background(k, s, (0,))
         size_of_b(0, 0)
         size_of_b(0, 1)
-        for k in range(3):
+        factor_by_banks(0)
+        size_of_b(1, 0)
+        size_of_b(1, 1)
+        for k in (1, 2):
             factor(k, [b_step(k + 1, 0)], [b_step(k + 1, 1)])
         for a in range(PASSES):
             round_w1(0, a)
@@ -495,14 +488,12 @@ def tile_list_adna_damage_tempering_kernel(
         page_square(1, high)
         temper(1, high)
         page_root(2, high)
-        page_square(2, low)
-        temper(2, low)
-        factor_last = staged([P, CHUNK], F32, "factor_last", TAIL_AT)
-        square(factor_last[:], factors[2][:, chunk(2)])
-        page_square(2, chunk(3))
-        temper(2, chunk(2), factor_last[:])
-        jobs = [(factors[2], 2, 3)] + [(pages[3], 3, c) for c in range(CHUNKS)]
-        tail = staged([P, 5 * CHUNK], F32, "tail", TAIL_AT)
+        factor_last = staged([P, HALF], F32, "factor_last", TAIL_AT)
+        square(factor_last[:], factors[2][:, low])
+        page_square(2, high)
+        temper(2, low, factor_last[:])
+        jobs = [(factors[2], 2, c) for c in (2, 3)] + [(pages[3], 3, c) for c in range(CHUNKS)]
+        tail = staged([P, 6 * CHUNK], F32, "tail", TAIL_AT)
         for i, (f, b, c) in enumerate(jobs):
             nc.vector.tensor_tensor(tail[:, chunk(i)], f[:, chunk(c)], held[1][:, b % 2, chunk(c)], MULT)
             nc.sync.dma_start(out[P * b : P * (b + 1), chunk(c)], tail[:, chunk(i)])

@@ -129,8 +129,8 @@ def tile_list_adna_damage_tempering_kernel(
         def round_w1(g, a):
             grouped = staged([P, PACK * HALF], BF16, "w1_bf%d_%d" % (g, a), ROUNDED_AT + 4 * KB * a)
             nc.vector.tensor_copy(
-                grouped[:].rearrange("p (t m j) -> p m t j", t=PACK, j=PACK),
-                w1_raw[g, a][:].rearrange("p j (m t) -> p m t j", t=PACK),
+                grouped[:].rearrange("p (t m j) -> p m j t", t=PACK, j=PACK),
+                w1_raw[g, a][:].rearrange("p j (m t) -> p m j t", t=PACK),
             )
             w1_bf[g, a] = grouped
 
@@ -488,12 +488,14 @@ def tile_list_adna_damage_tempering_kernel(
         page_square(1, high)
         temper(1, high)
         page_root(2, high)
-        factor_last = staged([P, HALF], F32, "factor_last", TAIL_AT)
-        square(factor_last[:], factors[2][:, low])
-        page_square(2, high)
-        temper(2, low, factor_last[:])
-        jobs = [(factors[2], 2, c) for c in (2, 3)] + [(pages[3], 3, c) for c in range(CHUNKS)]
-        tail = staged([P, 6 * CHUNK], F32, "tail", TAIL_AT)
+        page_square(2, low)
+        temper(2, low)
+        factor_last = staged([P, CHUNK], F32, "factor_last", TAIL_AT)
+        square(factor_last[:], factors[2][:, chunk(2)])
+        page_square(2, chunk(3))
+        temper(2, chunk(2), factor_last[:])
+        jobs = [(factors[2], 2, 3)] + [(pages[3], 3, c) for c in range(CHUNKS)]
+        tail = staged([P, 5 * CHUNK], F32, "tail", TAIL_AT)
         for i, (f, b, c) in enumerate(jobs):
             nc.vector.tensor_tensor(tail[:, chunk(i)], f[:, chunk(c)], held[1][:, b % 2, chunk(c)], MULT)
             nc.sync.dma_start(out[P * b : P * (b + 1), chunk(c)], tail[:, chunk(i)])

@@ -60,7 +60,8 @@ def tile_list_adna_damage_tempering_kernel(
         tab_sc = keep.tile([P, T], U8, name="tab_sc", align_bytes=64)
         w4_sc_raw = staged([P, 4 * KB + 128], U8, "w4_sc_raw", W4_AT - 64)[:, 0 : PASSES * H]
         v_sc = keep.tile([P, PASSES * S], U8, name="v_sc", align_bytes=64)
-        for plane in (tab_sc, w4_sc_raw, v_sc):
+        w8_sc = keep.tile([P, N], U8, name="w8_sc", align_bytes=64)
+        for plane in (tab_sc, w4_sc_raw, v_sc, w8_sc):
             nc.vector.memset(plane[:].bitcast(I32), 0)
 
         warm_in = keep.tile([P, 1], F32, name="warm_in")
@@ -94,12 +95,12 @@ def tile_list_adna_damage_tempering_kernel(
         w4 = staged([P, PASSES * 2 * H], U8, "w4", W4_AT)
         w4_sc = keep.tile([P, PASSES * H], U8, name="w4_sc", align_bytes=64)
         nc.vector.tensor_copy(
-            w4_sc[:].rearrange("p (u t m) -> p u t m", t=PACK, m=P),
-            w4_sc_raw[:].rearrange("p (u m t) -> p u t m", t=PACK, m=P),
+            w4_sc[:].rearrange("p (u t m) -> p u m t", t=PACK, m=P),
+            w4_sc_raw[:].rearrange("p (u m t) -> p u m t", t=PACK, m=P),
         )
         nc.vector.tensor_copy(
-            w4[:].bitcast(U16).rearrange("p (u t m) -> p u t m", t=PACK, m=P),
-            w4_raw[:].bitcast(U16).rearrange("p (u m t) -> p u t m", t=PACK, m=P),
+            w4[:].bitcast(U16).rearrange("p (u t m) -> p u m t", t=PACK, m=P),
+            w4_raw[:].bitcast(U16).rearrange("p (u m t) -> p u m t", t=PACK, m=P),
         )
 
         w1_raw = {}
@@ -247,9 +248,9 @@ def tile_list_adna_damage_tempering_kernel(
                 h_bf[k] = staged([P, CHUNK * PACK], BF16, "h_bf%d" % k, at)
             cols = slice(PACK * SUB * s, PACK * SUB * (s + 1))
             nc.vector.tensor_tensor(
-                h_bf[k][:, cols].rearrange("p (j e t) -> p j t e", t=PACK, e=2),
-                bank_of(k, s)[:].rearrange("p (t j e) -> p j t e", t=PACK, e=2),
-                factor_part(k, s).rearrange("p (t j e) -> p j t e", t=PACK, e=2),
+                h_bf[k][:, cols].rearrange("p (j e t) -> p j t e", t=PACK, e=4),
+                bank_of(k, s)[:].rearrange("p (t j e) -> p j t e", t=PACK, e=4),
+                factor_part(k, s).rearrange("p (t j e) -> p j t e", t=PACK, e=4),
                 MULT,
             )
 
@@ -345,8 +346,6 @@ def tile_list_adna_damage_tempering_kernel(
             w8[:].rearrange("p (a n) -> p a n", a=PASSES),
             w8_words.rearrange("a p n i -> p a (n i)").bitcast(I32),
         )
-        w8_sc = staged([P, N], U8, "w8_sc", RAW[0, 0] + 4 * KB)
-        nc.vector.memset(w8_sc[:].bitcast(I32), 0)
         for q in range(4):
             nc.sync.dma_start(
                 w8_sc[32 * q : 32 * q + 8, :].bitcast(I32),

from contextlib import ExitStack

import concourse.mybir as mybir

K, T, S, H, N = 1024, 4096, 1024, 1024, 512
FLOPS = 2 * K * H * S * 2 + 2 * H * N * S

F32 = mybir.dt.float32
BF16 = mybir.dt.bfloat16
I32 = mybir.dt.int32
U32 = mybir.dt.uint32
U16 = mybir.dt.uint16
U8 = mybir.dt.uint8
FP8X4 = mybir.dt.float8_e4m3fn_x4
FP4X4 = mybir.dt.float4_e2m1fn_x4
ACT = mybir.ActivationFunctionType
MULT = mybir.AluOpType.mult

P = 128
PACK = 4
KP = P * PACK
PASSES = K // KP
HALF = 512
CHUNK = 256
SUB = 128
CHUNKS = S // CHUNK
PAGES = N // P
KB = 1024
OPENED = 1
RAW = {(1, 0): 0, (1, 1): 8 * KB, (0, 0): 16 * KB, (0, 1): 28 * KB}
W4_AT = 24 * KB
X0_AT = (32 * KB, 2 * KB)
H_AT = 40 * KB
LAST_CODES_AT = 56 * KB
TAB_AT = 60 * KB
LATE_AT = 92 * KB
Y2_AT = 96 * KB
TAIL_AT = 102 * KB
ROUNDED_AT = 114 * KB
FIRST_CODES_AT = 124 * KB


def tile_list_adna_damage_tempering_kernel(
    tc, tab_words, tab_scales, offs, w1, w4_words, w4_scales, w8_words, w8_scales, offs2, wgo, x0, out
):
    nc = tc.nc
    with ExitStack() as ctx:
        keep = ctx.enter_context(tc.tile_pool(name="keep", bufs=1))
        ring = ctx.enter_context(tc.tile_pool(name="ring", bufs=2))
        stage = ctx.enter_context(tc.tile_pool(name="stage", bufs=1))
        psum = ctx.enter_context(tc.psum_pool(name="psum", bufs=1))

        def staged(shape, dtype, name, offset):
            return stage.tile(shape, dtype, name=name, align_bytes=64, offset=offset)

        picks = keep.tile([P, S // 16], U16, name="picks")
        places = keep.tile([P, S // 16], U16, name="places")
        nc.sync.dma_start(picks[:], offs)

        tab_sc = keep.tile([P, T], U8, name="tab_sc", align_bytes=64)
        w4_sc_raw = staged([P, 4 * KB + 128], U8, "w4_sc_raw", W4_AT - 64)[:, 0 : PASSES * H]
        v_sc = keep.tile([P, PASSES * S], U8, name="v_sc", align_bytes=64)
        w8_sc = keep.tile([P, N], U8, name="w8_sc", align_bytes=64)
        for plane in (tab_sc, w4_sc_raw, v_sc, w8_sc):
            nc.vector.memset(plane[:].bitcast(I32), 0)

        warm_in = keep.tile([P, 1], F32, name="warm_in")
        warm_out = keep.tile([P, 1], F32, name="warm_out")
        nc.vector.memset(warm_in[:], 1.0)
        nc.scalar.activation(warm_out[:], warm_in[:], ACT.Abs_reciprocal_sqrt)

        w4_raw = keep.tile([P, PASSES * 2 * H], U8, name="w4_raw", align_bytes=64)
        for a in range(PASSES):
            nc.sync.dma_start(w4_raw[:, 2 * H * a : 2 * H * (a + 1)].bitcast(I32), w4_words[a].bitcast(I32))
        nc.sync.dma_start(tab_sc[0:P:4, :].bitcast(I32), tab_scales.bitcast(I32).rearrange("a q n -> q a n"))
        for q in range(4):
            nc.sync.dma_start(
                w4_sc_raw[32 * q : 32 * q + 4, :].bitcast(I32).rearrange("r (a n) -> r a n", a=PASSES),
                w4_scales[:, 4 * q : 4 * q + 4, :].bitcast(I32).rearrange("a r n -> r a n"),
            )
        tab = []
        for a in range(PASSES):
            words = staged([P, T], I32, "tab%d" % a, TAB_AT + 16 * KB * a)
            nc.sync.dma_start(words[:], tab_words[a].rearrange("p n i -> p (n i)").bitcast(I32))
            tab.append(words)

        v_sc_spread = keep.tile([P, S], U8, name="v_sc_spread", align_bytes=64)
        nc.vector.tensor_copy(v_sc_spread[:], tab_sc[:].indirect(picks[:]))
        for q in range(4):
            nc.scalar.dma_start(
                v_sc[32 * q : 32 * q + 4, :].bitcast(I32).rearrange("r (a n) -> r a n", a=PASSES),
                v_sc_spread[32 * q : 32 * q + 32 : 4, :].bitcast(I32),
            )

        w4 = staged([P, PASSES * 2 * H], U8, "w4", W4_AT)
        w4_sc = keep.tile([P, PASSES * H], U8, name="w4_sc", align_bytes=64)
        nc.vector.tensor_copy(
            w4_sc[:].rearrange("p (u t m) -> p u m t", t=PACK, m=P),
            w4_sc_raw[:].rearrange("p (u m t) -> p u m t", t=PACK, m=P),
        )
        nc.vector.tensor_copy(
            w4[:].bitcast(U16).rearrange("p (u t m) -> p u m t", t=PACK, m=P),
            w4_raw[:].bitcast(U16).rearrange("p (u m t) -> p u m t", t=PACK, m=P),
        )

        w1_raw = {}

        def load_w1(g, a):
            raw = staged([P, PACK, HALF], F32, "w1_raw%d_%d" % (g, a), RAW[g, a])
            rows = w1[KP * a : KP * (a + 1), HALF * g : HALF * (g + 1)]
            nc.sync.dma_start(raw[:], rows.rearrange("(p j) c -> p j c", j=PACK))
            w1_raw[g, a] = raw

        for g in range(2):
            for a in range(PASSES):
                load_w1(g, a)

        v = {}
        for a, c0, count in ((0, 0, 2), (0, 2, 2), (1, 0, 1), (1, 1, 1), (1, 2, 2)):
            picked = keep.tile([P, CHUNK * count], U32, name="v%d_%d" % (a, c0), align_bytes=64)
            cols = CHUNK // 16
            nc.vector.tensor_copy(
                picked[:], tab[a][:].bitcast(U32).indirect(picks[:, cols * c0 : cols * (c0 + count)])
            )
            for i in range(count):
                v[a, c0 + i] = picked[:, CHUNK * i : CHUNK * (i + 1)]

        w1_bf, w1_codes, w1_sc = {}, {}, {}

        def round_w1(g, a):
            grouped = staged([P, PACK * HALF], BF16, "w1_bf%d_%d" % (g, a), ROUNDED_AT + 4 * KB * a)
            nc.vector.tensor_copy(
                grouped[:].rearrange("p (t m j) -> p m j t", t=PACK, j=PACK),
                w1_raw[g, a][:].rearrange("p j (m t) -> p m j t", t=PACK),
            )
            w1_bf[g, a] = grouped

        def quantise_w1(g, a):
            codes = keep.tile([P, HALF], U32, name="w1c%d_%d" % (g, a), align_bytes=64)
            plane = keep.tile([P, HALF], U8, name="w1s%d_%d" % (g, a), align_bytes=64)
            nc.vector.quantize_mx(out=codes[:].bitcast(FP8X4), scales=plane[:], in_=w1_bf[g, a][:])
            w1_codes[g, a], w1_sc[g, a] = codes, plane

        banks = [psum.tile([P, PACK * SUB], F32, name="bank%d" % e) for e in range(8)]

        def y_bank(c, e):
            return banks[(6 if c == 0 else 4) + e]

        def bank_of(k, s):
            return banks[(6 if k == 5 else 2 * (k % 3)) + s]

        def first_stage(bank, j0, stationary, one_group, passes=(0, 1)):
            c, c0 = divmod(j0, CHUNK)
            if one_group:
                steps = [(t, a) for a in range(PASSES) for t in range(PACK)]
            else:
                steps = [(t, a) for t in range(PACK) for a in reversed(range(PASSES))]
            for t, a in [step for step in steps if step[1] in passes]:
                codes, plane = stationary(t, a)
                nc.tensor.matmul_mx(
                    out=bank[:, SUB * t : SUB * (t + 1)],
                    lhsT=codes,
                    lhsT_scale=plane,
                    rhs=v[a, c][:, c0 : c0 + SUB].bitcast(FP8X4),
                    rhs_scale=v_sc[:, S * a + j0 : S * a + j0 + SUB],
                    start=((t, a) == steps[0] if one_group else a == PASSES - 1),
                    stop=((t, a) == steps[-1] if one_group else a == 0),
                )

        pairs = [(c, g) for g in range(2) for c in range(2)] + [(c, g) for c in range(2, CHUNKS) for g in range(2)]
        shrink = {}
        halves = [slice(m0, m0 + HALF) for m0 in range(0, S, HALF)]

        def background(k, s, passes):
            c, g = pairs[k]
            bank = banks[6 + s] if k == 3 else bank_of(k, s)

            def columns(t, a):
                col = H * a + HALF * g + P * t
                return w4[:, 2 * col : 2 * (col + P)].bitcast(FP4X4), w4_sc[:, col : col + P]

            first_stage(bank, CHUNK * c + SUB * s, columns, k < OPENED, passes)
            return bank

        parts = []

        def factor_part(k, s):
            return parts[s][:] if k == 4 else shrink[k][:, PACK * SUB * s : PACK * SUB * (s + 1)]

        def size_of_b(k, s):
            bank = background(k, s, (1,) if k < OPENED else (0, 1))
            if (k, s) == (3, 0):
                shrink[k] = staged([P, CHUNK * PACK], F32, "shrink3", root_at(4))
            elif k == 4:
                parts.append(staged([P, PACK * SUB], F32, "shrink4_%d" % s, FIRST_CODES_AT + (64 if s else -2 * KB)))
            elif s == 0:
                shrink[k] = ring.tile([P, CHUNK * PACK], F32, name="shrink", tag="shrink", bufs=3)
            nc.scalar.activation(factor_part(k, s), bank[:], ACT.Abs)

        def root(result, values):
            nc.scalar.activation(result, values, ACT.Abs_reciprocal_sqrt, bias=1.0)

        def square(result, values):
            nc.scalar.activation(result, values, ACT.Square)

        def root_at(k):
            return TAB_AT + 4 * KB * k

        def factor(k, first, second):
            r = staged([P, CHUNK * PACK], F32, "root%d" % k, root_at(k))
            for step in first:
                step()
            root(r[:], shrink[k][:])
            for step in second:
                step()
            square(shrink[k][:], r[:])

        def factor_by_banks(k):
            r = staged([P, CHUNK * PACK], F32, "root%d" % k, root_at(k))
            for cols in halves:
                root(r[:, cols], shrink[k][:, cols])
            for cols in halves:
                square(shrink[k][:, cols], r[:, cols])

        def b_step(k, s):
            return lambda: size_of_b(k, s)

        h_bf, h_codes, h_sc = {}, {}, {}

        def h_at(k):
            return H_AT + 2 * KB * k

        def signal(k):
            c, g = pairs[k]

            def columns(t, a):
                return (
                    w1_codes[g, a][:, P * t : P * (t + 1)].bitcast(FP8X4),
                    w1_sc[g, a][:, P * t : P * (t + 1)],
                )

            for s in range(2):
                first_stage(bank_of(k, s), CHUNK * c + SUB * s, columns, k < 4)

        def feature(k, s):
            if s == 0:
                at = RAW[1, 1] + 6 * KB if k == 1 else h_at(k)
                h_bf[k] = staged([P, CHUNK * PACK], BF16, "h_bf%d" % k, at)
            cols = slice(PACK * SUB * s, PACK * SUB * (s + 1))
            nc.vector.tensor_tensor(
                h_bf[k][:, cols].rearrange("p (j e t) -> p j t e", t=PACK, e=4),
                bank_of(k, s)[:].rearrange("p (t j e) -> p j t e", t=PACK, e=4),
                factor_part(k, s).rearrange("p (t j e) -> p j t e", t=PACK, e=4),
                MULT,
            )

        def features(k):
            signal(k)
            feature(k, 0)
            feature(k, 1)

        def quantise_h(k):
            if k + 1 == len(pairs):
                codes = staged([P, CHUNK], U32, "h_codes_last", LAST_CODES_AT)
            elif k == 2:
                codes = staged([P, CHUNK], U32, "h_codes%d" % k, FIRST_CODES_AT + 2 * KB)
            else:
                codes = keep.tile([P, CHUNK], U32, name="h_codes%d" % k, align_bytes=64)
            plane = keep.tile([P, CHUNK], U8, name="h_sc%d" % k, align_bytes=64)
            nc.vector.quantize_mx(out=codes[:].bitcast(FP8X4), scales=plane[:], in_=h_bf[k][:])
            h_codes[pairs[k]], h_sc[pairs[k]] = codes, plane

        y2 = {}

        def damage(c, e, blocks):
            for i, b in enumerate(blocks):
                for g in range(2):
                    nc.tensor.matmul_mx(
                        out=y_bank(c, e)[:, chunk(i)],
                        lhsT=w8[:, N * g + P * b : N * g + P * (b + 1)].bitcast(FP8X4),
                        lhsT_scale=w8_sc[4 * g : P, P * b : P * (b + 1)],
                        rhs=h_codes[c, g][:].bitcast(FP8X4),
                        rhs_scale=h_sc[c, g][:],
                        start=(g == 0),
                        stop=(g == 1),
                    )

        def read_y(c, e, blocks, first=0, at=None):
            shape, name = [P, CHUNK * len(blocks)], "y2_%d_%d" % (blocks[0], c)
            values = keep.tile(shape, F32, name=name) if at is None else staged(shape, F32, name, at)
            square(values[:], y_bank(c, e)[:, CHUNK * first : CHUNK * (first + len(blocks))])
            for i, b in enumerate(blocks):
                y2[b, c] = values[:, chunk(i)]

        def chunk(c):
            return slice(CHUNK * c, CHUNK * (c + 1))

        pages = [keep.tile([P, S], F32, name="page%d" % b) for b in range(PAGES - 1)]
        pages.append(staged([P, S], F32, "page_last", LAST_CODES_AT))

        def window(b, j0, width):
            return pages[b][:].indirect(places[:, j0 // 16 : (j0 + width) // 16])

        def place_weighed(b, c):
            nc.vector.tensor_tensor(window(b, CHUNK * c, CHUNK), y2[b, c], weight[c], MULT)

        def place(b, j0, values, width):
            nc.vector.tensor_copy(window(b, j0, width), values)

        held = []

        def load_x0(pair):
            x = staged([P, 2, S], F32, "x0_%d" % pair, X0_AT[pair])
            rows = x0[2 * P * pair : 2 * P * (pair + 1), :]
            nc.sync.dma_start(x[:], rows.rearrange("(e p) m -> p e m", p=P))
            held.append(x)

        factors = [keep.tile([P, S], F32, name="factor%d" % b) for b in range(PAGES - 1)]

        def page_root(b, cols):
            root(factors[b][:, cols], pages[b][:, cols])

        def page_square(b, cols):
            square(factors[b][:, cols], factors[b][:, cols])

        def temper(b, cols, values=None):
            f = factors[b][:, cols]
            nc.gpsimd.tensor_tensor(f, f if values is None else values, held[b // 2][:, b % 2, cols], MULT)
            nc.sync.dma_start(out[P * b : P * (b + 1), cols], f)

        for k in range(OPENED):
            for s in range(2):
                background(k, s, (0,))
        size_of_b(0, 0)
        size_of_b(0, 1)
        factor_by_banks(0)
        size_of_b(1, 0)
        size_of_b(1, 1)
        for k in (1, 2):
            factor(k, [b_step(k + 1, 0)], [b_step(k + 1, 1)])
        for a in range(PASSES):
            round_w1(0, a)
            quantise_w1(0, a)
        w8 = staged([P, PASSES * N], I32, "w8", RAW[0, 0])
        nc.sync.dma_start(
            w8[:].rearrange("p (a n) -> p a n", a=PASSES),
            w8_words.rearrange("a p n i -> p a (n i)").bitcast(I32),
        )
        for q in range(4):
            nc.sync.dma_start(
                w8_sc[32 * q : 32 * q + 8, :].bitcast(I32),
                w8_scales[:, 4 * q : 4 * q + 4, :].bitcast(I32),
            )
        nc.sync.dma_start(places[:], offs2)
        gain = staged([P, S], F32, "gain", RAW[0, 1])
        nc.sync.dma_start(gain[:], wgo)
        load_x0(0)

        round_w1(1, 0)
        signal(0)
        feature(0, 0)
        quantise_w1(1, 0)
        feature(0, 1)
        round_w1(1, 1)
        quantise_h(0)
        quantise_w1(1, 1)
        features(1)
        signal(2)
        signal(3)
        feature(2, 0)
        feature(2, 1)
        quantise_h(1)
        quantise_h(2)
        load_x0(1)

        weight = {}

        def weigh(c, at=None):
            name = "weight%d" % c
            weight[c] = (keep.tile([P, CHUNK], F32, name=name) if at is None else staged([P, CHUNK], F32, name, at))[:]
            square(weight[c], gain[:, chunk(c)])

        def weigh_beside(c, at):
            weight[c] = staged([P, CHUNK], F32, "weight%d" % c, at)[:]
            nc.gpsimd.tensor_tensor(weight[c], gain[:, chunk(c)], gain[:, chunk(c)], MULT)

        def weighed_early(c, over):
            z = staged([P, CHUNK], F32, "z3_%d" % c, over)
            nc.gpsimd.tensor_tensor(z[:], y2[3, c], weight[c], MULT)
            return z

        def y2_at(c):
            return Y2_AT + 2 * KB * c

        early = {}
        both = staged([P, 2 * CHUNK], F32, "weight01", ROUNDED_AT + 4 * KB)
        nc.gpsimd.tensor_tensor(both[:], gain[:, halves[0]], gain[:, halves[0]], MULT)
        weight[0], weight[1] = both[:, chunk(0)], both[:, chunk(1)]
        r3 = staged([P, CHUNK * PACK], F32, "root3", root_at(3))
        root(r3[:], shrink[3][:])
        size_of_b(4, 0)
        for cols in halves:
            square(shrink[3][:, cols], r3[:, cols])
        damage(0, 0, (0, 3))
        damage(0, 1, (1, 2))
        read_y(0, 0, (0, 3))
        size_of_b(4, 1)
        read_y(0, 1, (1, 2), at=y2_at(0))
        feature(3, 0)
        feature(3, 1)
        place_weighed(0, 0)
        quantise_h(3)
        place_weighed(1, 0)
        place_weighed(2, 0)
        early[0] = weighed_early(0, y2_at(0))
        r4 = staged([P, CHUNK * PACK], F32, "root4", root_at(4))
        for s in range(2):
            root(r4[:, halves[s]], parts[s][:])
        size_of_b(5, 0)
        size_of_b(5, 1)
        for s in range(2):
            square(parts[s][:], r4[:, halves[s]])

        def first_half(c):
            damage(c, 0, (0, 3))
            read_y(c, 0, (0, 3))
            features(2 * c + 2)
            place_weighed(0, c)
            quantise_h(2 * c + 2)
            damage(c, 1, (1, 2))

        def second_half(c):
            features(2 * c + 3)
            place_weighed(1, c)
            quantise_h(2 * c + 3)

        first_half(1)
        weigh_beside(2, h_at(4))
        factor(5, [], [b_step(6, 0)])
        read_y(1, 1, (1,))
        size_of_b(6, 1)
        second_half(1)
        factor(6, [lambda: read_y(1, 1, (2,), 1, y2_at(1))], [b_step(7, 0), b_step(7, 1)])
        place_weighed(2, 1)
        early[1] = weighed_early(1, y2_at(1))

        first_half(2)
        early[2] = weighed_early(2, h_at(6))
        factor(7, [], [lambda: root(early[0][:], early[0][:])])
        read_y(2, 1, (1,), at=root_at(7))
        weigh(3, root_at(7) + KB)
        second_half(2)

        last = keep.tile([P, S], F32, name="last")
        square(last[:, chunk(0)], early[0][:])
        root(early[1][:], early[1][:])
        read_y(2, 1, (2,), 1)
        place_weighed(2, 2)
        root(early[2][:], early[2][:])
        for c in (1, 2):
            square(last[:, chunk(c)], early[c][:])
        damage(3, 0, (0,))
        damage(3, 1, (1, 2))
        read_y(3, 0, (0,), at=LATE_AT)
        place_weighed(0, 3)
        read_y(3, 1, (1, 2))
        damage(3, 0, (3,))
        read_y(3, 0, (3,))
        place(3, 0, last[:, chunk(0)], CHUNK)
        late = staged([P, 3 * CHUNK], F32, "late", LATE_AT)
        for b in (1, 2, 3):
            nc.gpsimd.tensor_tensor(late[:, chunk(b - 1)], y2[b, 3], weight[3], MULT)
        for b in (1, 2):
            place(b, 3 * CHUNK, late[:, chunk(b - 1)], CHUNK)
        low, high = halves
        for step in (page_root, page_square, temper):
            for cols in halves:
                step(0, cols)
        root(late[:, chunk(2)], late[:, chunk(2)])
        page_root(1, low)
        square(last[:, chunk(3)], late[:, chunk(2)])
        place(3, CHUNK, last[:, CHUNK:S], S - CHUNK)
        page_square(1, low)
        temper(1, low)
        page_root(1, high)
        page_root(2, low)
        page_square(1, high)
        temper(1, high)
        page_root(2, high)
        page_square(2, low)
        temper(2, low)
        factor_last = staged([P, CHUNK], F32, "factor_last", TAIL_AT)
        square(factor_last[:], factors[2][:, chunk(2)])
        page_square(2, chunk(3))
        temper(2, chunk(2), factor_last[:])
        jobs = [(factors[2], 2, 3)] + [(pages[3], 3, c) for c in range(CHUNKS)]
        tail = staged([P, 5 * CHUNK], F32, "tail", TAIL_AT)
        for i, (f, b, c) in enumerate(jobs):
            nc.vector.tensor_tensor(tail[:, chunk(i)], f[:, chunk(c)], held[1][:, b % 2, chunk(c)], MULT)
            nc.sync.dma_start(out[P * b : P * (b + 1), chunk(c)], tail[:, chunk(i)])
